import numpy as np, ml_dtypes
CORES = [3,7,11,15,131,135,139,143]
N = 8
BF = ml_dtypes.bfloat16
B, W, CAP, RO = 1024, 3200, 32, 3
L = N * CAP
def parts(rng):
    share = rng.choice(np.array([0.1, 0.2, 0.4, 0.6]), (N, 8, 1, B))
    v = np.where(rng.random((N, 8, 16, B)) < share, -rng.integers(1, 256, (N, 8, 16, B)), rng.integers(0, 256, (N, 8, 16, B)))
    a = rng.integers(0, 256, (N, 8, 16, W)) * (rng.random((N, 8, 16, W)) < rng.choice(np.array([0.3, 0.6, 0.9]), (N, 8, 1, W))); a[..., W - 1] = 0
    u = rng.integers(0, W - 1, (N, 8, 16, B))
    u = np.where(rng.random(u.shape) < rng.choice(np.array([0.0, 0.0, 0.1, 0.1, 0.4, 0.96]), (N, 8, 1, B)), W - 1, u)
    to = np.where(rng.random((N, 8, W)) < rng.choice(np.array([0.0, 0.1, 0.25]), (N, 8, 1)), rng.integers(0, N, (N, 8, 1)), rng.integers(0, N, (N, 8, W)))
    pay = to * B + rng.integers(0, B, (N, 8, W))
    wk = np.where(rng.random((N, 8, L)) < 0.04, B, rng.integers(0, B, (N, 8, L)))
    return v, a, u, pay, wk
def pack(v, a, u, pay, wk):
    return {"vp": np.ascontiguousarray(v.reshape(N, 128, B)).astype(np.float32).astype(BF), "am": np.ascontiguousarray(a.reshape(N, 128, W)).astype(np.float32).astype(BF),
            "qu": np.ascontiguousarray(u.reshape(N, 128, B)).astype(np.int32), "pay": np.ascontiguousarray(pay).astype(np.int32), "wk": np.ascontiguousarray(wk).astype(np.int32)}
def setup_inputs(rng):
    return pack(*parts(rng))
def plant(rng, v, a, u, pay, wk, q, g, to):
    m = len(to); lanes = rng.permutation(L)[:m]; banks = rng.permutation(B)[:m]; lines = rng.permutation(W - 1)[:m]
    row = rng.integers(0, 16, m); j = rng.integers(0, 16, m)
    u[q, g][:, banks] = W - 1; u[q, g][row, banks] = lines
    v[q, g][j, banks] = -rng.integers(1, 256, m); a[q, g][j, lines] = 255
    order = np.argsort(lanes); pay[q, g][lines[order]] = to
    wk[q, g] = B; wk[q, g][lanes] = banks
def setup_inputs_room(rng):
    v, a, u, pay, wk = parts(rng)
    for q in range(N):
        for g in range(8):
            cnt = [CAP, CAP + 1, CAP - 1, 0, 1, 0, 2, CAP // 2][:N]
            if (q + g) % 4 == 3: cnt = [L] + [0] * (N - 1)
            to = np.concatenate([np.full(n, (q + 1 + g + j) % N, np.int64) for j, n in enumerate(cnt)])
            plant(rng, v, a, u, pay, wk, q, g, rng.permutation(to) * B + rng.integers(0, B, len(to)))
    return pack(v, a, u, pay, wk)
def setup_inputs_ties(rng):
    v, a, u, pay, wk = parts(rng)
    v[:, ::2] = rng.integers(-3, 3, (N, 4, 16, B)); a[:, ::2] = rng.integers(0, 4, (N, 4, 16, W))
    v[:, 1::2] = rng.integers(-3, 2, (N, 4, 16, B)) * 85; a[:, 1::2] = rng.integers(0, 4, (N, 4, 16, W)) * 85
    a = a * (rng.random((N, 8, 1, W)) < 0.6); a[..., W - 1] = 0
    u[:, :, 15] = np.where(rng.random((N, 8, B)) < 0.4, W - 1, u[:, :, 15])
    return pack(v, a, u, pay, wk)
def setup_inputs_alike(rng):
    v, a, u, pay, wk = parts(rng)
    wk[:, 0] = rng.choice(np.array([0, B - 1, 5, B // 2]), (N, L))
    u[:, 2] = rng.choice(np.array([0, W - 2, 7, W // 2, W - 1]), (N, 16, B))
    pay[:, 4] = rng.integers(0, N, (N, W)) * B + rng.choice(np.array([0, B - 1]), (N, W))
    u[:, 6] = np.repeat(u[:, 6, :1], 16, axis=1)
    wk[:, 1::2, L - 1] = wk[:, 1::2, 0]
    return pack(v, a, u, pay, wk)
def setup_inputs_dry(rng):
    v, a, u, pay, wk = parts(rng); o = rng.permutation(8)
    wk[:, o[0]] = B; a[:, o[1]] = 0; u[:, o[2]] = W - 1; v[:, o[3]] = np.abs(v[:, o[3]])
    v[:, o[4]] = -255; a[:, o[4]] = 255; a[..., W - 1] = 0
    wk[rng.integers(0, N), o[5]] = B
    h = int(o[6]); wk[:, h] = B
    for q in range(N):
        b = int(rng.integers(1, B)); n, m = [int(i) for i in rng.permutation(W - 1)[:2]]
        wk[q, h, int(rng.integers(0, L))] = b
        v[q, h, :, b] = -rng.integers(1, 256, 16); u[q, h, :, b] = n; a[q, h, :, n] = 0; pay[q, h, n] = (q + 1) % N * B
        v[q, h, :, 0] = -rng.integers(1, 256, 16); u[q, h, :, 0] = m; a[q, h, :, m] = 255; pay[q, h, m] = rng.integers(0, N) * B + rng.integers(1, B)
    return pack(v, a, u, pay, wk)
def setup_inputs_spread(rng):
    v, a, u, pay, wk = parts(rng)
    v = (np.exp2(8 * rng.random((N, 8, 1, B))) * rng.random((N, 8, 16, B))).astype(np.int64) * np.where(rng.random((N, 8, 16, B)) < 0.4, -1, 1)
    a = (np.exp2(8 * rng.random((N, 8, 1, W))) * rng.random((N, 8, 16, W))).astype(np.int64); a[..., W - 1] = 0
    u = np.where(u == W - 1, u, ((W - 1) * rng.random(u.shape) ** 2).astype(np.int64))
    pay = pay // B * B + (B * rng.random(pay.shape) ** 2).astype(np.int64)
    wk = np.where(wk == B, B, (B * rng.random(wk.shape) ** 2).astype(np.int64))
    return pack(v, a, u, pay, wk)
def check_inputs(d):
    bad = []
    for k, lo, hi in (("vp", -255, 255), ("am", 0, 255)):
        x = np.asarray(d[k]).astype(np.float32)
        if not np.all((x >= lo) & (x <= hi)): bad.append("range of " + k)
        elif not np.all(x == np.rint(x)): bad.append("whole numbers in " + k)
    if not np.all(np.asarray(d["am"]).astype(np.float32)[..., W - 1] == 0): bad.append("zeros in the last column of am")
    for k, hi in (("qu", W - 1), ("pay", N * B - 1), ("wk", B)):
        if np.min(d[k]) < 0 or np.max(d[k]) > hi: bad.append("range of " + k)
    return bad
def reference(vp, am, qu, pay, wk):
    v = vp.astype(np.float32).astype(np.int64).reshape(N, 8, 16, B); a = am.astype(np.float32).astype(np.int64).reshape(N, 8, 16, W)
    u = qu.astype(np.int64).reshape(N, 8, 16, B); payee = pay.astype(np.int64)
    w = wk.astype(np.int64); c = np.zeros((N, 8, 16, L), np.int64)
    for rnd in range(RO):
        w2 = np.full((N, 8, L), B, np.int64); c2 = np.zeros((N, 8, 16, L), np.int64)
        for q in range(N):
            for g in range(8):
                vv, aa, uu = v[q, g], a[q, g], u[q, g]
                lane = np.nonzero(w[q, g] < B)[0]
                lane = lane[np.sort(np.unique(w[q, g][lane], return_index=True)[1])]
                b = w[q, g][lane]
                x = np.maximum(vv[:, b] - c[q, g][:, lane], -255); vv[:, b] = x
                keep = np.any(x < 0, axis=0); b, x = b[keep], x[:, keep]
                n = uu[:, b]
                score = np.sum(x[:, None, :] + aa[:, n] >= 0, axis=0)
                best = 15 - np.argmax(score[::-1], axis=0)
                p = n[best, np.arange(len(b))]
                keep = p != W - 1; b, x, best, p = b[keep], x[:, keep], best[keep], p[keep]
                keep = np.sort(np.unique(p, return_index=True)[1]); b, x, best, p = b[keep], x[:, keep], best[keep], p[keep]
                t = np.minimum(aa[:, p], np.maximum(-x, 0))
                vv[:, b] = x + t; aa[:, p] = aa[:, p] - t; uu[best, b] = W - 1
                to = payee[q, g][p]
                for r in range(N):
                    k = np.nonzero(to // B == r)[0][:CAP]; s = q * CAP + np.arange(len(k))
                    w2[r, g][s] = to[k] % B; c2[r, g][:, s] = t[:, k]
        w, c = w2, c2
    return {"yv": v.reshape(N, 128, B).astype(np.float32).astype(BF), "yw": w.astype(np.float32), "yc": c.reshape(N, 128, L).astype(np.float32).astype(BF)}

@@ -1,0 +1,550 @@
+from concourse.bass import DstId, RemoteDMATransfer
+from concourse.mybir import AluOpType as O, ActivationFunctionType as F
+
+WIN = 2312
+SCRATCH = {}
+for _n in "wkb ci xi".split():
+    SCRATCH[_n] = ("sbuf", [128, 256], "int32")
+for _n in "wkf xz UI M1 M5 M6 SC5 SC6 t16 payf payg OHu UIn ywS cm land0 land1 land2".split():
+    SCRATCH[_n] = ("sbuf", [128, 256], "float32")
+for _n in "maskS rst ones V1 V2 NVr eqd eqe tt r8 sgn OH prod Vn An Agl cB".split():
+    SCRATCH[_n] = ("sbuf", [128, 256], "bfloat16")
+for _n in "blk1 blkT blk8 woff idB selb selL selC TTs0 TTs1".split():
+    SCRATCH[_n] = ("sbuf", [128, 128], "bfloat16")
+for _n in "BWu LWu OWu boU aoU".split():
+    SCRATCH[_n] = ("sbuf", [128, 16], "uint16")
+for _n in "xu Lu Uo".split():
+    SCRATCH[_n] = ("sbuf", [128, 256], "uint16")
+for _n in "NVx ge0 Ag ge1".split():
+    SCRATCH[_n] = ("sbuf", [128, 2048], "bfloat16")
+for _n in "onesF idF sel8 selT row0".split():
+    SCRATCH[_n] = ("sbuf", [128, 128], "float32")
+for _n in range(3):
+    SCRATCH["win%d" % _n] = ("sbuf", [128, WIN], "float32")
+for _n in range(8):
+    SCRATCH["b%d" % _n] = ("psum", [128, 512], "float32")
+for _n in range(2):
+    SCRATCH["so%d" % _n] = ("sbuf", [128, 64], "float32")
+    SCRATCH["mx%d" % _n] = ("sbuf", [128, 128], "float32")
+    SCRATCH["ki%d" % _n] = ("sbuf", [128, 8], "int32")
+    SCRATCH["digI%d" % _n] = ("sbuf", [128, 24], "int32")
+    SCRATCH["digB%d" % _n] = ("sbuf", [128, 32], "bfloat16")
+SCRATCH["quS"] = ("sbuf", [128, 1032], "int32")
+SCRATCH["ut"] = ("sbuf", [128, 1296], "float32")
+SCRATCH["vt"] = ("sbuf", [128, 1296], "bfloat16")
+SCRATCH["at"] = ("sbuf", [128, 3456], "bfloat16")
+SCRATCH["pt"] = ("sbuf", [128, 3200], "int32")
+SCRATCH["pq"] = ("sbuf", [128, 3200], "int32")
+SCRATCH["eqx"] = ("sbuf", [128, 3840], "bfloat16")
+SCRATCH["l15"] = ("sbuf", [128, 256], "int32")
+SCRATCH["l4"] = ("sbuf", [128, 128], "int32")
+SCRATCH["l16"] = ("sbuf", [128, 16], "int32")
+SCRATCH["pci"] = ("sbuf", [128, 8], "int32")
+SCRATCH["col"] = ("sbuf", [128, 32], "float32")
+SCRATCH["bs64"] = ("sbuf", [128, 8], "bfloat16")
+SCRATCH["dumpA"] = ("sbuf", [128, 16], "float32")
+SCRATCH["dumpB"] = ("sbuf", [128, 16], "float32")
+SCRATCH["sm"] = ("sbuf", [128, 192], "float32")
+SEMAPHORES = ["sv", "ss", "sp", "sg", "dwk", "dvp", "dqu", "dam", "dpq", "dpay", "dyv", "dyw", "dyc", "loc", "arr0", "arr1", "arr2"]
+NONE1 = 3200
+XKEY = 272 * 4096 + NONE1
+LOW = 2097152
+HALF = (XKEY + LOW) / 2.0
+MAGIC = 12582912.0
+XL = 224
+NV = 5
+ODD = list(range(1, 16, 2)) + list(range(0, 16, 2))
+ORDER0 = "a0 a1 a2 a4 a6 a7 a3 P0 a8 b0 b1 b2 b4 b6 b7 b3 P1 b8 a9 aa a5 ab b5 b9 ba bb".split()
+ORDER = "a0 a1 a2 a3 a4 P0 a6 a7 a8 b0 b1 b2 b3 b4 P1 b6 b7 b8 a9 aa a5 ab b5 b9 ba bb".split()
+
+
+def A(name, c0, c1, step=1, p0=0, p1=128):
+    return ("A", name, c0, c1, step, p0, p1)
+
+
+def IND(win, off):
+    return ("I", win, off)
+
+
+KB = ((A("b0", 0, 64), A("b5", 384, 448)), (A("b1", 0, 64), A("b6", 128, 192)))
+
+
+def KI(h, i):
+    k = KB[h][i % 2]
+    return A(k[1], k[2] + i // 2, k[3], 8)
+
+
+def is_view(x):
+    return isinstance(x, tuple) and len(x) > 0 and (x[0] == "A" or x[0] == "I")
+
+
+def hits(a, b):
+    if a[2] <= b[1] or b[2] <= a[1]:
+        return False
+    return not (a[3] > 1 and a[3] == b[3] and (a[1] - b[1]) % a[3] != 0)
+
+
+def is_psum(name):
+    return len(name) == 2 and name[0] == "b"
+
+
+def resolve(P, x):
+    if x[0] == "I":
+        return resolve(P, x[1]).indirect(resolve(P, x[2]))
+    t = P["T"][x[1]]
+    if x[4] == 1:
+        return t[x[5]:x[6], x[2]:x[3]]
+    return t[x[5]:x[6], x[2]:x[3]:x[4]]
+
+
+def regions(views):
+    out = []
+    for v in views:
+        if v[0] == "I":
+            out += regions([v[1], v[2]])
+        else:
+            out.append((v[1], v[2], v[3], v[4]))
+    return out
+
+
+def sync_for(P, q, reads, writes):
+    need = []
+    for kind, regs in (("r", reads), ("w", writes)):
+        for r in regs:
+            ps = is_psum(r[0])
+            for hk, hr, hq, sem, val, clock in P["hist"].get(r[0], []):
+                same = hq == q
+                if same or not ps:
+                    if (hk == "r" and (kind == "r" or same)) or (same and kind == "w" and q == "p") or not hits(r, hr):
+                        continue
+                need.append((sem, val, clock))
+    best = {}
+    for sem, val, clock in need:
+        if P["known"][q].get(sem, 0) < val and (sem not in best or best[sem][0] < val):
+            best[sem] = (val, clock)
+    for sem in list(best):
+        if any(s2 != sem and best[s2][1].get(sem, 0) >= best[sem][0] for s2 in best):
+            del best[sem]
+    for sem in best:
+        val, clock = best[sem]
+        P["eng"][q].wait_ge(P["T"].sem[sem], val)
+        k = P["known"][q]
+        for s2, v2 in clock.items():
+            if k.get(s2, 0) < v2:
+                k[s2] = v2
+
+
+def note(P, q, reads, writes, sem, val):
+    clock = dict(P["known"].get(q, {}))
+    clock[sem] = max(val, clock.get(sem, 0))
+    for kind, regs in (("r", reads), ("w", writes)):
+        for r in regs:
+            lst = P["hist"].setdefault(r[0], [])
+            if kind == "w" and r[3] == 1:
+                lst[:] = [h for h in lst if not (h[2] == q and r[1] <= h[1][1] and h[1][2] <= r[2])]
+            lst.append((kind, r, q, sem, val, clock))
+
+
+SEM_OF = {"v": "sv", "s": "ss", "p": "sp", "g": "sg"}
+
+
+def op(P, q, fn, out, *args, **kw):
+    reads = regions([a for a in args if is_view(a)] + [a for a in kw.values() if is_view(a)])
+    if out[0] == "I":
+        writes = regions([out[1]])
+        reads += regions([out[2]])
+    else:
+        writes = regions([out])
+    sync_for(P, q, reads, writes)
+    sem = SEM_OF[q]
+    P["cnt"][sem] += 1
+    fn(resolve(P, out), *[resolve(P, a) if is_view(a) else a for a in args],
+       **{k: (resolve(P, a) if is_view(a) else a) for k, a in kw.items()}).then_inc(P["T"].sem[sem], 1)
+    note(P, q, reads, writes, sem, P["cnt"][sem])
+
+
+def weave(first, second, start):
+    second = list(second)
+    for n, f in enumerate(first):
+        f()
+        if n >= start and second:
+            second.pop(0)()
+    for f in second:
+        f()
+
+
+def rank_program(g, core, T, topo):
+    me = T.rank_of(core)
+    if me is None:
+        return
+    v, s, pe, y = g.vector, g.scalar, g.tensor, g.sync
+    P = {"T": T, "hist": {}, "known": {q: {} for q in "vspyg"}, "cnt": {"sv": 0, "ss": 0, "sp": 0, "sg": 0},
+         "eng": {"v": v, "s": s, "p": pe, "y": y, "g": g}}
+
+    def cp(out, in_): op(P, "v", v.tensor_copy, out, in_)
+    def tt(out, a, b, o): op(P, "v", v.tensor_tensor, out, a, b, o)
+    def ts(out, a, s1, o1, s2=None, o2=None):
+        if o2 is None:
+            op(P, "v", v.tensor_scalar, out, a, s1, None, o1)
+        else:
+            op(P, "v", v.tensor_scalar, out, a, s1, s2, o1, o2)
+    def scan(out, d0, d1, ini=0.0): op(P, "v", v.tensor_tensor_scan, out, d0, d1, ini, O.mult, O.add)
+    def fill(out, c): op(P, "v", v.memset, out, c)
+    def act(out, in_, f, **kw): op(P, "s", s.activation, out, in_, f, **kw)
+    def mm(out, l, r, st, sp): op(P, "p", pe.matmul, out, l, r, st, sp)
+    def iota(out, pat, base, cm, **kw): op(P, "g", g.iota, out, pat, base, cm, **kw)
+    def pick(out, in_, pat, cmp, base, cm): op(P, "g", g.affine_select, out, in_, pat, cmp, 0.0, base, cm)
+    def H(name, h, c0=0): return A(name, c0 + 128 * h, c0 + 128 * h + 128)
+    def C(k, n=128): return A("col", k, k + 1, 1, 0, n)
+
+    def load(q, out, src, sem):
+        P["eng"][q].dma_start(resolve(P, out), src).then_inc(T.sem[sem], 16)
+        note(P, "d" + sem, [], regions([out]), sem, 16)
+    load("y", A("wkb", 0, 256, 1, 0, 8), T.wk[:], "dwk")
+    load("s", A("vt", 0, 1024), T.vp[:], "dvp")
+    load("y", A("quS", 0, 1024), T.qu[:], "dqu")
+    load("y", A("at", 0, 3200), T.am[:], "dam")
+
+    imp = {"allow_small_or_imprecise_dtypes": True}
+    iota(A("pci", 0, 1), [[1, 1]], 0, 1)
+    iota(A("l15", 0, 256), [[0, 16], [1, 16]], 0, 0)
+    iota(A("onesF", 0, 128), [[0, 128]], 1, 0, **imp)
+    pick(A("selT", 0, 128, 1, 0, 8), A("onesF", 0, 128, 1, 0, 8), [[1, 128]], O.is_ge, 0, -16)
+    pick(A("sel8", 0, 128, 1, 0, 8), A("selT", 0, 128, 1, 0, 8), [[-1, 128]], O.is_ge, 15, 16)
+    iota(A("l4", 0, 128), [[1, 8], [0, 16]], 0, 0)
+    iota(A("l16", 0, 16), [[16, 16]], 0, 0)
+    iota(A("ones", 0, 256), [[0, 256]], 1, 0, **imp)
+    pick(A("blkT", 0, 128), A("ones", 0, 128), [[-16, 8], [0, 16]], O.is_ge, 0, 1)
+    pick(A("blk1", 0, 128), A("blkT", 0, 128), [[16, 8], [0, 16]], O.is_ge, 15, -1)
+    pick(A("idF", 0, 128), A("onesF", 0, 128), [[-1, 128]], O.is_equal, 0, 1)
+    pick(A("row0", 0, 128), A("onesF", 0, 128), [[-16, 8], [0, 16]], O.is_equal, 0, 1)
+    pick(A("idB", 0, 128), A("ones", 0, 128), [[-1, 128]], O.is_equal, 0, 1)
+    iota(A("pq", 0, 3200), [[0, 3200]], 0, 0)
+    sync_for(P, "y", [], [("pq", 0, 3200, 1)])
+    y.dma_start(T.pq[0:128:16, :], T.pay[:]).then_inc(T.sem["dpq"], 16)
+    note(P, "dpq", [], [("pq", 0, 3200, 1)], "dpq", 16)
+    for j in range(16):
+        y.dma_start(T.pt[j:128:16, :], T.pay[:]).then_inc(T.sem["dpay"], 16)
+    note(P, "dpay", [], [("pt", 0, 3200, 1)], "dpay", 256)
+    for k in range(3):
+        for r in range(8):
+            iota(A("win%d" % k, 256 * r + 1, 256 * r + 33), [[0, 32]], 1024 * r + 1025 - 4096, 0, **imp)
+    p0 = A("pci", 0, 1)
+    ts(A("pci", 1, 2), p0, 15, O.bitwise_and)
+    ts(A("pci", 2, 3), p0, 3, O.arith_shift_right)
+    ts(A("pci", 3, 4), p0, 7, O.bitwise_and)
+    cp(A("col", 0, 4), A("pci", 0, 4))
+    PM, PD = C(1), C(2)
+    ADD1, NONEC, J256, NEG = C(4), C(5), C(8), C(9)
+    maskP = lambda h: H("b2", h)
+    SC = lambda h: H("b2", h, 256)
+    ts(A("b2", 0, 256), A("l15", 0, 256), PM, O.is_equal)
+    ts(A("rst", 0, 256), A("l15", 0, 256), 0.0, O.not_equal)
+    ts(NEG, PM, -4096.0, O.mult, -1.0, O.add)
+    ts(ADD1, PM, 4096.0, O.mult, 1.0, O.add)
+    ts(NONEC, PM, 4096.0, O.mult, float(NONE1), O.add)
+    ts(A("ut", 1024, 1032), A("l15", 0, 8), 0.0, O.mult, NONEC, O.add)
+    fill(A("quS", 1024, 1032), NONE1 - 1)
+    fill(A("vt", 1024, 1040), 0.0)
+    for a in list(range(7)) + list(range(8, 15)):
+        fill(A("eqx", 256 * a + (0 if a < 7 else 128), 256 * a + 16 * (a + 1)), 0.0)
+    blksel = A("blk1", 0, 128, 16)
+
+    def late_constants():
+        ts(A("maskS", 0, 256), A("l15", 0, 256), PM, O.is_equal)
+        ts(J256, PM, 256.0, O.mult)
+        ts(C(10), PD, 0.0, O.is_equal, 4096.0, O.mult)
+        ts(C(11), PD, 1.0, O.is_equal, 64.0, O.mult)
+        ts(C(12), PD, 2.0, O.is_equal)
+        ts(C(13), PD, 3.0, O.is_equal, 8192.0, O.mult)
+        ts(A("selb", 0, 128, 1, 0, 32), A("l4", 0, 128, 1, 0, 32), C(3, 32), O.is_equal)
+        tt(C(14), C(11), C(12), O.add)
+        ts(A("dumpB", 0, 16), A("l16", 0, 16), PM, O.add, 1025.0, O.add)
+        ts(A("dumpA", 0, 16), A("l16", 0, 16), PM, O.add, 3200.0, O.add)
+        tt(C(15), C(14), C(13), O.add)
+        tt(C(16), C(14), C(10), O.add)
+
+    def late_scalar():
+        act(A("bs64", 0, 8), blksel, F.Copy, scale=65536.0)
+        act(A("blk8", 0, 128), A("blk1", 0, 128), F.Copy, scale=8.0)
+        act(A("woff", 0, 128), A("blk1", 0, 128), F.Copy, scale=J256)
+        act(A("selL", 0, 128, 1, 0, 32), A("selb", 0, 128, 1, 0, 32), F.Copy, scale=C(15, 32))
+        act(A("selC", 0, 128, 1, 0, 32), A("selb", 0, 128, 1, 0, 32), F.Copy, scale=C(16, 32))
+
+    def pairs1():
+        for a in range(15):
+            c = 256 + 16 * a + 15
+            ts(A("eqx", 256 * a + 16 * (a + 1), 256 * a + 256), A("xu", 16 * (a + 1), 256), A("b2", c, c + 1), O.is_equal)
+
+    for st in range(3):
+        last = st == 2
+        win, land = "win%d" % st, "land%d" % st
+        base = 1 if st == 0 else 1 + 1024 * me
+        x = "xz" if st == 0 else "xi"
+        if st == 0:
+            ts(A("wkf", 0, 256, 1, 0, 8), A("wkb", 0, 256, 1, 0, 8), 1.0, O.add)
+            mm(A("b4", 256, 512), A("sel8", 0, 128, 1, 0, 8), A("wkf", 0, 256, 1, 0, 8), True, True)
+            late_constants()
+            for h in range(2):
+                cp(H("xz", h), H("b4", h, 256))
+        else:
+            old = "land%d" % (st - 1)
+            act(A("cm", 0, 256), A(old, 0, 256), F.Identity, bias=MAGIC, scale=1.0 / 16384)
+            act(A("cB", 0, 256), A("cm", 0, 256), F.Identity, bias=-MAGIC)
+            for h in range(2):
+                ts(H("ci", h), H(old, h), 4096.0, O.add)
+            for h in range(2):
+                ts(H("xi", h), H("ci", h), 16383, O.bitwise_and)
+        for h in range(2):
+            tt(H("M1", h), H(x, h), maskP(h), O.mult)
+        for h in range(2):
+            scan(SC(h), H("rst", h), H("M1", h))
+        scW = A("b2", 256 + 15, 512, 16)
+        ts(A("BWu", 0, 16), scW, float(-base), O.add)
+        BW = A("BWu", 0, 16)
+
+        def eqd1(h):
+            tt(H("eqd", h), SC(h), H(x, h), O.is_equal)
+        if st == 0:
+            cp(A("V2", 0, 256), IND(A("vt", 0, 1040), BW))
+            for h in range(2):
+                cp(H("xu", h), H(x, h))
+            for h in range(2):
+                eqd1(h)
+            pairs1()
+            cp(A("Uo", 0, 256), IND(A("quS", 0, 1032), BW))
+            ts(A("ut", 0, 1024), A("quS", 0, 1024), ADD1, O.add)
+            late_scalar()
+        else:
+            act(A("UI", 0, 256), IND(A("ut", 0, 1032), BW), F.Copy)
+            tt(A("V1", 0, 256), IND(A("vt", 0, 1040), BW), A("cB", 0, 256), O.subtract)
+            cp(H("xu", 0), H(x, 0))
+            ts(A("V2", 0, 256), A("V1", 0, 256), -255.0, O.max)
+            ts(A("Uo", 0, 256), A("UI", 0, 256), NEG, O.add)
+            cp(H("xu", 1), H(x, 1))
+            for h in range(2):
+                eqd1(h)
+            pairs1()
+        for i in range(16 - NV):
+            act(A("NVx", i, 2048, 16), A("V2", 0, 128), F.Copy, scale=-1.0)
+        for i in range(16 - NV, 16):
+            ts(A("NVx", i, 2048, 16), A("V2", 0, 128), -1.0, O.mult)
+        act(A("NVr", 0, 256), A("V2", 0, 256), F.Relu, scale=-1.0)
+        if st == 0:
+            act(A("UI", 0, 256), IND(A("ut", 0, 1032), BW), F.Copy)
+        act(A("b3", 128, XL), A("V2", 128, XL), F.Copy, scale=-1.0)
+        for c0, c1 in ((XL, 256), (128, 176), (176, XL)):
+            act(A("Ag", 16 * (c0 - 128), 16 * (c1 - 128)), IND(A("at", 0, 3200), A("Uo", c0, c1)), F.Copy)
+        for h in range(2):
+            for e in range(2):
+                mm(KB[h][e], H("UI", h), A("idF", e, 128, 2), True, False)
+        for h in range(2):
+            mm(A("b4", 8 * h, 8 * h + 8), H("NVr", h), blksel, True, True)
+        for h in range(2):
+            out = A("b4", 16 + 8 * h, 24 + 8 * h)
+            mm(out, H("eqd", h), blksel, True, False)
+            n = 7 if h == 0 else 15
+            for a in range(n):
+                mm(out, H("eqx", h, 256 * a), blksel, False, a == n - 1)
+        D0 = 16 * (XL - 128)
+        mm(A("b7", 0, 512), A("idB", 0, 128), A("Ag", D0, 2048), True, False)
+        for i in range(16):
+            mm(A("b7", i, 512, 16), A("idB", 0, 128), A("V2", XL, 256), False, i == 15)
+        act(A("ge1", D0, 2048), A("b7", 0, 512), F.Sign, bias=0.5)
+        tt(A("ge0", 0, 2048), IND(A("at", 0, 3200), A("Uo", 0, 128)), A("NVx", 0, 2048), O.is_ge)
+        for i in ODD:
+            mm(KI(0, i), A("ge0", i, 2048, 16), A("bs64", 0, 8), False, i >= 14)
+        act(A("so0", 0, 64), KB[0][1], F.Copy)
+        act(A("sm", 0, 16), A("b4", 0, 16), F.Sign, bias=-0.5)
+        act(A("sm", 16, 32), A("b4", 16, 32), F.Sign, bias=-1.5)
+        for h in range(2):
+            act(A("digB%d" % h, 24, 32), A("sm", 16 + 8 * h, 24 + 8 * h), F.Relu)
+        act(A("sm", 160, 176), A("sm", 0, 16), F.Identity, bias=HALF - LOW, scale=-HALF)
+        act(A("sm", 176, 192), A("sm", 16, 32), F.Identity, bias=HALF - LOW, scale=HALF)
+        RL = (H("b5", 0), A("b0", 128, 256))
+        CN = (A("b6", 0, 128), A("b7", 0, 128))
+        OFF = (A("b5", 256, 384), A("b1", 256, 384))
+
+        def best(h):
+            m = "mx%d" % h
+            ki, dI, dB, tp = A("ki%d" % h, 0, 8), "digI%d" % h, "digB%d" % h, A("b4", 128 + 128 * h, 256 + 128 * h, 1, 0, 32)
+            tr = A("TTs%d" % h, 0, 128, 1, 0, 32)
+
+            def row_digit():
+                if not last:
+                    ts(A(dI, 0, 8), ki, 12, O.arith_shift_right, 15, O.bitwise_and)
+
+            def to_r():
+                cp(A(dB, 0, 24), A(dI, 0, 24))
+                mm(tp, A(dB, 0, 32), A("idB", 0, 128), True, True)
+                act(tr, tp, F.Copy)
+                mm(RL[h], A("selL", 0, 128, 1, 0, 32), tr, True, True)
+                if not last:
+                    mm(H("b6", h, 256), A("selC", 0, 128, 1, 0, 32), tr, True, True)
+            return [lambda: tt(A(m, 0, 64), KB[h][0], A("so%d" % h, 0, 64), O.max),
+                    lambda: tt(A(m, 64, 96), A(m, 0, 64, 2), A(m, 1, 64, 2), O.max),
+                    lambda: tt(A(m, 96, 112), A(m, 64, 96, 2), A(m, 65, 96, 2), O.max),
+                    lambda: tt(A(m, 112, 120), A(m, 96, 112, 2), A(m, 97, 112, 2), O.max),
+                    lambda: tt(ki, A(m, 112, 120), A("sm", 32 + 8 * h, 40 + 8 * h), O.max),
+                    lambda: ts(A(dI, 8, 16), ki, 6, O.arith_shift_right, 63, O.bitwise_and),
+                    lambda: ts(A(dI, 16, 24), ki, 63, O.bitwise_and),
+                    row_digit, to_r]
+
+        def lines(h):
+            lw = A("LWu", 8 * h, 8 * h + 8)
+
+            def same():
+                tt(H("eqe", h), H("SC5", h), RL[h], O.is_equal)
+                mm(CN[h], A("blk8", 0, 128), H("eqe", h), True, False)
+
+            def to_w():
+                ts(lw, A("SC5", 128 * h + 15, 128 * h + 128, 16), float(NONE1), O.min, -1.0, O.add)
+                act(H("Agl", h), IND(A("at", 0, 3200), lw), F.Copy)
+
+            def draw():
+                tt(H("tt", h), H("Agl", h), H("b3", h), O.min)
+                act(H("t16", h), H("tt", h), F.Identity, bias=1.0 - 4096.0, scale=16384.0)
+
+            def payees():
+                if st > 0:
+                    cp(H("payf", h), IND(A("pt", 0, 3200), lw))
+                else:
+                    cp(H("payg", h), IND(A("pq", 0, 3200), lw))
+                    mm(H("b4", h, 128), A("row0", 0, 128), H("payg", h), True, True)
+                    act(H("payf", h), H("b4", h, 128), F.Copy)
+
+            def pay_r():
+                act(H("cm", h), H("payf", h), F.Identity, bias=-511.5 / 1024, scale=1.0 / 1024)
+                act(H("M1", h), H("cm", h), F.Identity, bias=MAGIC)
+                act(H("r8", h), H("M1", h), F.Identity, bias=-MAGIC - 8.0)
+
+            def one_hot():
+                ts(H("OH", h), CN[h], 8.0, O.min, PM, O.is_equal)
+                mm(OFF[h], A("woff", 0, 128), H("OH", h), True, False)
+
+            def product():
+                tt(H("prod", h), H("b3", h, 256), H("OH", h), O.mult)
+                mm(OFF[h], A("blk1", 0, 128), H("prod", h), False, True)
+            return [lambda: tt(H("M5", h), RL[h], H("maskS", h), O.mult),
+                    lambda: cp(H("Lu", h), RL[h]),
+                    lambda: scan(H("SC5", h), H("rst", h), H("M5", h)),
+                    same, to_w, draw, payees, pay_r,
+                    lambda: mm(CN[h], A("idB", 0, 128), H("r8", h), False, True),
+                    one_hot,
+                    lambda: scan(H("b3", h, 256), H("ones", h), H("OH", h), 0.0 if h == 0 else A("b3", 383, 384)),
+                    product]
+
+        def pairs5(h):
+            for a in range(7 if h == 0 else 15):
+                lo, c = max(128 * h, 16 * (a + 1)), 16 * a + 15
+                e = A("eqx", 256 * a + lo, 256 * a + 128 * h + 128)
+                ts(e, A("Lu", lo, 128 * h + 128), A("SC5", c, c + 1), O.is_equal)
+                mm(A(CN[h][1], lo - 128 * h, 128), A("blk8", 0, 128), e, False, False)
+
+        def ge1(i):
+            tt(A("ge1", i, D0, 16), A("Ag", i, D0, 16), A("b3", 128, XL), O.is_ge)
+            mm(KI(1, i), A("ge1", i, 2048, 16), A("bs64", 0, 8), False, i >= 14)
+            if i == 15:
+                act(A("so1", 0, 64), KB[1][1], F.Copy)
+        best0, lines0, lines1 = best(0), lines(0), lines(1)
+        no_key = lambda: tt(A("sm", 32, 48), A("sm", 160, 176), A("sm", 176, 192), O.max)
+        weave([lambda i=i: ge1(i) for i in ODD], best0[:3] + [no_key] + best0[3:], 11)
+        for f in best(1):
+            f()
+        act(A("b3", 0, 256), A("V2", 0, 256), F.Relu, scale=-1.0)
+        if not last:
+            fill(A("pq" if st == 0 else "pt", 3199, 3200), 8192)
+        calls = {"P0": lambda: pairs5(0), "P1": lambda: pairs5(1)}
+        for k in range(12):
+            calls["a%x" % k], calls["b%x" % k] = lines0[k], lines1[k]
+        for k in ORDER0 if st == 0 else ORDER:
+            calls[k]()
+        for h in range(2):
+            act(H("sgn", h), CN[h], F.Sign, bias=7.5, scale=-1.0)
+            act(H("b3", h, 256), H("sgn", h), F.Relu)
+        tm = A("b3", 0, 256)
+        tt(H("M6", 0), OFF[0], H("maskS", 0), O.mult)
+        tt(H("M6", 1), OFF[1], H("maskS", 1), O.mult)
+        for h in range(2):
+            scan(H("SC6", h), H("rst", h), H("M6", h))
+        o6, l5 = A("SC6", 15, 256, 16), A("SC5", 15, 256, 16)
+        ts(A("sm", 64, 80), scW, float(-base), O.add)
+        ts(A("sm", 48, 64), l5, 4096.0, O.is_gt)
+        cp(A("OWu", 0, 16), o6)
+        tt(IND(A(win, 0, WIN), A("OWu", 0, 16)), A("t16", 0, 256), A("payf", 0, 256), O.add)
+        sync_for(P, "g", [(win, 0, WIN, 1)], [])
+        sends = plan(topo, T.cores, me)
+        for c in sends:
+            g.remote_dma_fused([RemoteDMATransfer(
+                dst_ids=[DstId(rid=topo.addr(T.cores[r], core)[0], pnc=topo.addr(T.cores[r], core)[1])],
+                dma_engine_mask=sum(1 << e for e in engines), remote_sem=T.sem["arr%d" % st],
+                src=T[win][:, 256 * r + 1:256 * r + 33], dst=T[land][:, 32 * me:32 * me + 32])
+                for r, engines in c], local_sem=T.sem["loc"])
+        out_n = sum(len(e) for c in sends for r, e in c)
+        arrive = sum(len(e) for q in range(8) if q != me for c in plan(topo, T.cores, q) for r, e in c if r == me)
+        for q in range(8):
+            if q != me:
+                note(P, "remote", [], [(land, 32 * q, 32 * q + 32, 1)], "arr%d" % st, arrive)
+        cp(A(land, 32 * me, 32 * me + 32), A(win, 256 * me + 1, 256 * me + 33))
+        tt(tm, A("b3", 256, 512), A("tt", 0, 256), O.mult)
+        tt(A("sm", 48, 64), A("sm", 48, 64), A("dumpB", 0, 16), O.mult)
+        tt(A("Vn", 0, 256), tm, A("V2", 0, 256), O.add)
+        tt(A("sm", 80, 96), A("sm", 48, 64), A("sm", 64, 80), O.max)
+        if not last:
+            tt(A("OHu", 0, 256), A("b6", 256, 512), A("UI", 0, 256), O.is_equal)
+        cp(A("boU", 0, 16), A("sm", 80, 96))
+        if not last:
+            for h in range(2):
+                act(H("b7", h, 128), H("sgn", h), F.Relu, scale=NONEC)
+            ts(A("sm", 96, 112), o6, 2048.5, O.is_gt)
+            ts(A("sm", 112, 128), l5, float(NONE1), O.min, -1.0, O.add)
+        cp(IND(A("vt", 0, 1296), A("boU", 0, 16)), A("Vn", 0, 256))
+        if last:
+            break
+        okX = A("b7", 128, 384)
+        tt(okX, okX, A("OHu", 0, 256), O.mult)
+        tt(A("sm", 128, 144), A("sm", 96, 112), A("dumpA", 0, 16), O.mult)
+        tt(A("UIn", 0, 256), A("UI", 0, 256), okX, O.max)
+        tt(A("sm", 144, 160), A("sm", 128, 144), A("sm", 112, 128), O.max)
+        tt(A("An", 0, 256), A("Agl", 0, 256), tm, O.subtract)
+        cp(A("aoU", 0, 16), A("sm", 144, 160))
+        cp(IND(A("ut", 0, 1296), A("boU", 0, 16)), A("UIn", 0, 256))
+        cp(IND(A("at", 0, 3456), A("aoU", 0, 16)), A("An", 0, 256))
+
+    sync_for(P, "y", [("vt", 0, 1024, 1)], [])
+    y.dma_start(T.yv[:], T.vt[:, 0:1024]).then_inc(T.sem["dyv"], 16)
+    act(A("cm", 0, 256), A("land2", 0, 256), F.Identity, bias=MAGIC, scale=1.0 / 16384)
+    act(A("cB", 0, 256), A("cm", 0, 256), F.Identity, bias=-MAGIC)
+    for h in range(2):
+        ts(H("ci", h), H("land2", h), 4096.0, O.add)
+    for h in range(2):
+        ts(H("xi", h), H("ci", h), 16383, O.bitwise_and)
+    for h in range(2):
+        ts(H("ywS", h), H("xi", h), float(-(1 + 1024 * me)), O.add)
+    sync_for(P, "s", regions([A("cB", 0, 256)]), [])
+    s.dma_start(T.yc[:], T.cB[:, 0:256]).then_inc(T.sem["dyc"], 16)
+    sync_for(P, "y", regions([A("ywS", 0, 256)]), [])
+    y.dma_start(T.yw[:], T.ywS[0:128:16, 0:256]).then_inc(T.sem["dyw"], 16)
+    for sem in ("sv", "ss", "sp", "sg"):
+        g.wait_ge(T.sem[sem], P["cnt"][sem])
+    for sem in ("dwk", "dvp", "dqu", "dam", "dpq", "dyv", "dyw", "dyc"):
+        g.wait_ge(T.sem[sem], 16)
+    g.wait_ge(T.sem["dpay"], 256)
+    g.wait_ge(T.sem["loc"], 3 * out_n)
+    for k in range(3):
+        g.wait_ge(T.sem["arr%d" % k], arrive)
+
+
+def plan(topo, cores, q):
+    src = cores[q]
+    others = [(q + k) % len(cores) for k in range(1, len(cores))]
+    near = [r for r in others if cores[r] in topo.cores_of(src)]
+    far = [r for r in others if r not in near]
+    far.sort(key=lambda r: topo.same_plane(src, cores[r]) or topo.mates(src, cores[r]))
+    out = [e for e in topo.engines(src, cores[far[0]])]
+    inside = [e for e in topo.engines(src, cores[near[0]]) if e not in out]
+    n = len(out) // 4
+    first = [(r, out[n * k:n * k + n]) for k, r in enumerate(far[:4])]
+    first += [(r, inside[n * k:n * k + n]) for k, r in enumerate(near)]
+    m = len(out) // 2
+    return [first, [(r, out[m * k:m * k + m]) for k, r in enumerate(far[4:])]]

@@ -1,61 +1,60 @@
 from concourse.bass import DstId, RemoteDMATransfer
 from concourse.mybir import AluOpType as O, ActivationFunctionType as F
 
-WIN = 2312
+WIN = 4096
 SCRATCH = {}
-for _n in "wkb ci xi".split():
-    SCRATCH[_n] = ("sbuf", [128, 256], "int32")
-for _n in "wkf xz UI M1 M5 M6 SC5 SC6 t16 payf payg OHu UIn ywS cm land0 land1 land2".split():
+for _n in "land0 land1 land2 land3 M1 SC cm cm2 UI sS M5 SC5 G t32 M6 SC6 ywS E r32".split():
     SCRATCH[_n] = ("sbuf", [128, 256], "float32")
-for _n in "maskS rst ones V1 V2 NVr eqd eqe tt r8 sgn OH prod Vn An Agl cB".split():
+for _n in "maskS rst ones V1 V2 NVr eqd eqe w nsgn OH Agl nt tm cB".split():
     SCRATCH[_n] = ("sbuf", [128, 256], "bfloat16")
-for _n in "blk1 blkT blk8 woff idB selb selL selC TTs0 TTs1".split():
+for _n in "xh wkh pU prod".split():
+    SCRATCH[_n] = ("sbuf", [128, 256], "float16")
+for _n in "blk1 blkT blkZ blkL blkS blk2 idB nI DM DM0 W5 W5a W5b TC S8 PB PB0 sel8 selT".split():
     SCRATCH[_n] = ("sbuf", [128, 128], "bfloat16")
-for _n in "BWu LWu OWu boU aoU".split():
-    SCRATCH[_n] = ("sbuf", [128, 16], "uint16")
-for _n in "xu Lu Uo".split():
+for _n in "Lu Uo".split():
     SCRATCH[_n] = ("sbuf", [128, 256], "uint16")
-for _n in "NVx ge0 Ag ge1".split():
-    SCRATCH[_n] = ("sbuf", [128, 2048], "bfloat16")
-for _n in "onesF idF sel8 selT row0".split():
-    SCRATCH[_n] = ("sbuf", [128, 128], "float32")
+for _n in "BWu LWu OWu boU".split():
+    SCRATCH[_n] = ("sbuf", [128, 16], "uint16")
+for _n in "ge Ag eqx".split():
+    SCRATCH[_n] = ("sbuf", [128, 4096], "bfloat16")
 for _n in range(3):
     SCRATCH["win%d" % _n] = ("sbuf", [128, WIN], "float32")
 for _n in range(8):
     SCRATCH["b%d" % _n] = ("psum", [128, 512], "float32")
-for _n in range(2):
-    SCRATCH["so%d" % _n] = ("sbuf", [128, 64], "float32")
-    SCRATCH["mx%d" % _n] = ("sbuf", [128, 128], "float32")
-    SCRATCH["ki%d" % _n] = ("sbuf", [128, 8], "int32")
-    SCRATCH["digI%d" % _n] = ("sbuf", [128, 24], "int32")
-    SCRATCH["digB%d" % _n] = ("sbuf", [128, 32], "bfloat16")
-SCRATCH["quS"] = ("sbuf", [128, 1032], "int32")
-SCRATCH["ut"] = ("sbuf", [128, 1296], "float32")
-SCRATCH["vt"] = ("sbuf", [128, 1296], "bfloat16")
-SCRATCH["at"] = ("sbuf", [128, 3456], "bfloat16")
-SCRATCH["pt"] = ("sbuf", [128, 3200], "int32")
-SCRATCH["pq"] = ("sbuf", [128, 3200], "int32")
-SCRATCH["eqx"] = ("sbuf", [128, 3840], "bfloat16")
+SCRATCH["wkb"] = ("sbuf", [128, 256], "int32")
 SCRATCH["l15"] = ("sbuf", [128, 256], "int32")
+SCRATCH["i144"] = ("sbuf", [128, 144], "int32")
 SCRATCH["l4"] = ("sbuf", [128, 128], "int32")
 SCRATCH["l16"] = ("sbuf", [128, 16], "int32")
 SCRATCH["pci"] = ("sbuf", [128, 8], "int32")
-SCRATCH["col"] = ("sbuf", [128, 32], "float32")
-SCRATCH["bs64"] = ("sbuf", [128, 8], "bfloat16")
-SCRATCH["dumpA"] = ("sbuf", [128, 16], "float32")
+SCRATCH["selB"] = ("sbuf", [128, 144], "bfloat16")
+SCRATCH["quS"] = ("sbuf", [128, 1024], "int32")
+SCRATCH["payS"] = ("sbuf", [128, 400], "int32")
+SCRATCH["payI"] = ("sbuf", [128, 400], "int32")
+SCRATCH["payH"] = ("sbuf", [128, 400], "float16")
+SCRATCH["PL"] = ("sbuf", [128, 1024], "bfloat16")
+SCRATCH["ut"] = ("sbuf", [128, WIN], "float32")
+SCRATCH["vt"] = ("sbuf", [128, 1296], "bfloat16")
+SCRATCH["at"] = ("sbuf", [128, WIN], "bfloat16")
+SCRATCH["pt"] = ("sbuf", [128, 3200], "float32")
+SCRATCH["col"] = ("sbuf", [128, 48], "float32")
 SCRATCH["dumpB"] = ("sbuf", [128, 16], "float32")
-SCRATCH["sm"] = ("sbuf", [128, 192], "float32")
-SEMAPHORES = ["sv", "ss", "sp", "sg", "dwk", "dvp", "dqu", "dam", "dpq", "dpay", "dyv", "dyw", "dyc", "loc", "arr0", "arr1", "arr2"]
-NONE1 = 3200
-XKEY = 272 * 4096 + NONE1
-LOW = 2097152
-HALF = (XKEY + LOW) / 2.0
+SCRATCH["uaU"] = ("sbuf", [128, 32], "uint16")
+SCRATCH["sm"] = ("sbuf", [128, 96], "float32")
+SEMAPHORES = ["sv", "ss", "sp", "sg", "dwk", "dvp", "dqu", "dam", "dpa", "dpb", "dyv", "dyw", "dyc", "loc", "arr0", "arr1", "arr2"]
+NONE = 3199
 MAGIC = 12582912.0
-XL = 224
-NV = 5
-ODD = list(range(1, 16, 2)) + list(range(0, 16, 2))
-ORDER0 = "a0 a1 a2 a4 a6 a7 a3 P0 a8 b0 b1 b2 b4 b6 b7 b3 P1 b8 a9 aa a5 ab b5 b9 ba bb".split()
-ORDER = "a0 a1 a2 a3 a4 P0 a6 a7 a8 b0 b1 b2 b3 b4 P1 b6 b7 b8 a9 aa a5 ab b5 b9 ba bb".split()
+U0 = NONE - 2048
+WR = 17 * 2 ** 17
+BIG = 2 ** 22
+T0 = 17 * 2 ** 16
+KS = 2304
+RL0 = U0 + 15 * 2048 + 16 * KS
+BETA, THETA = 0.58, 0.40625
+CHUNKS = [(192, 256), (128, 192), (64, 128), (0, 64)]
+GROUPS = [(128, 256), (64, 128), (0, 64)]
+SBANK, RBANK = ["b3", "b4", "b2"], ["b5", "b6", "b5"]
+THR = ["b1", "b7"]
 
 
 def A(name, c0, c1, step=1, p0=0, p1=128):
@@ -64,14 +63,6 @@ def A(name, c0, c1, step=1, p0=0, p1=128):
 
 def IND(win, off):
     return ("I", win, off)
-
-
-KB = ((A("b0", 0, 64), A("b5", 384, 448)), (A("b1", 0, 64), A("b6", 128, 192)))
-
-
-def KI(h, i):
-    k = KB[h][i % 2]
-    return A(k[1], k[2] + i // 2, k[3], 8)
 
 
 def is_view(x):
@@ -115,7 +106,7 @@ def sync_for(P, q, reads, writes):
             for hk, hr, hq, sem, val, clock in P["hist"].get(r[0], []):
                 same = hq == q
                 if same or not ps:
-                    if (hk == "r" and (kind == "r" or same)) or (same and kind == "w" and q == "p") or not hits(r, hr):
+                    if (hk == "r" and kind == "r") or (same and kind == "w" and q == "p") or not hits(r, hr):
                         continue
                 need.append((sem, val, clock))
     best = {}
@@ -163,16 +154,6 @@ def op(P, q, fn, out, *args, **kw):
     note(P, q, reads, writes, sem, P["cnt"][sem])
 
 
-def weave(first, second, start):
-    second = list(second)
-    for n, f in enumerate(first):
-        f()
-        if n >= start and second:
-            second.pop(0)()
-    for f in second:
-        f()
-
-
 def rank_program(g, core, T, topo):
     me = T.rank_of(core)
     if me is None:
@@ -193,343 +174,333 @@ def rank_program(g, core, T, topo):
     def act(out, in_, f, **kw): op(P, "s", s.activation, out, in_, f, **kw)
     def mm(out, l, r, st, sp): op(P, "p", pe.matmul, out, l, r, st, sp)
     def iota(out, pat, base, cm, **kw): op(P, "g", g.iota, out, pat, base, cm, **kw)
-    def pick(out, in_, pat, cmp, base, cm): op(P, "g", g.affine_select, out, in_, pat, cmp, 0.0, base, cm)
+    def pick(out, in_, pat, cmp, base, cm, fill=0.0): op(P, "g", g.affine_select, out, in_, pat, cmp, fill, base, cm)
     def H(name, h, c0=0): return A(name, c0 + 128 * h, c0 + 128 * h + 128)
-    def C(k, n=128): return A("col", k, k + 1, 1, 0, n)
+    def R(name, lo=0, hi=256, c0=0): return A(name, c0 + lo, c0 + hi)
+    def W(name, lo=0, hi=256): return A(name, lo + 15, hi, 16)
+    def M(name): return A(name, 0, 128)
+    def C(k): return A("col", k, k + 1)
 
     def load(q, out, src, sem):
         P["eng"][q].dma_start(resolve(P, out), src).then_inc(T.sem[sem], 16)
         note(P, "d" + sem, [], regions([out]), sem, 16)
     load("y", A("wkb", 0, 256, 1, 0, 8), T.wk[:], "dwk")
     load("s", A("vt", 0, 1024), T.vp[:], "dvp")
+    load("y", A("payS", 0, 400, 1, 0, 64), T.pay[:], "dpa")
+    load("y", A("payS", 0, 400, 1, 64, 128), T.pay[:], "dpb")
     load("y", A("quS", 0, 1024), T.qu[:], "dqu")
     load("y", A("at", 0, 3200), T.am[:], "dam")
 
     imp = {"allow_small_or_imprecise_dtypes": True}
+
+    def block(out, tmp, src):
+        pick(tmp, src, [[-16, 8], [0, 16]], O.is_ge, 0, 1)
+        pick(out, tmp, [[16, 8], [0, 16]], O.is_ge, 15, -1)
     iota(A("pci", 0, 1), [[1, 1]], 0, 1)
-    iota(A("l15", 0, 256), [[0, 16], [1, 16]], 0, 0)
-    iota(A("onesF", 0, 128), [[0, 128]], 1, 0, **imp)
-    pick(A("selT", 0, 128, 1, 0, 8), A("onesF", 0, 128, 1, 0, 8), [[1, 128]], O.is_ge, 0, -16)
+    iota(R("l15"), [[0, 16], [1, 16]], 0, 0)
+    iota(R("ones"), [[0, 256]], 1, 0, **imp)
+    pick(A("selT", 0, 128, 1, 0, 8), A("ones", 0, 128, 1, 0, 8), [[1, 128]], O.is_ge, 0, -16)
     pick(A("sel8", 0, 128, 1, 0, 8), A("selT", 0, 128, 1, 0, 8), [[-1, 128]], O.is_ge, 15, 16)
-    iota(A("l4", 0, 128), [[1, 8], [0, 16]], 0, 0)
-    iota(A("l16", 0, 16), [[16, 16]], 0, 0)
-    iota(A("ones", 0, 256), [[0, 256]], 1, 0, **imp)
-    pick(A("blkT", 0, 128), A("ones", 0, 128), [[-16, 8], [0, 16]], O.is_ge, 0, 1)
-    pick(A("blk1", 0, 128), A("blkT", 0, 128), [[16, 8], [0, 16]], O.is_ge, 15, -1)
-    pick(A("idF", 0, 128), A("onesF", 0, 128), [[-1, 128]], O.is_equal, 0, 1)
-    pick(A("row0", 0, 128), A("onesF", 0, 128), [[-16, 8], [0, 16]], O.is_equal, 0, 1)
-    pick(A("idB", 0, 128), A("ones", 0, 128), [[-1, 128]], O.is_equal, 0, 1)
-    iota(A("pq", 0, 3200), [[0, 3200]], 0, 0)
-    sync_for(P, "y", [], [("pq", 0, 3200, 1)])
-    y.dma_start(T.pq[0:128:16, :], T.pay[:]).then_inc(T.sem["dpq"], 16)
-    note(P, "dpq", [], [("pq", 0, 3200, 1)], "dpq", 16)
-    for j in range(16):
-        y.dma_start(T.pt[j:128:16, :], T.pay[:]).then_inc(T.sem["dpay"], 16)
-    note(P, "dpay", [], [("pt", 0, 3200, 1)], "dpay", 256)
-    for k in range(3):
-        for r in range(8):
-            iota(A("win%d" % k, 256 * r + 1, 256 * r + 33), [[0, 32]], 1024 * r + 1025 - 4096, 0, **imp)
+    iota(M("l4"), [[1, 8], [0, 16]], 0, 0)
+    iota(A("i144", 0, 144), [[1, 144]], 0, 0)
+    block(M("blk1"), M("blkT"), M("ones"))
     p0 = A("pci", 0, 1)
     ts(A("pci", 1, 2), p0, 15, O.bitwise_and)
-    ts(A("pci", 2, 3), p0, 3, O.arith_shift_right)
-    ts(A("pci", 3, 4), p0, 7, O.bitwise_and)
-    cp(A("col", 0, 4), A("pci", 0, 4))
-    PM, PD = C(1), C(2)
-    ADD1, NONEC, J256, NEG = C(4), C(5), C(8), C(9)
-    maskP = lambda h: H("b2", h)
-    SC = lambda h: H("b2", h, 256)
-    ts(A("b2", 0, 256), A("l15", 0, 256), PM, O.is_equal)
-    ts(A("rst", 0, 256), A("l15", 0, 256), 0.0, O.not_equal)
-    ts(NEG, PM, -4096.0, O.mult, -1.0, O.add)
-    ts(ADD1, PM, 4096.0, O.mult, 1.0, O.add)
-    ts(NONEC, PM, 4096.0, O.mult, float(NONE1), O.add)
-    ts(A("ut", 1024, 1032), A("l15", 0, 8), 0.0, O.mult, NONEC, O.add)
-    fill(A("quS", 1024, 1032), NONE1 - 1)
+    ts(A("pci", 2, 3), p0, 7, O.bitwise_and)
+    ts(A("pci", 3, 4), p0, 3, O.arith_shift_right, 7, O.bitwise_and)
+    ts(A("pci", 4, 5), p0, 6, O.arith_shift_right)
+    cp(A("col", 0, 5), A("pci", 0, 5))
+    PM, J8, SCE, BPT, Q, SIG, SG, K0, K1, K2, K3 = C(1), C(5), C(6), C(7), C(8), C(9), C(10), C(11), C(12), C(13), C(14)
+    EJ, INI, NOW, EQ8 = C(16), C(17), C(18), C(19)
+    maskP, nP, SCc, XP, Z = "b0", "b0", "b1", "b2", "b2"
+
+    def add_thr(l, rhs, c0, lo, hi, start=False, stop=False, halves=(0, 1)):
+        for h in halves:
+            a, b = max(lo, 128 * h), min(hi, 128 * h + 128)
+            if a < b:
+                mm(A(THR[h], 256 + a, 256 + b), l, A(rhs, c0 + a, c0 + b), start, stop)
+    ts(J8, PM, 8.0, O.is_lt)
+    ts(R(maskP), R("l15"), PM, O.is_equal)
+    ts(SCE, J8, float(WR), O.mult)
+    ts(C(20), J8, float(-WR), O.mult, float(WR + 1024), O.add)
+    ts(R("rst"), R("l15"), 0.0, O.not_equal)
+    ts(C(21), SCE, PM, O.mult)
+    ts(EQ8, PM, 8.0, O.is_equal)
+    tt(BPT, C(20), C(21), O.subtract)
+    ts(C(22), SCE, float(me), O.mult, -1024.0, O.add)
+    ts(C(23), C(0), PM, O.subtract, 16.0, O.add)
+    tt(Q, C(22), BPT, O.add)
+    ts(C(24), C(4), float(WR - 1024), O.mult, 1024.0, O.add)
+    ts(C(25), PM, BETA, O.mult, -7.5 * BETA, O.add)
+    ts(C(26), Q, 0.0, O.is_ge, 2.0, O.mult)
+    ts(K0, Q, 1024.0, O.add)
+    ts(K1, Q, -1.0 / 1024, O.mult, -0.75, O.add)
+    ts(SIG, C(26), -1.0, O.add)
+    ts(K2, Q, -1.0 / 1024, O.mult, 1023.0, O.add)
+    ts(K3, Q, -1.0 / 1024, O.mult, MAGIC + 1023.0, O.add)
+    ts(SG, SIG, 1.0 / 1024, O.mult)
+    act(EJ, C(25), F.Exp)
     fill(A("vt", 1024, 1040), 0.0)
-    for a in list(range(7)) + list(range(8, 15)):
-        fill(A("eqx", 256 * a + (0 if a < 7 else 128), 256 * a + 16 * (a + 1)), 0.0)
-    blksel = A("blk1", 0, 128, 16)
+    fill(A("ut", 1024, 1032), 1.0)
+
+    def payee_table():
+        ts(M("PB0"), M("l4"), C(3), O.is_equal, C(24), O.mult)
+        ts(A("col", 32, 40), A("i144", 0, 8), C(2), O.is_equal)
+        ts(C(31), C(4), -8.0, O.mult, 16.0, O.add)
+        ts(A("payI", 0, 400, 1, 0, 64), A("payS", 0, 400, 1, 0, 64), 1023, O.bitwise_and)
+        ts(M("DM0"), M("l15"), C(31), O.is_lt)
+        ts(A("payI", 0, 400, 1, 64, 128), A("payS", 0, 400, 1, 64, 128), 10, O.arith_shift_right)
+        tt(M("PB"), M("PB0"), M("DM0"), O.mult)
+        cp(A("payH", 0, 400), A("payI", 0, 400))
+        for c in range(8):
+            ts(A("PL", 128 * c, 128 * c + 128), M("PB"), C(32 + c), O.mult)
+            bank = A("b%d" % (3 + c % 4), 0, 400)
+            mm(bank, A("PL", 128 * c, 128 * c + 128), A("payH", 0, 400), True, True)
+            act(A("pt", 400 * c, 400 * c + 400), bank, F.Abs, bias=BPT)
+        ts(NOW, EQ8, float(-WR), O.mult, float(WR), O.add)
+        act(A("pt", NONE, NONE + 1), NOW, F.Copy)
+
+    def pool_constants():
+        iota(R("r32"), [[1, 8], [0, 32]], 0, 0, **imp)
+        pick(M("idB"), M("ones"), [[-1, 128]], O.is_equal, 0, 1)
+        iota(M("W5a"), [[0, 128]], -BIG, 0, **imp)
+        iota(A("l16", 0, 16), [[16, 16]], 0, 0)
+        pick(M("W5b"), M("W5a"), [[0, 8], [1, 16]], O.not_equal, -8, 0, float(BIG))
+        block(M("W5"), M("W5a"), M("W5b"))
+        ts(C(30), BPT, 1024.0 * 1024, O.add)
+        act(R("E"), R("r32"), F.Abs, scale=SCE, bias=C(30))
+        for k in range(3):
+            for r in range(8):
+                pick(A("win%d" % k, 256 * r, 256 * r + 32), A("E", 32 * r, 32 * r + 32), [[0, 32]], O.is_ge, 0, 0)
 
     def late_constants():
-        ts(A("maskS", 0, 256), A("l15", 0, 256), PM, O.is_equal)
-        ts(J256, PM, 256.0, O.mult)
-        ts(C(10), PD, 0.0, O.is_equal, 4096.0, O.mult)
-        ts(C(11), PD, 1.0, O.is_equal, 64.0, O.mult)
-        ts(C(12), PD, 2.0, O.is_equal)
-        ts(C(13), PD, 3.0, O.is_equal, 8192.0, O.mult)
-        ts(A("selb", 0, 128, 1, 0, 32), A("l4", 0, 128, 1, 0, 32), C(3, 32), O.is_equal)
-        tt(C(14), C(11), C(12), O.add)
+        ts(A("selB", 0, 144), A("i144", 0, 144), C(23), O.is_equal)
+        ts(R("maskS"), R("l15"), PM, O.is_equal)
+        ts(M("blkL"), M("blk1"), 2048.0, O.mult)
+        ts(M("blkS"), M("blk1"), float(KS), O.mult)
+        ts(M("blk2"), M("blk1"), 2.0, O.mult)
+        ts(C(27), EQ8, -512.0, O.mult)
+        ts(C(28), EQ8, -2.0 * BIG, O.mult, float(T0 + BIG), O.add)
+        ts(C(29), EQ8, 1792.0, O.mult, -2049.0, O.add)
+        ts(M("DM0"), M("blk1"), -THETA, O.mult)
+        ts(M("S8"), M("blk1"), C(27), O.mult)
+        ts(M("TC"), M("idB"), C(28), O.mult)
+        ts(INI, PM, 256.0, O.mult, C(29), O.add)
+        tt(M("DM0"), M("DM0"), M("idB"), O.add)
+        ts(M("nI"), M("idB"), -1.0, O.mult)
         ts(A("dumpB", 0, 16), A("l16", 0, 16), PM, O.add, 1025.0, O.add)
-        ts(A("dumpA", 0, 16), A("l16", 0, 16), PM, O.add, 3200.0, O.add)
-        tt(C(15), C(14), C(13), O.add)
-        tt(C(16), C(14), C(10), O.add)
+        ts(M("DM"), M("DM0"), EJ, O.mult)
 
-    def late_scalar():
-        act(A("bs64", 0, 8), blksel, F.Copy, scale=65536.0)
-        act(A("blk8", 0, 128), A("blk1", 0, 128), F.Copy, scale=8.0)
-        act(A("woff", 0, 128), A("blk1", 0, 128), F.Copy, scale=J256)
-        act(A("selL", 0, 128, 1, 0, 32), A("selb", 0, 128, 1, 0, 32), F.Copy, scale=C(15, 32))
-        act(A("selC", 0, 128, 1, 0, 32), A("selb", 0, 128, 1, 0, 32), F.Copy, scale=C(16, 32))
+    def whole(src):
+        for h in range(2):
+            act(H("cm", h), H(src, h), F.Identity, bias=MAGIC, scale=1.0 / 1024)
+        for h in range(2):
+            act(H(XP, h), H("cm", h), F.Identity, bias=-1024.0 * MAGIC, scale=1024.0)
 
-    def pairs1():
-        for a in range(15):
-            c = 256 + 16 * a + 15
-            ts(A("eqx", 256 * a + 16 * (a + 1), 256 * a + 256), A("xu", 16 * (a + 1), 256), A("b2", c, c + 1), O.is_equal)
+    wk8 = A("wkh", 0, 256, 1, 0, 8)
+    cp(wk8, A("wkb", 0, 256, 1, 0, 8))
+    mm(R("b7"), A("sel8", 0, 128, 1, 0, 8), wk8, True, True)
+    payee_table()
+    ts(R("cm"), R("b7"), 1024.0, O.mult, K0, O.add)
+    ts(M("blkZ"), M("blk1"), -16384.0, O.mult)
+    ts(R("land0"), R("cm"), SIG, O.mult)
 
     for st in range(3):
-        last = st == 2
-        win, land = "win%d" % st, "land%d" % st
-        base = 1 if st == 0 else 1 + 1024 * me
-        x = "xz" if st == 0 else "xi"
-        if st == 0:
-            ts(A("wkf", 0, 256, 1, 0, 8), A("wkb", 0, 256, 1, 0, 8), 1.0, O.add)
-            mm(A("b4", 256, 512), A("sel8", 0, 128, 1, 0, 8), A("wkf", 0, 256, 1, 0, 8), True, True)
+        first, last = st == 0, st == 2
+        old, win, land = "land%d" % st, "win%d" % st, "land%d" % (st + 1)
+
+        def queues(lo, hi):
+            return IND(A("ut", 0, 1032), A("BWu", lo // 16, hi // 16))
+
+        def entries_top():
+            ts(R("Uo", 192, 256), queues(192, 256), 2048.0, O.mult, float(U0), O.add)
+
+        def entries_rest():
+            cp(R("UI", 0, 192), queues(0, 192))
+
+        def lists_rest():
+            ts(R("Uo", 0, 192), R("UI", 0, 192), 2048.0, O.mult, float(U0), O.add)
+
+        def gather(lo, hi):
+            act(A("Ag", 16 * lo, 16 * hi), IND(A("at", 0, 3200), R("Uo", lo, hi)), F.Copy)
+
+        def compare(lo, hi):
+            k = [n for n, (a, b) in enumerate(GROUPS) if a <= lo < b][0]
+            out = A(SBANK[k], lo - GROUPS[k][0], hi - GROUPS[k][0])
+            for i in range(16):
+                tt(A("ge", 16 * lo + i, 16 * hi, 16), A("Ag", 16 * lo + i, 16 * hi, 16), R(nP, lo, hi, 256), O.is_ge)
+                mm(out, A("selB", 16 - i, 144 - i), A("ge", 16 * lo + i, 16 * hi, 16), i == 0, i == 15)
+
+        if not first:
+            whole(old)
+        tt(R("M1", 192, 256), R(old, 192, 256), R(maskP, 192, 256), O.mult)
+        tt(R("M1", 0, 192), R(old, 0, 192), R(maskP, 0, 192), O.mult)
+        scan(R("SC", 192, 256), R("rst", 192, 256), R("M1", 192, 256))
+        ts(H("xh", 1), H(old, 1), SG, O.mult, K2, O.add)
+        scan(R("SC", 0, 192), R("rst", 0, 192), R("M1", 0, 192))
+        ts(A("BWu", 12, 16), W("SC", 192, 256), SG, O.mult, K1, O.add)
+        ts(H("xh", 0), H(old, 0), SG, O.mult, K2, O.add)
+        ts(A("BWu", 0, 12), W("SC", 0, 192), SG, O.mult, K1, O.add)
+        for lo, hi in ((192, 256), (0, 192)):
+            act(R("cm2", lo, hi), R("SC", lo, hi), F.Identity, bias=K3, scale=SG)
+        for lo, hi in ((192, 256), (0, 192)):
+            act(R(SCc, lo, hi), R("cm2", lo, hi), F.Identity, bias=-MAGIC)
+        banks = IND(A("vt", 0, 1040), A("BWu", 0, 16))
+        if not first:
+            entries_top()
+            gather(*CHUNKS[0])
+            entries_rest()
+            tt(R("cB"), R(old), R(XP), O.subtract)
+            lists_rest()
+        tt(R("eqd"), R("xh"), R(SCc), O.is_equal)
+        mm(R(Z, 0, 256, 256), M("blkZ"), R("eqd"), True, False)
+        for a in range(15):
+            lo = 16 * (a + 1)
+            e = R("eqx", lo, 256, 256 * a)
+            ts(e, R("xh", lo, 256), A(SCc, lo - 1, lo), O.is_equal)
+            mm(R(Z, lo, 256, 256), M("blkZ"), e, False, False)
+            if a == 7 and first:
+                cp(R("V1"), banks)
+            if a == 7 and not first:
+                tt(R("V1"), banks, R("cB"), O.subtract)
+            if a == 11:
+                ts(R("NVr"), R("V1"), -1.0, O.mult, 0.0, O.max)
+        ts(R(nP, 0, 256, 256), R("NVr"), 255.0, O.min)
+        mm(R(Z, 0, 256, 256), M("blk1"), R("NVr"), False, True)
+        if first:
+            ts(A("ut", 0, 1024), A("quS", 0, 1024), float(-U0), O.add, 1.0 / 2048, O.mult)
+            pool_constants()
+            entries_top()
+            entries_rest()
+            gather(*CHUNKS[0])
+            lists_rest()
             late_constants()
-            for h in range(2):
-                cp(H("xz", h), H("b4", h, 256))
-        else:
-            old = "land%d" % (st - 1)
-            act(A("cm", 0, 256), A(old, 0, 256), F.Identity, bias=MAGIC, scale=1.0 / 16384)
-            act(A("cB", 0, 256), A("cm", 0, 256), F.Identity, bias=-MAGIC)
-            for h in range(2):
-                ts(H("ci", h), H(old, h), 4096.0, O.add)
-            for h in range(2):
-                ts(H("xi", h), H("ci", h), 16383, O.bitwise_and)
-        for h in range(2):
-            tt(H("M1", h), H(x, h), maskP(h), O.mult)
-        for h in range(2):
-            scan(SC(h), H("rst", h), H("M1", h))
-        scW = A("b2", 256 + 15, 512, 16)
-        ts(A("BWu", 0, 16), scW, float(-base), O.add)
-        BW = A("BWu", 0, 16)
+        ts(R("UI", 192, 256), R("Uo", 192, 256), float(-U0), O.add, 1.0 / 2048, O.mult)
+        add_thr(M("TC"), "ones", 0, 0, 256, start=True)
 
-        def eqd1(h):
-            tt(H("eqd", h), SC(h), H(x, h), O.is_equal)
-        if st == 0:
-            cp(A("V2", 0, 256), IND(A("vt", 0, 1040), BW))
-            for h in range(2):
-                cp(H("xu", h), H(x, h))
-            for h in range(2):
-                eqd1(h)
-            pairs1()
-            cp(A("Uo", 0, 256), IND(A("quS", 0, 1032), BW))
-            ts(A("ut", 0, 1024), A("quS", 0, 1024), ADD1, O.add)
-            late_scalar()
-        else:
-            act(A("UI", 0, 256), IND(A("ut", 0, 1032), BW), F.Copy)
-            tt(A("V1", 0, 256), IND(A("vt", 0, 1040), BW), A("cB", 0, 256), O.subtract)
-            cp(H("xu", 0), H(x, 0))
-            ts(A("V2", 0, 256), A("V1", 0, 256), -255.0, O.max)
-            ts(A("Uo", 0, 256), A("UI", 0, 256), NEG, O.add)
-            cp(H("xu", 1), H(x, 1))
-            for h in range(2):
-                eqd1(h)
-            pairs1()
-        for i in range(16 - NV):
-            act(A("NVx", i, 2048, 16), A("V2", 0, 128), F.Copy, scale=-1.0)
-        for i in range(16 - NV, 16):
-            ts(A("NVx", i, 2048, 16), A("V2", 0, 128), -1.0, O.mult)
-        act(A("NVr", 0, 256), A("V2", 0, 256), F.Relu, scale=-1.0)
-        if st == 0:
-            act(A("UI", 0, 256), IND(A("ut", 0, 1032), BW), F.Copy)
-        act(A("b3", 128, XL), A("V2", 128, XL), F.Copy, scale=-1.0)
-        for c0, c1 in ((XL, 256), (128, 176), (176, XL)):
-            act(A("Ag", 16 * (c0 - 128), 16 * (c1 - 128)), IND(A("at", 0, 3200), A("Uo", c0, c1)), F.Copy)
-        for h in range(2):
-            for e in range(2):
-                mm(KB[h][e], H("UI", h), A("idF", e, 128, 2), True, False)
-        for h in range(2):
-            mm(A("b4", 8 * h, 8 * h + 8), H("NVr", h), blksel, True, True)
-        for h in range(2):
-            out = A("b4", 16 + 8 * h, 24 + 8 * h)
-            mm(out, H("eqd", h), blksel, True, False)
-            n = 7 if h == 0 else 15
-            for a in range(n):
-                mm(out, H("eqx", h, 256 * a), blksel, False, a == n - 1)
-        D0 = 16 * (XL - 128)
-        mm(A("b7", 0, 512), A("idB", 0, 128), A("Ag", D0, 2048), True, False)
-        for i in range(16):
-            mm(A("b7", i, 512, 16), A("idB", 0, 128), A("V2", XL, 256), False, i == 15)
-        act(A("ge1", D0, 2048), A("b7", 0, 512), F.Sign, bias=0.5)
-        tt(A("ge0", 0, 2048), IND(A("at", 0, 3200), A("Uo", 0, 128)), A("NVx", 0, 2048), O.is_ge)
-        for i in ODD:
-            mm(KI(0, i), A("ge0", i, 2048, 16), A("bs64", 0, 8), False, i >= 14)
-        act(A("so0", 0, 64), KB[0][1], F.Copy)
-        act(A("sm", 0, 16), A("b4", 0, 16), F.Sign, bias=-0.5)
-        act(A("sm", 16, 32), A("b4", 16, 32), F.Sign, bias=-1.5)
-        for h in range(2):
-            act(A("digB%d" % h, 24, 32), A("sm", 16 + 8 * h, 24 + 8 * h), F.Relu)
-        act(A("sm", 160, 176), A("sm", 0, 16), F.Identity, bias=HALF - LOW, scale=-HALF)
-        act(A("sm", 176, 192), A("sm", 16, 32), F.Identity, bias=HALF - LOW, scale=HALF)
-        RL = (H("b5", 0), A("b0", 128, 256))
-        CN = (A("b6", 0, 128), A("b7", 0, 128))
-        OFF = (A("b5", 256, 384), A("b1", 256, 384))
+        def stages(k):
+            lo, hi = GROUPS[k]
+            n = hi - lo
+            S, D, sg, RL = A(SBANK[k], 0, n), A(SBANK[k], 128, 128 + n), A(SBANK[k], 256, 256 + n), A(RBANK[k], lo, hi)
+            lw = A("LWu", lo // 16, hi // 16)
 
-        def best(h):
-            m = "mx%d" % h
-            ki, dI, dB, tp = A("ki%d" % h, 0, 8), "digI%d" % h, "digB%d" % h, A("b4", 128 + 128 * h, 256 + 128 * h, 1, 0, 32)
-            tr = A("TTs%d" % h, 0, 128, 1, 0, 32)
+            def weigh():
+                act(R("w", lo, hi), S, F.Exp, bias=-74.0, scale=16 * BETA)
+                mm(D, M("DM"), R("w", lo, hi), True, True)
+                mm(RL, M("blkS"), R("nsgn", lo, hi), True, False)
 
-            def row_digit():
-                if not last:
-                    ts(A(dI, 0, 8), ki, 12, O.arith_shift_right, 15, O.bitwise_and)
-
-            def to_r():
-                cp(A(dB, 0, 24), A(dI, 0, 24))
-                mm(tp, A(dB, 0, 32), A("idB", 0, 128), True, True)
-                act(tr, tp, F.Copy)
-                mm(RL[h], A("selL", 0, 128, 1, 0, 32), tr, True, True)
-                if not last:
-                    mm(H("b6", h, 256), A("selC", 0, 128, 1, 0, 32), tr, True, True)
-            return [lambda: tt(A(m, 0, 64), KB[h][0], A("so%d" % h, 0, 64), O.max),
-                    lambda: tt(A(m, 64, 96), A(m, 0, 64, 2), A(m, 1, 64, 2), O.max),
-                    lambda: tt(A(m, 96, 112), A(m, 64, 96, 2), A(m, 65, 96, 2), O.max),
-                    lambda: tt(A(m, 112, 120), A(m, 96, 112, 2), A(m, 97, 112, 2), O.max),
-                    lambda: tt(ki, A(m, 112, 120), A("sm", 32 + 8 * h, 40 + 8 * h), O.max),
-                    lambda: ts(A(dI, 8, 16), ki, 6, O.arith_shift_right, 63, O.bitwise_and),
-                    lambda: ts(A(dI, 16, 24), ki, 63, O.bitwise_and),
-                    row_digit, to_r]
-
-        def lines(h):
-            lw = A("LWu", 8 * h, 8 * h + 8)
+            def line():
+                tt(R("pU", lo, hi), R("UI", lo, hi), sg, O.min)
+                mm(RL, M("blkL"), R("pU", lo, hi), False, True)
 
             def same():
-                tt(H("eqe", h), H("SC5", h), RL[h], O.is_equal)
-                mm(CN[h], A("blk8", 0, 128), H("eqe", h), True, False)
+                tt(R("eqe", lo, hi), R("SC5", lo, hi), RL, O.is_equal)
+                add_thr(M("W5"), "eqe", 0, lo, hi)
 
-            def to_w():
-                ts(lw, A("SC5", 128 * h + 15, 128 * h + 128, 16), float(NONE1), O.min, -1.0, O.add)
-                act(H("Agl", h), IND(A("at", 0, 3200), lw), F.Copy)
+            def pairs():
+                chunks = range(lo // 16, min(hi // 16, 15))
+                for a in chunks:
+                    c = 16 * (a + 1)
+                    ts(R("eqx", c, 256, 256 * a), R("Lu", c, 256), -1.0 - RL0, O.add, A("SC5", c - 1, c), O.is_equal)
+                    add_thr(M("W5"), "eqx", 256 * a, c, 256, stop=lo == 0 and a == chunks[-1], halves=(0,) if lo == 0 else (0, 1))
+                for a in chunks if lo == 0 else ():
+                    add_thr(M("W5"), "eqx", 256 * a, 128, 256, stop=a == chunks[-1])
 
-            def draw():
-                tt(H("tt", h), H("Agl", h), H("b3", h), O.min)
-                act(H("t16", h), H("tt", h), F.Identity, bias=1.0 - 4096.0, scale=16384.0)
-
-            def payees():
-                if st > 0:
-                    cp(H("payf", h), IND(A("pt", 0, 3200), lw))
-                else:
-                    cp(H("payg", h), IND(A("pq", 0, 3200), lw))
-                    mm(H("b4", h, 128), A("row0", 0, 128), H("payg", h), True, True)
-                    act(H("payf", h), H("b4", h, 128), F.Copy)
-
-            def pay_r():
-                act(H("cm", h), H("payf", h), F.Identity, bias=-511.5 / 1024, scale=1.0 / 1024)
-                act(H("M1", h), H("cm", h), F.Identity, bias=MAGIC)
-                act(H("r8", h), H("M1", h), F.Identity, bias=-MAGIC - 8.0)
-
-            def one_hot():
-                ts(H("OH", h), CN[h], 8.0, O.min, PM, O.is_equal)
-                mm(OFF[h], A("woff", 0, 128), H("OH", h), True, False)
-
-            def product():
-                tt(H("prod", h), H("b3", h, 256), H("OH", h), O.mult)
-                mm(OFF[h], A("blk1", 0, 128), H("prod", h), False, True)
-            return [lambda: tt(H("M5", h), RL[h], H("maskS", h), O.mult),
-                    lambda: cp(H("Lu", h), RL[h]),
-                    lambda: scan(H("SC5", h), H("rst", h), H("M5", h)),
-                    same, to_w, draw, payees, pay_r,
-                    lambda: mm(CN[h], A("idB", 0, 128), H("r8", h), False, True),
-                    one_hot,
-                    lambda: scan(H("b3", h, 256), H("ones", h), H("OH", h), 0.0 if h == 0 else A("b3", 383, 384)),
-                    product]
-
-        def pairs5(h):
-            for a in range(7 if h == 0 else 15):
-                lo, c = max(128 * h, 16 * (a + 1)), 16 * a + 15
-                e = A("eqx", 256 * a + lo, 256 * a + 128 * h + 128)
-                ts(e, A("Lu", lo, 128 * h + 128), A("SC5", c, c + 1), O.is_equal)
-                mm(A(CN[h][1], lo - 128 * h, 128), A("blk8", 0, 128), e, False, False)
-
-        def ge1(i):
-            tt(A("ge1", i, D0, 16), A("Ag", i, D0, 16), A("b3", 128, XL), O.is_ge)
-            mm(KI(1, i), A("ge1", i, 2048, 16), A("bs64", 0, 8), False, i >= 14)
-            if i == 15:
-                act(A("so1", 0, 64), KB[1][1], F.Copy)
-        best0, lines0, lines1 = best(0), lines(0), lines(1)
-        no_key = lambda: tt(A("sm", 32, 48), A("sm", 160, 176), A("sm", 176, 192), O.max)
-        weave([lambda i=i: ge1(i) for i in ODD], best0[:3] + [no_key] + best0[3:], 11)
-        for f in best(1):
+            def keep():
+                if not last:
+                    act(R("sS", lo, hi), sg, F.Copy)
+            return {"weigh": weigh, "sign": lambda: act(sg, D, F.Sign), "line": line, "keep": keep,
+                    "mask": lambda: tt(R("M5", lo, hi), RL, R("maskS", lo, hi), O.mult),
+                    "short": lambda: ts(R("Lu", lo, hi), RL, RL0 + 1.0, O.add),
+                    "sum": lambda: scan(R("SC5", lo, hi), R("rst", lo, hi), R("M5", lo, hi)),
+                    "same": same, "pairs": pairs,
+                    "list": lambda: ts(lw, W("SC5", lo, hi), float(NONE - RL0), O.min, float(RL0), O.add),
+                    "payee": lambda: act(R("G", lo, hi), IND(A("pt", 0, 3200), lw), F.Copy),
+                    "amount": lambda: act(R("Agl", lo, hi), IND(A("at", 0, 3200), lw), F.Copy),
+                    "draw": lambda: tt(R("t32", lo, hi), R("Agl", lo, hi), R(nP, lo, hi, 256), O.min)}
+        a, b, c = stages(0), stages(1), stages(2)
+        BWf = A("sm", 0, 16)
+        compare(*CHUNKS[0])
+        gather(*CHUNKS[1])
+        compare(*CHUNKS[1])
+        gather(*CHUNKS[2])
+        act(R("nsgn"), R(Z, 0, 256, 256), F.Sign, bias=-16384.0, scale=-1.0)
+        a["weigh"]()
+        gather(32, 64)
+        a["sign"]()
+        gather(0, 32)
+        compare(*CHUNKS[2])
+        for f in (a["line"], b["weigh"], lambda: ts(R("V2"), R("V1"), -255.0, O.max), lambda: cp(BWf, A("BWu", 0, 16)),
+                  a["mask"], a["short"], a["sum"], a["keep"], b["sign"]):
             f()
-        act(A("b3", 0, 256), A("V2", 0, 256), F.Relu, scale=-1.0)
+        compare(*CHUNKS[3])
+        for f in (b["line"], a["same"], a["list"], c["weigh"], a["payee"], b["mask"], b["short"], c["sign"], a["amount"],
+                  b["sum"], a["pairs"], c["line"], b["keep"], b["same"], b["list"], b["payee"], b["amount"], b["pairs"], c["keep"],
+                  c["mask"], c["short"], c["sum"], a["draw"], b["draw"], c["list"], c["same"], c["payee"], c["amount"], c["pairs"]):
+            f()
+        cnt = lambda h: H("b6", h, 256)
+        OFF = (A("b3", 0, 128), A("b4", 0, 128))
+        tt(A("sm", 16, 32), W("SC5"), A("dumpB", 0, 16), O.min)
         if not last:
-            fill(A("pq" if st == 0 else "pt", 3199, 3200), 8192)
-        calls = {"P0": lambda: pairs5(0), "P1": lambda: pairs5(1)}
-        for k in range(12):
-            calls["a%x" % k], calls["b%x" % k] = lines0[k], lines1[k]
-        for k in ORDER0 if st == 0 else ORDER:
-            calls[k]()
+            ts(A("sm", 48, 64), W("SC5"), float(NONE - RL0), O.min, float(RL0), O.add)
         for h in range(2):
-            act(H("sgn", h), CN[h], F.Sign, bias=7.5, scale=-1.0)
-            act(H("b3", h, 256), H("sgn", h), F.Relu)
-        tm = A("b3", 0, 256)
-        tt(H("M6", 0), OFF[0], H("maskS", 0), O.mult)
-        tt(H("M6", 1), OFF[1], H("maskS", 1), O.mult)
+            tt(H("OH", h), H("G", h), H(THR[h], h, 256), O.is_le)
+        scan(cnt(0), H("ones", 0), H("OH", 0), INI)
+        c["draw"]()
+        scan(cnt(1), H("ones", 1), H("OH", 1), A("b6", 383, 384))
+        act(R("nt"), R("t32"), F.Copy, scale=-1.0)
+        for h in range(2):
+            tt(H("prod", h), cnt(h), H("OH", h), O.mult)
+            mm(OFF[h], M("blk2"), H("prod", h), True, True)
+        mm(R("b2"), M("S8"), R("OH"), True, False)
+        mm(R("b2"), M("nI"), R("nt"), False, True)
+        act(R("tm"), R("b2"), F.Relu)
+        tt(A("sm", 32, 48), A("sm", 16, 32), BWf, O.max)
+        for h in range(2):
+            tt(H("M6", h), OFF[h], H("maskS", h), O.mult)
         for h in range(2):
             scan(H("SC6", h), H("rst", h), H("M6", h))
-        o6, l5 = A("SC6", 15, 256, 16), A("SC5", 15, 256, 16)
-        ts(A("sm", 64, 80), scW, float(-base), O.add)
-        ts(A("sm", 48, 64), l5, 4096.0, O.is_gt)
-        cp(A("OWu", 0, 16), o6)
-        tt(IND(A(win, 0, WIN), A("OWu", 0, 16)), A("t16", 0, 256), A("payf", 0, 256), O.add)
+        cp(A("boU", 0, 16), A("sm", 32, 48))
+        ts(A("OWu", 0, 16), W("SC6"), 0.5, O.mult, 2048.0, O.add)
+        if not last:
+            tt(A("sm", 64, 80), W("SC6"), BWf, O.max)
+            tt(A("sm", 80, 96), W("SC6"), A("sm", 48, 64), O.max)
+        tt(IND(A(win, 0, WIN), A("OWu", 0, 16)), R("t32"), R("G"), O.add)
         sync_for(P, "g", [(win, 0, WIN, 1)], [])
         sends = plan(topo, T.cores, me)
-        for c in sends:
+        for call in sends:
             g.remote_dma_fused([RemoteDMATransfer(
                 dst_ids=[DstId(rid=topo.addr(T.cores[r], core)[0], pnc=topo.addr(T.cores[r], core)[1])],
                 dma_engine_mask=sum(1 << e for e in engines), remote_sem=T.sem["arr%d" % st],
-                src=T[win][:, 256 * r + 1:256 * r + 33], dst=T[land][:, 32 * me:32 * me + 32])
-                for r, engines in c], local_sem=T.sem["loc"])
-        out_n = sum(len(e) for c in sends for r, e in c)
-        arrive = sum(len(e) for q in range(8) if q != me for c in plan(topo, T.cores, q) for r, e in c if r == me)
+                src=T[win][:, 256 * r:256 * r + 32], dst=T[land][:, 32 * me:32 * me + 32])
+                for r, engines in call], local_sem=T.sem["loc"])
+        out_n = sum(len(e) for call in sends for r, e in call)
+        arrive = sum(len(e) for q in range(8) if q != me for call in plan(topo, T.cores, q) for r, e in call if r == me)
         for q in range(8):
             if q != me:
                 note(P, "remote", [], [(land, 32 * q, 32 * q + 32, 1)], "arr%d" % st, arrive)
-        cp(A(land, 32 * me, 32 * me + 32), A(win, 256 * me + 1, 256 * me + 33))
-        tt(tm, A("b3", 256, 512), A("tt", 0, 256), O.mult)
-        tt(A("sm", 48, 64), A("sm", 48, 64), A("dumpB", 0, 16), O.mult)
-        tt(A("Vn", 0, 256), tm, A("V2", 0, 256), O.add)
-        tt(A("sm", 80, 96), A("sm", 48, 64), A("sm", 64, 80), O.max)
+        act(A(land, 32 * me, 32 * me + 32), A(win, 256 * me, 256 * me + 32), F.Copy)
         if not last:
-            tt(A("OHu", 0, 256), A("b6", 256, 512), A("UI", 0, 256), O.is_equal)
-        cp(A("boU", 0, 16), A("sm", 80, 96))
+            cp(A("uaU", 0, 32), A("sm", 64, 96))
+        tt(IND(A("vt", 0, 1296), A("boU", 0, 16)), R("V2"), R("tm"), O.add)
         if not last:
-            for h in range(2):
-                act(H("b7", h, 128), H("sgn", h), F.Relu, scale=NONEC)
-            ts(A("sm", 96, 112), o6, 2048.5, O.is_gt)
-            ts(A("sm", 112, 128), l5, float(NONE1), O.min, -1.0, O.add)
-        cp(IND(A("vt", 0, 1296), A("boU", 0, 16)), A("Vn", 0, 256))
-        if last:
-            break
-        okX = A("b7", 128, 384)
-        tt(okX, okX, A("OHu", 0, 256), O.mult)
-        tt(A("sm", 128, 144), A("sm", 96, 112), A("dumpA", 0, 16), O.mult)
-        tt(A("UIn", 0, 256), A("UI", 0, 256), okX, O.max)
-        tt(A("sm", 144, 160), A("sm", 128, 144), A("sm", 112, 128), O.max)
-        tt(A("An", 0, 256), A("Agl", 0, 256), tm, O.subtract)
-        cp(A("aoU", 0, 16), A("sm", 144, 160))
-        cp(IND(A("ut", 0, 1296), A("boU", 0, 16)), A("UIn", 0, 256))
-        cp(IND(A("at", 0, 3456), A("aoU", 0, 16)), A("An", 0, 256))
+            tt(IND(A("ut", 0, WIN), A("uaU", 0, 16)), R("UI"), R("sS"), O.max)
+            tt(IND(A("at", 0, WIN), A("uaU", 16, 32)), R("Agl"), R("nt"), O.add)
 
     sync_for(P, "y", [("vt", 0, 1024, 1)], [])
     y.dma_start(T.yv[:], T.vt[:, 0:1024]).then_inc(T.sem["dyv"], 16)
-    act(A("cm", 0, 256), A("land2", 0, 256), F.Identity, bias=MAGIC, scale=1.0 / 16384)
-    act(A("cB", 0, 256), A("cm", 0, 256), F.Identity, bias=-MAGIC)
+    whole("land3")
+    act(R("ywS"), R("cm"), F.Identity, bias=-MAGIC - WR // 1024 * me - 1)
     for h in range(2):
-        ts(H("ci", h), H("land2", h), 4096.0, O.add)
-    for h in range(2):
-        ts(H("xi", h), H("ci", h), 16383, O.bitwise_and)
-    for h in range(2):
-        ts(H("ywS", h), H("xi", h), float(-(1 + 1024 * me)), O.add)
-    sync_for(P, "s", regions([A("cB", 0, 256)]), [])
-    s.dma_start(T.yc[:], T.cB[:, 0:256]).then_inc(T.sem["dyc"], 16)
-    sync_for(P, "y", regions([A("ywS", 0, 256)]), [])
-    y.dma_start(T.yw[:], T.ywS[0:128:16, 0:256]).then_inc(T.sem["dyw"], 16)
+        tt(H("cB", h), H("land3", h), H(XP, h), O.subtract)
+    sync_for(P, "s", regions([R("ywS")]), [])
+    s.dma_start(T.yw[:], T.ywS[0:128:16, 0:256]).then_inc(T.sem["dyw"], 16)
+    sync_for(P, "y", regions([R("cB")]), [])
+    y.dma_start(T.yc[:], T.cB[:, 0:256]).then_inc(T.sem["dyc"], 16)
     for sem in ("sv", "ss", "sp", "sg"):
         g.wait_ge(T.sem[sem], P["cnt"][sem])
-    for sem in ("dwk", "dvp", "dqu", "dam", "dpq", "dyv", "dyw", "dyc"):
+    for sem in ("dwk", "dvp", "dqu", "dam", "dpa", "dpb", "dyv", "dyw", "dyc"):
         g.wait_ge(T.sem[sem], 16)
-    g.wait_ge(T.sem["dpay"], 256)
     g.wait_ge(T.sem["loc"], 3 * out_n)
     for k in range(3):
         g.wait_ge(T.sem["arr%d" % k], arrive)

@@ -3,28 +3,25 @@ from concourse.mybir import AluOpType as O, ActivationFunctionType as F
 
 WIN = 4096
 SCRATCH = {}
-for _n in "land0 land1 land2 land3 M1 SC cm cm2 UI sS M5 SC5 G t32 M6 SC6 ywS E r32".split():
+for _n in "land0 land1 land2 land3 M1 SC cm cm2 cm3 UI sS M5 SC5 G t32 ywS E r32".split():
     SCRATCH[_n] = ("sbuf", [128, 256], "float32")
-for _n in "maskS rst ones V1 V2 NVr eqd eqe w nsgn OH Agl nt tm cB".split():
+for _n in "maskS rst ones V1 V2 NVr eqd eqe w nsgn OH Agl nt tm cB l15 i144 l4".split():
     SCRATCH[_n] = ("sbuf", [128, 256], "bfloat16")
-for _n in "xh wkh pU prod".split():
+for _n in "xh wkh pU prod M6 SC6".split():
     SCRATCH[_n] = ("sbuf", [128, 256], "float16")
-for _n in "blk1 blkT blkZ blkL blkS blk2 idB nI DM DM0 W5 W5a W5b TC S8 PB PB0 sel8 selT".split():
+for _n in "blk1 blkT blkZ blkL blkS blk2 idB nI DM DM0 DM1 W5 W5a W5b W5c TC S8 PB PB0 PB1 sel8 selT".split():
     SCRATCH[_n] = ("sbuf", [128, 128], "bfloat16")
 for _n in "Lu Uo".split():
     SCRATCH[_n] = ("sbuf", [128, 256], "uint16")
 for _n in "BWu LWu OWu boU".split():
     SCRATCH[_n] = ("sbuf", [128, 16], "uint16")
-for _n in "ge Ag eqx".split():
+for _n in "ge Ag eqx eqy".split():
     SCRATCH[_n] = ("sbuf", [128, 4096], "bfloat16")
 for _n in range(3):
     SCRATCH["win%d" % _n] = ("sbuf", [128, WIN], "float32")
 for _n in range(8):
     SCRATCH["b%d" % _n] = ("psum", [128, 512], "float32")
 SCRATCH["wkb"] = ("sbuf", [128, 256], "int32")
-SCRATCH["l15"] = ("sbuf", [128, 256], "int32")
-SCRATCH["i144"] = ("sbuf", [128, 144], "int32")
-SCRATCH["l4"] = ("sbuf", [128, 128], "int32")
 SCRATCH["l16"] = ("sbuf", [128, 16], "int32")
 SCRATCH["pci"] = ("sbuf", [128, 8], "int32")
 SCRATCH["selB"] = ("sbuf", [128, 144], "bfloat16")
@@ -51,10 +48,16 @@ T0 = 17 * 2 ** 16
 KS = 2304
 RL0 = U0 + 15 * 2048 + 16 * KS
 BETA, THETA = 0.58, 0.40625
-CHUNKS = [(192, 256), (128, 192), (64, 128), (0, 64)]
-GROUPS = [(128, 256), (64, 128), (0, 64)]
-SBANK, RBANK = ["b3", "b4", "b2"], ["b5", "b6", "b5"]
-THR = ["b1", "b7"]
+GATHERS = [(0, 64), (64, 128), (128, 192), (192, 224), (224, 256)]
+CHUNKS = [(0, 64), (64, 128), (128, 192), (192, 256)]
+GROUPS = [(0, 128), (128, 192), (192, 256)]
+PLACES = [(0, 192), (192, 256)]
+SBANK, RBANK, TBANK = ["b3", "b4", "b2"], ["b5", "b6", "b5"], ["b7", "b1"]
+HOP, CYCLE, GATHER, SCATTER = 150.0, 0.83, 1.56, 3.8
+ROWS = [("s", "Ag"), ("v", "ge"), ("v", "eqx"), ("v", "eqy"), ("s", "pt")] + [("p", "b%d" % k) for k in range(8)]
+SAME = {("s", "b1"): ("s", "Ag"), ("v", "eqx"): ("v", "ge"), ("v", "eqd"): ("v", "ge")}
+TURNS = 2
+BYTE, DMA, SEND, FLIGHT = 0.0045, 1200.0, 1000.0, 2000.0
 
 
 def A(name, c0, c1, step=1, p0=0, p1=128):
@@ -98,6 +101,14 @@ def regions(views):
     return out
 
 
+def width(x):
+    return 16 * width(x[2]) if x[0] == "I" else (x[3] - x[2] + x[4] - 1) // x[4]
+
+
+def dtype(x):
+    return SCRATCH[x[1]][2]
+
+
 def sync_for(P, q, reads, writes):
     need = []
     for kind, regs in (("r", reads), ("w", writes)):
@@ -139,19 +150,128 @@ def note(P, q, reads, writes, sem, val):
 SEM_OF = {"v": "sv", "s": "ss", "p": "sp", "g": "sg"}
 
 
-def op(P, q, fn, out, *args, **kw):
-    reads = regions([a for a in args if is_view(a)] + [a for a in kw.values() if is_view(a)])
+def record(P, q, ns, reads, writes, emit, lag=0.0, group=None):
+    P["calls"].append({"q": q, "ns": ns, "lag": lag, "r": reads, "w": writes, "emit": emit, "group": group})
+
+
+def op(P, q, cycles, fn, out, *args, **kw):
+    ins = [a for a in args if is_view(a)] + [a for a in kw.values() if is_view(a)]
+    reads = regions(ins)
+    n = width(out)
     if out[0] == "I":
         writes = regions([out[1]])
         reads += regions([out[2]])
+        ns = 50 + n * SCATTER * CYCLE
     else:
         writes = regions([out])
-    sync_for(P, q, reads, writes)
-    sem = SEM_OF[q]
-    P["cnt"][sem] += 1
-    fn(resolve(P, out), *[resolve(P, a) if is_view(a) else a for a in args],
-       **{k: (resolve(P, a) if is_view(a) else a) for k, a in kw.items()}).then_inc(P["T"].sem[sem], 1)
-    note(P, q, reads, writes, sem, P["cnt"][sem])
+        if any(a[0] == "I" for a in ins):
+            ns = 60 + n * GATHER * CYCLE
+        elif q == "g":
+            ns = 150 + 2 * n * CYCLE
+        else:
+            ns = max(64, n * cycles) * CYCLE
+
+    def emit():
+        sync_for(P, q, reads, writes)
+        sem = SEM_OF[q]
+        P["cnt"][sem] += 1
+        fn(resolve(P, out), *[resolve(P, a) if is_view(a) else a for a in args],
+           **{k: (resolve(P, a) if is_view(a) else a) for k, a in kw.items()}).then_inc(P["T"].sem[sem], 1)
+        note(P, q, reads, writes, sem, P["cnt"][sem])
+    record(P, q, ns, reads, writes, emit, group=(out[1], args[2], args[3]) if q == "p" else None)
+
+
+def issue_all(P):
+    calls = P["calls"]
+    seen, closed = {}, {}
+    for n, c in enumerate(calls):
+        pre = {}
+        for kind in "rw":
+            for r in c[kind]:
+                for m, k2, r2 in seen.get(r[0], []):
+                    if (kind == "w" or k2 == "w") and hits(r, r2):
+                        both = c["group"] and calls[m]["group"] and kind == "w"
+                        if both and not any(c["group"][1:] + calls[m]["group"][1:]):
+                            continue
+                        pre[m] = max(pre.get(m, 0.0), 0.0 if both else HOP)
+        row = (c["q"], c["w"][0][0]) if c["w"] else None
+        row = SAME.get(row, row)
+        if row in ROWS:
+            if row in closed:
+                pre.setdefault(closed[row], 0.0)
+            closed[row] = n
+        if c["group"]:
+            bank, start, stop = c["group"]
+            if start:
+                if bank in closed:
+                    pre.setdefault(closed[bank], 0.0)
+                P["open"][bank] = []
+            for m in P["open"][bank][:None if stop else 1]:
+                pre.setdefault(m, 0.0)
+            P["open"][bank].append(n)
+            if stop:
+                closed[bank] = n
+        for kind in "rw":
+            for r in c[kind]:
+                lst = seen.setdefault(r[0], [])
+                if kind == "w" and r[3] == 1 and not c["group"]:
+                    lst[:] = [h for h in lst if not (r[1] <= h[2][1] and h[2][2] <= r[2])]
+                lst.append((n, kind, r))
+        c["pre"], c["post"] = pre, []
+        c["banks"] = sorted(set(r[0] for r in c["r"] + c["w"] if is_psum(r[0])))
+        for m in pre:
+            calls[m]["post"].append(n)
+    for n in range(len(calls) - 1, -1, -1):
+        c = calls[n]
+        c["way"] = c["ns"] + c["lag"] + max([calls[m]["way"] + calls[m]["pre"][n] for m in c["post"]] + [0.0])
+    order = sorted(range(len(calls)), key=lambda n: (-calls[n]["way"], n))
+    best = None
+    for turn in range(TURNS):
+        at = place(calls, order, False)
+        end = max(at[n] + c["ns"] + c["lag"] for n, c in enumerate(calls))
+        if best is None or end < best[0]:
+            best = (end, sorted(range(len(calls)), key=lambda n: (at[n], n)))
+        back = place(calls, sorted(range(len(calls)), key=lambda n: (-at[n] - calls[n]["ns"], -n)), True)
+        order = sorted(range(len(calls)), key=lambda n: (-back[n] - calls[n]["ns"], n))
+    for n in best[1]:
+        calls[n]["emit"]()
+
+
+def place(calls, order, back):
+    at, busy = {}, {}
+    for n in order:
+        c = calls[n]
+        if back:
+            t = c["lag"] + max([at[m] + calls[m]["ns"] + calls[m]["pre"][n] for m in c["post"]] + [0.0])
+        else:
+            t = max([at[m] + calls[m]["ns"] + calls[m]["lag"] + hop for m, hop in c["pre"].items()] + [0.0])
+        moved = True
+        while moved:
+            moved = False
+            for key in [c["q"]] + c["banks"]:
+                lst = busy.setdefault(key, [])
+                k = after(lst, t - 2000.0)
+                while k < len(lst) and lst[k][0] < t + c["ns"] + HOP:
+                    a, b, q = lst[k]
+                    gap = 0.0 if q == c["q"] else HOP
+                    if a - gap < t + c["ns"] and t < b + gap:
+                        t, moved = b + gap, True
+                    k += 1
+        at[n] = t
+        for key in [c["q"]] + c["banks"]:
+            busy[key].insert(after(busy[key], t), (t, t + c["ns"], c["q"]))
+    return at
+
+
+def after(lst, t):
+    lo, hi = 0, len(lst)
+    while lo < hi:
+        mid = (lo + hi) // 2
+        if lst[mid][0] < t:
+            lo = mid + 1
+        else:
+            hi = mid
+    return lo
 
 
 def rank_program(g, core, T, topo):
@@ -160,36 +280,42 @@ def rank_program(g, core, T, topo):
         return
     v, s, pe, y = g.vector, g.scalar, g.tensor, g.sync
     P = {"T": T, "hist": {}, "known": {q: {} for q in "vspyg"}, "cnt": {"sv": 0, "ss": 0, "sp": 0, "sg": 0},
-         "eng": {"v": v, "s": s, "p": pe, "y": y, "g": g}}
+         "eng": {"v": v, "s": s, "p": pe, "y": y, "g": g}, "calls": [], "open": {}}
 
-    def cp(out, in_): op(P, "v", v.tensor_copy, out, in_)
-    def tt(out, a, b, o): op(P, "v", v.tensor_tensor, out, a, b, o)
+    def short(*views): return 0.5 if all(x[0] == "A" and dtype(x)[-2:] == "16" for x in views) else 1
+    def cp(out, in_): op(P, "v", short(out, in_), v.tensor_copy, out, in_)
+    def tt(out, a, b, o): op(P, "v", 1 if is_psum(a[1]) or is_psum(b[1]) else 2, v.tensor_tensor, out, a, b, o)
     def ts(out, a, s1, o1, s2=None, o2=None):
         if o2 is None:
-            op(P, "v", v.tensor_scalar, out, a, s1, None, o1)
+            op(P, "v", short(out, a), v.tensor_scalar, out, a, s1, None, o1)
         else:
-            op(P, "v", v.tensor_scalar, out, a, s1, s2, o1, o2)
-    def scan(out, d0, d1, ini=0.0): op(P, "v", v.tensor_tensor_scan, out, d0, d1, ini, O.mult, O.add)
-    def fill(out, c): op(P, "v", v.memset, out, c)
-    def act(out, in_, f, **kw): op(P, "s", s.activation, out, in_, f, **kw)
-    def mm(out, l, r, st, sp): op(P, "p", pe.matmul, out, l, r, st, sp)
-    def iota(out, pat, base, cm, **kw): op(P, "g", g.iota, out, pat, base, cm, **kw)
-    def pick(out, in_, pat, cmp, base, cm, fill=0.0): op(P, "g", g.affine_select, out, in_, pat, cmp, fill, base, cm)
+            op(P, "v", short(out, a), v.tensor_scalar, out, a, s1, s2, o1, o2)
+    def scan(out, d0, d1, ini=0.0): op(P, "v", short(out, d0, d1), v.tensor_tensor_scan, out, d0, d1, ini, O.mult, O.add)
+    def fill(out, c): op(P, "v", 1, v.memset, out, c)
+    def act(out, in_, f, **kw): op(P, "s", 1, s.activation, out, in_, f, **kw)
+    def mm(out, l, r, st, sp): op(P, "p", 1, pe.matmul, out, l, r, st, sp)
+    def iota(out, pat, base, cm, **kw): op(P, "g", 2, g.iota, out, pat, base, cm, **kw)
+    def pick(out, in_, pat, cmp, base, cm, fill=0.0): op(P, "g", 2, g.affine_select, out, in_, pat, cmp, fill, base, cm)
     def H(name, h, c0=0): return A(name, c0 + 128 * h, c0 + 128 * h + 128)
     def R(name, lo=0, hi=256, c0=0): return A(name, c0 + lo, c0 + hi)
     def W(name, lo=0, hi=256): return A(name, lo + 15, hi, 16)
+    def L(name, lo=0, hi=256): return A(name, lo // 16, hi // 16)
     def M(name): return A(name, 0, 128)
     def C(k): return A("col", k, k + 1)
 
-    def load(q, out, src, sem):
+    landed = [DMA]
+
+    def load(q, out, src, sem, size):
         P["eng"][q].dma_start(resolve(P, out), src).then_inc(T.sem[sem], 16)
         note(P, "d" + sem, [], regions([out]), sem, 16)
-    load("y", A("wkb", 0, 256, 1, 0, 8), T.wk[:], "dwk")
-    load("s", A("vt", 0, 1024), T.vp[:], "dvp")
-    load("y", A("payS", 0, 400, 1, 0, 64), T.pay[:], "dpa")
-    load("y", A("payS", 0, 400, 1, 64, 128), T.pay[:], "dpb")
-    load("y", A("quS", 0, 1024), T.qu[:], "dqu")
-    load("y", A("at", 0, 3200), T.am[:], "dam")
+        landed[0] += size * BYTE
+        record(P, sem, 1.0, [], regions([out]), lambda: None, lag=landed[0])
+    load("y", A("wkb", 0, 256, 1, 0, 8), T.wk[:], "dwk", 8192)
+    load("y", A("payS", 0, 400, 1, 0, 64), T.pay[:], "dpa", 102400)
+    load("y", A("payS", 0, 400, 1, 64, 128), T.pay[:], "dpb", 102400)
+    load("s", A("vt", 0, 1024), T.vp[:], "dvp", 262144)
+    load("y", A("quS", 0, 1024), T.qu[:], "dqu", 524288)
+    load("y", A("at", 0, 3200), T.am[:], "dam", 819200)
 
     imp = {"allow_small_or_imprecise_dtypes": True}
 
@@ -197,13 +323,19 @@ def rank_program(g, core, T, topo):
         pick(tmp, src, [[-16, 8], [0, 16]], O.is_ge, 0, 1)
         pick(out, tmp, [[16, 8], [0, 16]], O.is_ge, 15, -1)
     iota(A("pci", 0, 1), [[1, 1]], 0, 1)
-    iota(R("l15"), [[0, 16], [1, 16]], 0, 0)
-    iota(R("ones"), [[0, 256]], 1, 0, **imp)
-    pick(A("selT", 0, 128, 1, 0, 8), A("ones", 0, 128, 1, 0, 8), [[1, 128]], O.is_ge, 0, -16)
-    pick(A("sel8", 0, 128, 1, 0, 8), A("selT", 0, 128, 1, 0, 8), [[-1, 128]], O.is_ge, 15, 16)
-    iota(M("l4"), [[1, 8], [0, 16]], 0, 0)
-    iota(A("i144", 0, 144), [[1, 144]], 0, 0)
+    iota(R("l15"), [[0, 16], [1, 16]], 0, 0, **imp)
+    fill(R("ones"), 1.0)
+    pick(A("sel8", 0, 128, 1, 0, 8), A("ones", 0, 128, 1, 0, 8), [[1, 8], [0, 16]], O.is_equal, 0, -1)
+    pick(R("rst"), R("ones"), [[0, 16], [1, 16]], O.not_equal, 0, 0)
+    iota(M("l4"), [[1, 8], [0, 16]], 0, 0, **imp)
+    iota(A("i144", 0, 144), [[1, 144]], 0, 0, **imp)
     block(M("blk1"), M("blkT"), M("ones"))
+    iota(R("r32"), [[1, 8], [0, 32]], 0, 0, **imp)
+    pick(M("idB"), M("ones"), [[-1, 128]], O.is_equal, 0, 1)
+    iota(M("W5a"), [[0, 128]], -BIG, 0, **imp)
+    iota(A("l16", 0, 16), [[16, 16]], 0, 0)
+    pick(M("W5b"), M("W5a"), [[0, 8], [1, 16]], O.not_equal, -8, 0, float(BIG))
+    block(M("W5"), M("W5c"), M("W5b"))
     p0 = A("pci", 0, 1)
     ts(A("pci", 1, 2), p0, 15, O.bitwise_and)
     ts(A("pci", 2, 3), p0, 7, O.bitwise_and)
@@ -212,146 +344,123 @@ def rank_program(g, core, T, topo):
     cp(A("col", 0, 5), A("pci", 0, 5))
     PM, J8, SCE, BPT, Q, SIG, SG, K0, K1, K2, K3 = C(1), C(5), C(6), C(7), C(8), C(9), C(10), C(11), C(12), C(13), C(14)
     EJ, INI, NOW, EQ8 = C(16), C(17), C(18), C(19)
-    maskP, nP, SCc, XP, Z = "b0", "b0", "b1", "b2", "b2"
-
-    def add_thr(l, rhs, c0, lo, hi, start=False, stop=False, halves=(0, 1)):
-        for h in halves:
-            a, b = max(lo, 128 * h), min(hi, 128 * h + 128)
-            if a < b:
-                mm(A(THR[h], 256 + a, 256 + b), l, A(rhs, c0 + a, c0 + b), start, stop)
+    maskP, nP, SCc, XP, Z = "b0", "b0", "b1", "b2", "b6"
     ts(J8, PM, 8.0, O.is_lt)
     ts(R(maskP), R("l15"), PM, O.is_equal)
+    ts(R("maskS"), R("l15"), PM, O.is_equal)
     ts(SCE, J8, float(WR), O.mult)
     ts(C(20), J8, float(-WR), O.mult, float(WR + 1024), O.add)
-    ts(R("rst"), R("l15"), 0.0, O.not_equal)
     ts(C(21), SCE, PM, O.mult)
     ts(EQ8, PM, 8.0, O.is_equal)
     tt(BPT, C(20), C(21), O.subtract)
     ts(C(22), SCE, float(me), O.mult, -1024.0, O.add)
-    ts(C(23), C(0), PM, O.subtract, 16.0, O.add)
     tt(Q, C(22), BPT, O.add)
-    ts(C(24), C(4), float(WR - 1024), O.mult, 1024.0, O.add)
-    ts(C(25), PM, BETA, O.mult, -7.5 * BETA, O.add)
     ts(C(26), Q, 0.0, O.is_ge, 2.0, O.mult)
-    ts(K0, Q, 1024.0, O.add)
-    ts(K1, Q, -1.0 / 1024, O.mult, -0.75, O.add)
     ts(SIG, C(26), -1.0, O.add)
+    ts(SG, SIG, 1.0 / 1024, O.mult)
+    ts(K1, Q, -1.0 / 1024, O.mult, -0.75, O.add)
     ts(K2, Q, -1.0 / 1024, O.mult, 1023.0, O.add)
     ts(K3, Q, -1.0 / 1024, O.mult, MAGIC + 1023.0, O.add)
-    ts(SG, SIG, 1.0 / 1024, O.mult)
-    act(EJ, C(25), F.Exp)
     fill(A("vt", 1024, 1040), 0.0)
     fill(A("ut", 1024, 1032), 1.0)
+    ts(C(23), C(0), PM, O.subtract, 16.0, O.add)
+    ts(A("selB", 0, 144), A("i144", 0, 144), C(23), O.is_equal)
+    for name, factor in (("blkL", 2048.0), ("blkS", float(KS)), ("blk2", 2.0), ("blkZ", -16384.0), ("DM0", -THETA)):
+        act(M(name), M("blk1"), F.Copy, scale=factor)
+    ts(C(27), EQ8, -512.0, O.mult)
+    act(M("S8"), M("blk1"), F.Copy, scale=C(27))
+    ts(C(28), EQ8, -2.0 * BIG, O.mult, float(T0 + BIG), O.add)
+    act(M("TC"), M("idB"), F.Copy, scale=C(28))
+    ts(C(29), EQ8, 1792.0, O.mult, -2049.0, O.add)
+    ts(INI, PM, 256.0, O.mult, C(29), O.add)
+    act(M("nI"), M("idB"), F.Copy, scale=-1.0)
+    ts(A("dumpB", 0, 16), A("l16", 0, 16), PM, O.add, 1025.0, O.add)
+    ts(C(25), PM, BETA, O.mult, -7.5 * BETA, O.add)
+    act(EJ, C(25), F.Exp)
+    P["calls"][-1]["ns"] += 1300.0
+    pick(M("DM1"), M("DM0"), [[-1, 128]], O.not_equal, 0, 1, 1.0 - THETA)
+    act(M("DM"), M("DM1"), F.Copy, scale=EJ)
+    ts(C(30), BPT, 1024.0 * 1024, O.add)
+    act(R("E"), R("r32"), F.Abs, scale=SCE, bias=C(30))
+    for k in range(3):
+        for r in range(8):
+            pick(A("win%d" % k, 256 * r, 256 * r + 32), A("E", 32 * r, 32 * r + 32), [[0, 32]], O.is_ge, 0, 0)
 
-    def payee_table():
-        ts(M("PB0"), M("l4"), C(3), O.is_equal, C(24), O.mult)
-        ts(A("col", 32, 40), A("i144", 0, 8), C(2), O.is_equal)
-        ts(C(31), C(4), -8.0, O.mult, 16.0, O.add)
-        ts(A("payI", 0, 400, 1, 0, 64), A("payS", 0, 400, 1, 0, 64), 1023, O.bitwise_and)
-        ts(M("DM0"), M("l15"), C(31), O.is_lt)
-        ts(A("payI", 0, 400, 1, 64, 128), A("payS", 0, 400, 1, 64, 128), 10, O.arith_shift_right)
-        tt(M("PB"), M("PB0"), M("DM0"), O.mult)
-        cp(A("payH", 0, 400), A("payI", 0, 400))
-        for c in range(8):
-            ts(A("PL", 128 * c, 128 * c + 128), M("PB"), C(32 + c), O.mult)
-            bank = A("b%d" % (3 + c % 4), 0, 400)
-            mm(bank, A("PL", 128 * c, 128 * c + 128), A("payH", 0, 400), True, True)
-            act(A("pt", 400 * c, 400 * c + 400), bank, F.Abs, bias=BPT)
-        ts(NOW, EQ8, float(-WR), O.mult, float(WR), O.add)
-        act(A("pt", NONE, NONE + 1), NOW, F.Copy)
-
-    def pool_constants():
-        iota(R("r32"), [[1, 8], [0, 32]], 0, 0, **imp)
-        pick(M("idB"), M("ones"), [[-1, 128]], O.is_equal, 0, 1)
-        iota(M("W5a"), [[0, 128]], -BIG, 0, **imp)
-        iota(A("l16", 0, 16), [[16, 16]], 0, 0)
-        pick(M("W5b"), M("W5a"), [[0, 8], [1, 16]], O.not_equal, -8, 0, float(BIG))
-        block(M("W5"), M("W5a"), M("W5b"))
-        ts(C(30), BPT, 1024.0 * 1024, O.add)
-        act(R("E"), R("r32"), F.Abs, scale=SCE, bias=C(30))
-        for k in range(3):
-            for r in range(8):
-                pick(A("win%d" % k, 256 * r, 256 * r + 32), A("E", 32 * r, 32 * r + 32), [[0, 32]], O.is_ge, 0, 0)
-
-    def late_constants():
-        ts(A("selB", 0, 144), A("i144", 0, 144), C(23), O.is_equal)
-        ts(R("maskS"), R("l15"), PM, O.is_equal)
-        ts(M("blkL"), M("blk1"), 2048.0, O.mult)
-        ts(M("blkS"), M("blk1"), float(KS), O.mult)
-        ts(M("blk2"), M("blk1"), 2.0, O.mult)
-        ts(C(27), EQ8, -512.0, O.mult)
-        ts(C(28), EQ8, -2.0 * BIG, O.mult, float(T0 + BIG), O.add)
-        ts(C(29), EQ8, 1792.0, O.mult, -2049.0, O.add)
-        ts(M("DM0"), M("blk1"), -THETA, O.mult)
-        ts(M("S8"), M("blk1"), C(27), O.mult)
-        ts(M("TC"), M("idB"), C(28), O.mult)
-        ts(INI, PM, 256.0, O.mult, C(29), O.add)
-        tt(M("DM0"), M("DM0"), M("idB"), O.add)
-        ts(M("nI"), M("idB"), -1.0, O.mult)
-        ts(A("dumpB", 0, 16), A("l16", 0, 16), PM, O.add, 1025.0, O.add)
-        ts(M("DM"), M("DM0"), EJ, O.mult)
+    ts(C(24), C(4), float(WR - 1024), O.mult, 1024.0, O.add)
+    ts(M("PB0"), M("l4"), C(3), O.is_equal, C(24), O.mult)
+    ts(A("col", 32, 40), A("i144", 0, 8), C(2), O.is_equal)
+    ts(C(31), C(4), -8.0, O.mult, 16.0, O.add)
+    ts(M("PB1"), M("l15"), C(31), O.is_lt)
+    tt(M("PB"), M("PB0"), M("PB1"), O.mult)
+    ts(A("payI", 0, 400, 1, 0, 64), A("payS", 0, 400, 1, 0, 64), 1023, O.bitwise_and)
+    ts(A("payH", 0, 400, 1, 64, 128), A("payS", 0, 400, 1, 64, 128), 1.0 / 1024, O.mult, 1025 - 511.5 / 1024, O.add)
+    cp(A("payH", 0, 400, 1, 0, 64), A("payI", 0, 400, 1, 0, 64))
+    ts(C(15), SCE, -1025.0, O.mult, BPT, O.add)
+    for c in range(8):
+        ts(A("PL", 128 * c, 128 * c + 128), M("PB"), C(32 + c), O.mult)
+        bank = A("b%d" % (3 + c % 4), 0, 400)
+        mm(bank, A("PL", 128 * c, 128 * c + 128), A("payH", 0, 400), True, True)
+        act(A("pt", 400 * c, 400 * c + 400), bank, F.Abs, bias=C(15))
+    ts(NOW, EQ8, float(-WR), O.mult, float(WR), O.add)
+    act(A("pt", NONE, NONE + 1), NOW, F.Copy)
+    for c in range(4):
+        ts(A("ut", 256 * c, 256 * c + 256), A("quS", 256 * c, 256 * c + 256), float(-U0), O.add, 1.0 / 2048, O.mult)
 
     def whole(src):
         for h in range(2):
             act(H("cm", h), H(src, h), F.Identity, bias=MAGIC, scale=1.0 / 1024)
-        for h in range(2):
             act(H(XP, h), H("cm", h), F.Identity, bias=-1024.0 * MAGIC, scale=1024.0)
 
     wk8 = A("wkh", 0, 256, 1, 0, 8)
     cp(wk8, A("wkb", 0, 256, 1, 0, 8))
     mm(R("b7"), A("sel8", 0, 128, 1, 0, 8), wk8, True, True)
-    payee_table()
-    ts(R("cm"), R("b7"), 1024.0, O.mult, K0, O.add)
-    ts(M("blkZ"), M("blk1"), -16384.0, O.mult)
-    ts(R("land0"), R("cm"), SIG, O.mult)
+    act(R("land0"), R("b7"), F.Identity, bias=1024.0, scale=1024.0)
+    sends = plan(topo, T.cores, me)
+    out_n = sum(len(e) for call in sends for r, e in call)
+    arrive = sum(len(e) for q in range(8) if q != me for call in plan(topo, T.cores, q) for r, e in call if r == me)
+
+    def exchange(st, win, land):
+        src, dst = [(win, 0, WIN, 1)], [(land, 32 * q, 32 * q + 32, 1) for q in range(8) if q != me]
+
+        def emit():
+            sync_for(P, "g", src, [])
+            for call in sends:
+                g.remote_dma_fused([RemoteDMATransfer(
+                    dst_ids=[DstId(rid=topo.addr(T.cores[r], core)[0], pnc=topo.addr(T.cores[r], core)[1])],
+                    dma_engine_mask=sum(1 << e for e in engines), remote_sem=T.sem["arr%d" % st],
+                    src=T[win][:, 256 * r:256 * r + 32], dst=T[land][:, 32 * me:32 * me + 32])
+                    for r, engines in call], local_sem=T.sem["loc"])
+            note(P, "remote", [], dst, "arr%d" % st, arrive)
+        record(P, "g", SEND * len(sends), src, dst, emit, lag=FLIGHT)
 
     for st in range(3):
         first, last = st == 0, st == 2
         old, win, land = "land%d" % st, "win%d" % st, "land%d" % (st + 1)
-
-        def queues(lo, hi):
-            return IND(A("ut", 0, 1032), A("BWu", lo // 16, hi // 16))
-
-        def entries_top():
-            ts(R("Uo", 192, 256), queues(192, 256), 2048.0, O.mult, float(U0), O.add)
-
-        def entries_rest():
-            cp(R("UI", 0, 192), queues(0, 192))
-
-        def lists_rest():
-            ts(R("Uo", 0, 192), R("UI", 0, 192), 2048.0, O.mult, float(U0), O.add)
-
-        def gather(lo, hi):
-            act(A("Ag", 16 * lo, 16 * hi), IND(A("at", 0, 3200), R("Uo", lo, hi)), F.Copy)
-
-        def compare(lo, hi):
-            k = [n for n, (a, b) in enumerate(GROUPS) if a <= lo < b][0]
-            out = A(SBANK[k], lo - GROUPS[k][0], hi - GROUPS[k][0])
-            for i in range(16):
-                tt(A("ge", 16 * lo + i, 16 * hi, 16), A("Ag", 16 * lo + i, 16 * hi, 16), R(nP, lo, hi, 256), O.is_ge)
-                mm(out, A("selB", 16 - i, 144 - i), A("ge", 16 * lo + i, 16 * hi, 16), i == 0, i == 15)
-
-        if not first:
-            whole(old)
-        tt(R("M1", 192, 256), R(old, 192, 256), R(maskP, 192, 256), O.mult)
-        tt(R("M1", 0, 192), R(old, 0, 192), R(maskP, 0, 192), O.mult)
-        scan(R("SC", 192, 256), R("rst", 192, 256), R("M1", 192, 256))
-        ts(H("xh", 1), H(old, 1), SG, O.mult, K2, O.add)
-        scan(R("SC", 0, 192), R("rst", 0, 192), R("M1", 0, 192))
-        ts(A("BWu", 12, 16), W("SC", 192, 256), SG, O.mult, K1, O.add)
-        ts(H("xh", 0), H(old, 0), SG, O.mult, K2, O.add)
-        ts(A("BWu", 0, 12), W("SC", 0, 192), SG, O.mult, K1, O.add)
-        for lo, hi in ((192, 256), (0, 192)):
-            act(R("cm2", lo, hi), R("SC", lo, hi), F.Identity, bias=K3, scale=SG)
-        for lo, hi in ((192, 256), (0, 192)):
+        head = ((0, 64), (64, 256))
+        sg, k1, k2, k3 = (1.0 / 1024, -0.75, 1023.0, MAGIC + 1023.0) if first else (SG, K1, K2, K3)
+        for lo, hi in head:
+            tt(R("M1", lo, hi), R(old, lo, hi), R(maskP, lo, hi), O.mult)
+            scan(R("SC", lo, hi), R("rst", lo, hi), R("M1", lo, hi))
+            ts(L("BWu", lo, hi), W("SC", lo, hi), sg, O.mult, k1, O.add)
+            act(R("cm2", lo, hi), R("SC", lo, hi), F.Identity, bias=k3, scale=sg)
             act(R(SCc, lo, hi), R("cm2", lo, hi), F.Identity, bias=-MAGIC)
-        banks = IND(A("vt", 0, 1040), A("BWu", 0, 16))
-        if not first:
-            entries_top()
-            gather(*CHUNKS[0])
-            entries_rest()
+        ts(R("Uo", 0, 64), IND(A("ut", 0, 1032), L("BWu", 0, 64)), 2048.0, O.mult, float(U0), O.add)
+        ts(R("UI", 0, 64), R("Uo", 0, 64), float(-U0), O.add, 1.0 / 2048, O.mult)
+        cp(R("UI", 64, 256), IND(A("ut", 0, 1032), L("BWu", 64, 256)))
+        ts(R("Uo", 64, 256), R("UI", 64, 256), 2048.0, O.mult, float(U0), O.add)
+        banks = IND(A("vt", 0, 1040), L("BWu"))
+        if first:
+            cp(R("V1"), banks)
+        else:
+            whole(old)
             tt(R("cB"), R(old), R(XP), O.subtract)
-            lists_rest()
+            tt(R("V1"), banks, R("cB"), O.subtract)
+        ts(R("NVr"), R("V1"), -1.0, O.mult, 0.0, O.max)
+        ts(R(nP, 0, 256, 256), R("NVr"), 255.0, O.min)
+        act(R("cm3"), R("V1"), F.Relu, bias=255.0)
+        act(R("V2"), R("cm3"), F.Identity, bias=-255.0)
+        for h in range(2):
+            ts(H("xh", h), H(old, h), sg, O.mult, k2, O.add)
         tt(R("eqd"), R("xh"), R(SCc), O.is_equal)
         mm(R(Z, 0, 256, 256), M("blkZ"), R("eqd"), True, False)
         for a in range(15):
@@ -359,144 +468,96 @@ def rank_program(g, core, T, topo):
             e = R("eqx", lo, 256, 256 * a)
             ts(e, R("xh", lo, 256), A(SCc, lo - 1, lo), O.is_equal)
             mm(R(Z, lo, 256, 256), M("blkZ"), e, False, False)
-            if a == 7 and first:
-                cp(R("V1"), banks)
-            if a == 7 and not first:
-                tt(R("V1"), banks, R("cB"), O.subtract)
-            if a == 11:
-                ts(R("NVr"), R("V1"), -1.0, O.mult, 0.0, O.max)
-        ts(R(nP, 0, 256, 256), R("NVr"), 255.0, O.min)
         mm(R(Z, 0, 256, 256), M("blk1"), R("NVr"), False, True)
-        if first:
-            ts(A("ut", 0, 1024), A("quS", 0, 1024), float(-U0), O.add, 1.0 / 2048, O.mult)
-            pool_constants()
-            entries_top()
-            entries_rest()
-            gather(*CHUNKS[0])
-            lists_rest()
-            late_constants()
-        ts(R("UI", 192, 256), R("Uo", 192, 256), float(-U0), O.add, 1.0 / 2048, O.mult)
-        add_thr(M("TC"), "ones", 0, 0, 256, start=True)
-
-        def stages(k):
-            lo, hi = GROUPS[k]
-            n = hi - lo
-            S, D, sg, RL = A(SBANK[k], 0, n), A(SBANK[k], 128, 128 + n), A(SBANK[k], 256, 256 + n), A(RBANK[k], lo, hi)
-            lw = A("LWu", lo // 16, hi // 16)
-
-            def weigh():
-                act(R("w", lo, hi), S, F.Exp, bias=-74.0, scale=16 * BETA)
-                mm(D, M("DM"), R("w", lo, hi), True, True)
-                mm(RL, M("blkS"), R("nsgn", lo, hi), True, False)
-
-            def line():
-                tt(R("pU", lo, hi), R("UI", lo, hi), sg, O.min)
-                mm(RL, M("blkL"), R("pU", lo, hi), False, True)
-
-            def same():
-                tt(R("eqe", lo, hi), R("SC5", lo, hi), RL, O.is_equal)
-                add_thr(M("W5"), "eqe", 0, lo, hi)
-
-            def pairs():
-                chunks = range(lo // 16, min(hi // 16, 15))
-                for a in chunks:
-                    c = 16 * (a + 1)
-                    ts(R("eqx", c, 256, 256 * a), R("Lu", c, 256), -1.0 - RL0, O.add, A("SC5", c - 1, c), O.is_equal)
-                    add_thr(M("W5"), "eqx", 256 * a, c, 256, stop=lo == 0 and a == chunks[-1], halves=(0,) if lo == 0 else (0, 1))
-                for a in chunks if lo == 0 else ():
-                    add_thr(M("W5"), "eqx", 256 * a, 128, 256, stop=a == chunks[-1])
-
-            def keep():
-                if not last:
-                    act(R("sS", lo, hi), sg, F.Copy)
-            return {"weigh": weigh, "sign": lambda: act(sg, D, F.Sign), "line": line, "keep": keep,
-                    "mask": lambda: tt(R("M5", lo, hi), RL, R("maskS", lo, hi), O.mult),
-                    "short": lambda: ts(R("Lu", lo, hi), RL, RL0 + 1.0, O.add),
-                    "sum": lambda: scan(R("SC5", lo, hi), R("rst", lo, hi), R("M5", lo, hi)),
-                    "same": same, "pairs": pairs,
-                    "list": lambda: ts(lw, W("SC5", lo, hi), float(NONE - RL0), O.min, float(RL0), O.add),
-                    "payee": lambda: act(R("G", lo, hi), IND(A("pt", 0, 3200), lw), F.Copy),
-                    "amount": lambda: act(R("Agl", lo, hi), IND(A("at", 0, 3200), lw), F.Copy),
-                    "draw": lambda: tt(R("t32", lo, hi), R("Agl", lo, hi), R(nP, lo, hi, 256), O.min)}
-        a, b, c = stages(0), stages(1), stages(2)
-        BWf = A("sm", 0, 16)
-        compare(*CHUNKS[0])
-        gather(*CHUNKS[1])
-        compare(*CHUNKS[1])
-        gather(*CHUNKS[2])
         act(R("nsgn"), R(Z, 0, 256, 256), F.Sign, bias=-16384.0, scale=-1.0)
-        a["weigh"]()
-        gather(32, 64)
-        a["sign"]()
-        gather(0, 32)
-        compare(*CHUNKS[2])
-        for f in (a["line"], b["weigh"], lambda: ts(R("V2"), R("V1"), -255.0, O.max), lambda: cp(BWf, A("BWu", 0, 16)),
-                  a["mask"], a["short"], a["sum"], a["keep"], b["sign"]):
-            f()
-        compare(*CHUNKS[3])
-        for f in (b["line"], a["same"], a["list"], c["weigh"], a["payee"], b["mask"], b["short"], c["sign"], a["amount"],
-                  b["sum"], a["pairs"], c["line"], b["keep"], b["same"], b["list"], b["payee"], b["amount"], b["pairs"], c["keep"],
-                  c["mask"], c["short"], c["sum"], a["draw"], b["draw"], c["list"], c["same"], c["payee"], c["amount"], c["pairs"]):
-            f()
-        cnt = lambda h: H("b6", h, 256)
-        OFF = (A("b3", 0, 128), A("b4", 0, 128))
-        tt(A("sm", 16, 32), W("SC5"), A("dumpB", 0, 16), O.min)
-        if not last:
-            ts(A("sm", 48, 64), W("SC5"), float(NONE - RL0), O.min, float(RL0), O.add)
-        for h in range(2):
-            tt(H("OH", h), H("G", h), H(THR[h], h, 256), O.is_le)
-        scan(cnt(0), H("ones", 0), H("OH", 0), INI)
-        c["draw"]()
-        scan(cnt(1), H("ones", 1), H("OH", 1), A("b6", 383, 384))
+        BWf = A("sm", 0, 16)
+        cp(BWf, L("BWu"))
+        for lo, hi in GATHERS:
+            if first and lo == 0:
+                cp(A("Ag", 16 * lo, 16 * hi), IND(A("at", 0, 3200), R("Uo", lo, hi)))
+            else:
+                act(A("Ag", 16 * lo, 16 * hi), IND(A("at", 0, 3200), R("Uo", lo, hi)), F.Copy)
+
+        def thr(lo, hi):
+            k = [n for n, (a, b) in enumerate(PLACES) if a <= lo < b][0]
+            return A(TBANK[k], lo - PLACES[k][0], hi - PLACES[k][0])
+        for k, (lo, hi) in enumerate(GROUPS):
+            n = hi - lo
+            S, D, sg, RL = SBANK[k], A(SBANK[k], 128, 128 + n), A(SBANK[k], 256, 256 + n), A(RBANK[k], lo, hi)
+            for c0, c1 in CHUNKS:
+                for i in range(16) if lo <= c0 < hi else ():
+                    bits = A("ge", 16 * c0 + i, 16 * c1, 16)
+                    tt(bits, A("Ag", 16 * c0 + i, 16 * c1, 16), R(nP, c0, c1, 256), O.is_ge)
+                    mm(A(S, c0 - lo, c1 - lo), A("selB", 16 - i, 144 - i), bits, i == 0, i == 15)
+            act(R("w", lo, hi), A(S, 0, n), F.Exp, bias=-74.0, scale=16 * BETA)
+            mm(D, M("DM"), R("w", lo, hi), True, True)
+            act(sg, D, F.Sign)
+            mm(RL, M("blkS"), R("nsgn", lo, hi), True, False)
+            tt(R("pU", lo, hi), R("UI", lo, hi), sg, O.min)
+            mm(RL, M("blkL"), R("pU", lo, hi), False, True)
+            if not last:
+                act(R("sS", lo, hi), sg, F.Copy)
+            tt(R("M5", lo, hi), RL, R("maskS", lo, hi), O.mult)
+            ts(R("Lu", lo, hi), RL, RL0 + 1.0, O.add)
+            scan(R("SC5", lo, hi), R("rst", lo, hi), R("M5", lo, hi))
+            lw = L("LWu", lo, hi)
+            ts(lw, W("SC5", lo, hi), float(NONE - RL0), O.min, float(RL0), O.add)
+            act(R("G", lo, hi), IND(A("pt", 0, 3200), lw), F.Copy)
+            act(R("Agl", lo, hi), IND(A("at", 0, 3200), lw), F.Copy)
+            tt(R("t32", lo, hi), R("Agl", lo, hi), R(nP, lo, hi, 256), O.min)
+            for p0, p1 in PLACES:
+                if p0 == lo:
+                    mm(thr(p0, p1), M("TC"), R("ones", p0, p1), True, False)
+            for a in range(hi // 16 - 1):
+                c = max(lo, 16 * (a + 1))
+                e = R("eqy", c, hi, 256 * a)
+                ts(e, R("Lu", c, hi), -1.0 - RL0, O.add, A("SC5", 16 * a + 15, 16 * a + 16), O.is_equal)
+                mm(thr(c, hi), M("W5"), e, False, False)
+            tt(R("eqe", lo, hi), R("SC5", lo, hi), RL, O.is_equal)
+            mm(thr(lo, hi), M("W5"), R("eqe", lo, hi), False, any(hi == p1 for p0, p1 in PLACES))
+            for m, (p0, p1) in enumerate(PLACES):
+                if p1 == hi:
+                    cnt, off = A(TBANK[m], 192, 192 + p1 - p0), A(TBANK[m], 0, p1 - p0)
+                    tt(R("OH", p0, p1), R("G", p0, p1), thr(p0, p1), O.is_le)
+                    scan(cnt, R("ones", p0, p1), R("OH", p0, p1), INI if m == 0 else so_far)
+                    so_far = A(cnt[1], cnt[3] - 1, cnt[3])
+                    tt(R("prod", p0, p1), cnt, R("OH", p0, p1), O.mult)
+                    mm(off, M("blk2"), R("prod", p0, p1), True, True)
+                    tt(R("M6", p0, p1), off, R("maskS", p0, p1), O.mult)
+                    scan(R("SC6", p0, p1), R("rst", p0, p1), R("M6", p0, p1))
+                    ts(L("OWu", p0, p1), W("SC6", p0, p1), 0.5, O.mult, 2048.0, O.add)
+                    tt(IND(A(win, 0, WIN), L("OWu", p0, p1)), R("t32", p0, p1), R("G", p0, p1), O.add)
+        exchange(st, win, land)
+        act(A(land, 32 * me, 32 * me + 32), A(win, 256 * me, 256 * me + 32), F.Copy)
         act(R("nt"), R("t32"), F.Copy, scale=-1.0)
-        for h in range(2):
-            tt(H("prod", h), cnt(h), H("OH", h), O.mult)
-            mm(OFF[h], M("blk2"), H("prod", h), True, True)
         mm(R("b2"), M("S8"), R("OH"), True, False)
         mm(R("b2"), M("nI"), R("nt"), False, True)
         act(R("tm"), R("b2"), F.Relu)
+        tt(A("sm", 16, 32), W("SC5"), A("dumpB", 0, 16), O.min)
         tt(A("sm", 32, 48), A("sm", 16, 32), BWf, O.max)
-        for h in range(2):
-            tt(H("M6", h), OFF[h], H("maskS", h), O.mult)
-        for h in range(2):
-            scan(H("SC6", h), H("rst", h), H("M6", h))
-        cp(A("boU", 0, 16), A("sm", 32, 48))
-        ts(A("OWu", 0, 16), W("SC6"), 0.5, O.mult, 2048.0, O.add)
+        cp(L("boU"), A("sm", 32, 48))
+        tt(IND(A("vt", 0, 1296), L("boU")), R("V2"), R("tm"), O.add)
         if not last:
+            ts(A("sm", 48, 64), W("SC5"), float(NONE - RL0), O.min, float(RL0), O.add)
             tt(A("sm", 64, 80), W("SC6"), BWf, O.max)
             tt(A("sm", 80, 96), W("SC6"), A("sm", 48, 64), O.max)
-        tt(IND(A(win, 0, WIN), A("OWu", 0, 16)), R("t32"), R("G"), O.add)
-        sync_for(P, "g", [(win, 0, WIN, 1)], [])
-        sends = plan(topo, T.cores, me)
-        for call in sends:
-            g.remote_dma_fused([RemoteDMATransfer(
-                dst_ids=[DstId(rid=topo.addr(T.cores[r], core)[0], pnc=topo.addr(T.cores[r], core)[1])],
-                dma_engine_mask=sum(1 << e for e in engines), remote_sem=T.sem["arr%d" % st],
-                src=T[win][:, 256 * r:256 * r + 32], dst=T[land][:, 32 * me:32 * me + 32])
-                for r, engines in call], local_sem=T.sem["loc"])
-        out_n = sum(len(e) for call in sends for r, e in call)
-        arrive = sum(len(e) for q in range(8) if q != me for call in plan(topo, T.cores, q) for r, e in call if r == me)
-        for q in range(8):
-            if q != me:
-                note(P, "remote", [], [(land, 32 * q, 32 * q + 32, 1)], "arr%d" % st, arrive)
-        act(A(land, 32 * me, 32 * me + 32), A(win, 256 * me, 256 * me + 32), F.Copy)
-        if not last:
             cp(A("uaU", 0, 32), A("sm", 64, 96))
-        tt(IND(A("vt", 0, 1296), A("boU", 0, 16)), R("V2"), R("tm"), O.add)
-        if not last:
             tt(IND(A("ut", 0, WIN), A("uaU", 0, 16)), R("UI"), R("sS"), O.max)
             tt(IND(A("at", 0, WIN), A("uaU", 16, 32)), R("Agl"), R("nt"), O.add)
 
-    sync_for(P, "y", [("vt", 0, 1024, 1)], [])
-    y.dma_start(T.yv[:], T.vt[:, 0:1024]).then_inc(T.sem["dyv"], 16)
+    def store(q, dst, src, view, sem, size):
+        def emit():
+            sync_for(P, q, regions([view]), [])
+            P["eng"][q].dma_start(dst, src).then_inc(T.sem[sem], 16)
+        record(P, q, 50.0, regions([view]), [], emit, lag=DMA + size * BYTE)
+    store("y", T.yv[:], T.vt[:, 0:1024], A("vt", 0, 1024), "dyv", 262144)
     whole("land3")
     act(R("ywS"), R("cm"), F.Identity, bias=-MAGIC - WR // 1024 * me - 1)
     for h in range(2):
         tt(H("cB", h), H("land3", h), H(XP, h), O.subtract)
-    sync_for(P, "s", regions([R("ywS")]), [])
-    s.dma_start(T.yw[:], T.ywS[0:128:16, 0:256]).then_inc(T.sem["dyw"], 16)
-    sync_for(P, "y", regions([R("cB")]), [])
-    y.dma_start(T.yc[:], T.cB[:, 0:256]).then_inc(T.sem["dyc"], 16)
+    store("s", T.yw[:], T.ywS[0:128:16, 0:256], R("ywS"), "dyw", 8192)
+    store("y", T.yc[:], T.cB[:, 0:256], R("cB"), "dyc", 65536)
+    issue_all(P)
     for sem in ("sv", "ss", "sp", "sg"):
         g.wait_ge(T.sem[sem], P["cnt"][sem])
     for sem in ("dwk", "dvp", "dqu", "dam", "dpa", "dpb", "dyv", "dyw", "dyc"):

@@ -5,14 +5,13 @@ WIN = 4096
 SCRATCH = {}
 for _n in "land0 land1 land2 land3 M1 SC cm cm2 cm3 UI sS M5 SC5 G t32 ywS E r32".split():
     SCRATCH[_n] = ("sbuf", [128, 256], "float32")
-for _n in "maskS rst ones V1 V2 NVr eqd eqe w nsgn OH Agl nt tm cB l15 i144 l4".split():
+for _n in "maskS rst ones V1 V2 NVr eqd eqe w nsgn OH Agl An tm cB l15 i144 l4".split():
     SCRATCH[_n] = ("sbuf", [128, 256], "bfloat16")
 for _n in "xh wkh pU prod M6 SC6".split():
     SCRATCH[_n] = ("sbuf", [128, 256], "float16")
-for _n in "blk1 blkT blkZ blkL blkS blk2 idB nI DM DM0 DM1 W5 W5a W5b W5c TC S8 PB PB0 PB1 sel8 selT".split():
+for _n in "blk1 blkT blkZ blkL blkS blk2 idB nI DM DM0 DM1 W5 W5a W5b W5c TC S8 PB PB0 PB1 sel8".split():
     SCRATCH[_n] = ("sbuf", [128, 128], "bfloat16")
-for _n in "Lu Uo".split():
-    SCRATCH[_n] = ("sbuf", [128, 256], "uint16")
+SCRATCH["Uo"] = ("sbuf", [128, 256], "uint16")
 for _n in "BWu LWu OWu boU".split():
     SCRATCH[_n] = ("sbuf", [128, 16], "uint16")
 for _n in "ge Ag eqx eqy".split():
@@ -22,10 +21,10 @@ for _n in range(3):
 for _n in range(8):
     SCRATCH["b%d" % _n] = ("psum", [128, 512], "float32")
 SCRATCH["wkb"] = ("sbuf", [128, 256], "int32")
-SCRATCH["l16"] = ("sbuf", [128, 16], "int32")
+SCRATCH["l16"] = ("sbuf", [128, 16], "float32")
 SCRATCH["pci"] = ("sbuf", [128, 8], "int32")
 SCRATCH["selB"] = ("sbuf", [128, 144], "bfloat16")
-SCRATCH["quS"] = ("sbuf", [128, 1024], "int32")
+SCRATCH["quS"] = ("sbuf", [128, 1032], "int32")
 SCRATCH["payS"] = ("sbuf", [128, 400], "int32")
 SCRATCH["payI"] = ("sbuf", [128, 400], "int32")
 SCRATCH["payH"] = ("sbuf", [128, 400], "float16")
@@ -37,7 +36,7 @@ SCRATCH["pt"] = ("sbuf", [128, 3200], "float32")
 SCRATCH["col"] = ("sbuf", [128, 48], "float32")
 SCRATCH["dumpB"] = ("sbuf", [128, 16], "float32")
 SCRATCH["uaU"] = ("sbuf", [128, 32], "uint16")
-SCRATCH["sm"] = ("sbuf", [128, 96], "float32")
+SCRATCH["sm"] = ("sbuf", [128, 112], "float32")
 SEMAPHORES = ["sv", "ss", "sp", "sg", "dwk", "dvp", "dqu", "dam", "dpa", "dpb", "dyv", "dyw", "dyc", "loc", "arr0", "arr1", "arr2"]
 NONE = 3199
 MAGIC = 12582912.0
@@ -48,16 +47,19 @@ T0 = 17 * 2 ** 16
 KS = 2304
 RL0 = U0 + 15 * 2048 + 16 * KS
 BETA, THETA = 0.58, 0.40625
-GATHERS = [(0, 64), (64, 128), (128, 192), (192, 224), (224, 256)]
+HEAD = [(0, 64), (64, 256)]
+GATHERS = [(0, 64), (64, 128), (128, 192), (192, 232), (232, 256)]
 CHUNKS = [(0, 64), (64, 128), (128, 192), (192, 256)]
 GROUPS = [(0, 128), (128, 192), (192, 256)]
-PLACES = [(0, 192), (192, 256)]
-SBANK, RBANK, TBANK = ["b3", "b4", "b2"], ["b5", "b6", "b5"], ["b7", "b1"]
+PLACES = GROUPS
+SBANK, RBANK, TBANK = ["b3", "b4", "b2"], ["b5", "b6", "b5"], ["b7", "b1", "b6"]
 HOP, CYCLE, GATHER, SCATTER = 150.0, 0.83, 1.56, 3.8
 ROWS = [("s", "Ag"), ("v", "ge"), ("v", "eqx"), ("v", "eqy"), ("s", "pt")] + [("p", "b%d" % k) for k in range(8)]
-SAME = {("s", "b1"): ("s", "Ag"), ("v", "eqx"): ("v", "ge"), ("v", "eqd"): ("v", "ge")}
-TURNS = 2
-BYTE, DMA, SEND, FLIGHT = 0.0045, 1200.0, 1000.0, 2000.0
+ROWS += [("v", "M1")]
+SAME = {("v", "vt"): ("v", "M1"), ("s", "b1"): ("s", "Ag"), ("v", "eqx"): ("v", "ge"), ("v", "eqd"): ("v", "ge")}
+TURNS, PATIENCE = 6, [100.0, 100.0, 200.0]
+GOALS = "".split()
+BYTE, DMA, SEND, FLIGHT = 0.004, 1350.0, 700.0, 1550.0
 
 
 def A(name, c0, c1, step=1, p0=0, p1=128):
@@ -188,7 +190,7 @@ def issue_all(P):
         pre = {}
         for kind in "rw":
             for r in c[kind]:
-                for m, k2, r2 in seen.get(r[0], []):
+                for m, k2, r2 in seen.get(r[0], []) if c["q"] in P["eng"] else ():
                     if (kind == "w" or k2 == "w") and hits(r, r2):
                         both = c["group"] and calls[m]["group"] and kind == "w"
                         if both and not any(c["group"][1:] + calls[m]["group"][1:]):
@@ -224,15 +226,17 @@ def issue_all(P):
     for n in range(len(calls) - 1, -1, -1):
         c = calls[n]
         c["way"] = c["ns"] + c["lag"] + max([calls[m]["way"] + calls[m]["pre"][n] for m in c["post"]] + [0.0])
-    order = sorted(range(len(calls)), key=lambda n: (-calls[n]["way"], n))
+        name = c["w"][0][0] if c["w"] and n < P["first"] else None
+        c["goal"] = min([GOALS.index(name) if name in GOALS else len(GOALS)] + [calls[m]["goal"] for m in c["post"]])
+    order = sorted(range(len(calls)), key=lambda n: (calls[n]["goal"], -calls[n]["way"], n))
     best = None
     for turn in range(TURNS):
-        at = place(calls, order, False)
+        at = eager(calls, order, PATIENCE[turn // 2]) if turn % 2 else place(calls, order, False)
         end = max(at[n] + c["ns"] + c["lag"] for n, c in enumerate(calls))
         if best is None or end < best[0]:
             best = (end, sorted(range(len(calls)), key=lambda n: (at[n], n)))
         back = place(calls, sorted(range(len(calls)), key=lambda n: (-at[n] - calls[n]["ns"], -n)), True)
-        order = sorted(range(len(calls)), key=lambda n: (-back[n] - calls[n]["ns"], n))
+        order = sorted(range(len(calls)), key=lambda n: (calls[n]["goal"], -back[n] - calls[n]["ns"], n))
     for n in best[1]:
         calls[n]["emit"]()
 
@@ -260,6 +264,29 @@ def place(calls, order, back):
         at[n] = t
         for key in [c["q"]] + c["banks"]:
             busy[key].insert(after(busy[key], t), (t, t + c["ns"], c["q"]))
+    return at
+
+
+def eager(calls, order, patience):
+    rank = {n: k for k, n in enumerate(order)}
+    left = [len(c["pre"]) for c in calls]
+    at, free, used = {}, {}, {}
+    ready = {n: 0.0 for n, c in enumerate(calls) if not c["pre"]}
+    while ready:
+        can = {n: max([t, free.get(calls[n]["q"], 0.0)] + [e + HOP for b in calls[n]["banks"] for q, e in used.get(b, {}).items()
+                                                           if q != calls[n]["q"]]) for n, t in ready.items()}
+        soon = min(can, key=lambda n: can[n])
+        n = min((m for m in can if calls[m]["q"] == calls[soon]["q"] and can[m] <= can[soon] + patience), key=lambda m: rank[m])
+        c = calls[n]
+        at[n] = can[n]
+        free[c["q"]] = at[n] + c["ns"]
+        for b in c["banks"]:
+            used.setdefault(b, {})[c["q"]] = free[c["q"]]
+        del ready[n]
+        for m in c["post"]:
+            left[m] -= 1
+            if left[m] == 0:
+                ready[m] = max(at[k] + calls[k]["ns"] + calls[k]["lag"] + hop for k, hop in calls[m]["pre"].items())
     return at
 
 
@@ -313,30 +340,31 @@ def rank_program(g, core, T, topo):
     load("y", A("wkb", 0, 256, 1, 0, 8), T.wk[:], "dwk", 8192)
     load("y", A("payS", 0, 400, 1, 0, 64), T.pay[:], "dpa", 102400)
     load("y", A("payS", 0, 400, 1, 64, 128), T.pay[:], "dpb", 102400)
-    load("s", A("vt", 0, 1024), T.vp[:], "dvp", 262144)
     load("y", A("quS", 0, 1024), T.qu[:], "dqu", 524288)
     load("y", A("at", 0, 3200), T.am[:], "dam", 819200)
+    load("y", A("vt", 0, 1024), T.vp[:], "dvp", 262144)
 
     imp = {"allow_small_or_imprecise_dtypes": True}
 
     def block(out, tmp, src):
         pick(tmp, src, [[-16, 8], [0, 16]], O.is_ge, 0, 1)
         pick(out, tmp, [[16, 8], [0, 16]], O.is_ge, 15, -1)
-    iota(A("pci", 0, 1), [[1, 1]], 0, 1)
+    iota(A("pci", 5, 6), [[1, 1]], 0, 1)
     iota(R("l15"), [[0, 16], [1, 16]], 0, 0, **imp)
     fill(R("ones"), 1.0)
     pick(A("sel8", 0, 128, 1, 0, 8), A("ones", 0, 128, 1, 0, 8), [[1, 8], [0, 16]], O.is_equal, 0, -1)
-    pick(R("rst"), R("ones"), [[0, 16], [1, 16]], O.not_equal, 0, 0)
+    ts(R("rst"), R("l15"), 0.0, O.not_equal)
     iota(M("l4"), [[1, 8], [0, 16]], 0, 0, **imp)
-    iota(A("i144", 0, 144), [[1, 144]], 0, 0, **imp)
+    iota(A("i144", 0, 144), [[1, 144]], -16, 0, **imp)
     block(M("blk1"), M("blkT"), M("ones"))
     iota(R("r32"), [[1, 8], [0, 32]], 0, 0, **imp)
     pick(M("idB"), M("ones"), [[-1, 128]], O.is_equal, 0, 1)
     iota(M("W5a"), [[0, 128]], -BIG, 0, **imp)
-    iota(A("l16", 0, 16), [[16, 16]], 0, 0)
+    iota(A("l16", 0, 16), [[16, 16]], 1025, 0, **imp)
     pick(M("W5b"), M("W5a"), [[0, 8], [1, 16]], O.not_equal, -8, 0, float(BIG))
     block(M("W5"), M("W5c"), M("W5b"))
-    p0 = A("pci", 0, 1)
+    p0 = A("pci", 5, 6)
+    ts(A("pci", 0, 1), p0, 112, O.bitwise_and)
     ts(A("pci", 1, 2), p0, 15, O.bitwise_and)
     ts(A("pci", 2, 3), p0, 7, O.bitwise_and)
     ts(A("pci", 3, 4), p0, 3, O.arith_shift_right, 7, O.bitwise_and)
@@ -348,39 +376,38 @@ def rank_program(g, core, T, topo):
     ts(J8, PM, 8.0, O.is_lt)
     ts(R(maskP), R("l15"), PM, O.is_equal)
     ts(R("maskS"), R("l15"), PM, O.is_equal)
-    ts(SCE, J8, float(WR), O.mult)
-    ts(C(20), J8, float(-WR), O.mult, float(WR + 1024), O.add)
-    ts(C(21), SCE, PM, O.mult)
     ts(EQ8, PM, 8.0, O.is_equal)
-    tt(BPT, C(20), C(21), O.subtract)
-    ts(C(22), SCE, float(me), O.mult, -1024.0, O.add)
-    tt(Q, C(22), BPT, O.add)
-    ts(C(26), Q, 0.0, O.is_ge, 2.0, O.mult)
-    ts(SIG, C(26), -1.0, O.add)
-    ts(SG, SIG, 1.0 / 1024, O.mult)
-    ts(K1, Q, -1.0 / 1024, O.mult, -0.75, O.add)
-    ts(K2, Q, -1.0 / 1024, O.mult, 1023.0, O.add)
-    ts(K3, Q, -1.0 / 1024, O.mult, MAGIC + 1023.0, O.add)
-    fill(A("vt", 1024, 1040), 0.0)
+
+    def lin(out, x, scale, bias): act(out, x, F.Identity, scale=scale, bias=bias)
+    lin(SCE, J8, float(WR), 0.0)
+    lin(C(20), J8, float(-WR), float(WR + 1024))
+    ts(C(21), PM, float(-WR), O.mult, J8, O.mult)
+    lin(BPT, C(21), 1.0, C(20))
+    lin(Q, SCE, float(me), BPT)
+    act(SIG, Q, F.Sign)
+    lin(SG, SIG, 1.0 / 1024, 0.0)
+    lin(K1, Q, -1.0 / 1024, 0.25)
+    lin(K2, Q, -1.0 / 1024, 1024.0)
+    lin(K3, Q, -1.0 / 1024, MAGIC + 1024.0)
+    act(A("vt", 1024, 1040), A("ones", 0, 16), F.Copy, scale=0.0)
     fill(A("ut", 1024, 1032), 1.0)
-    ts(C(23), C(0), PM, O.subtract, 16.0, O.add)
-    ts(A("selB", 0, 144), A("i144", 0, 144), C(23), O.is_equal)
+    fill(A("quS", 1024, 1032), NONE)
+    ts(A("selB", 0, 144), A("i144", 0, 144), C(0), O.is_equal)
     for name, factor in (("blkL", 2048.0), ("blkS", float(KS)), ("blk2", 2.0), ("blkZ", -16384.0), ("DM0", -THETA)):
         act(M(name), M("blk1"), F.Copy, scale=factor)
-    ts(C(27), EQ8, -512.0, O.mult)
+    lin(C(27), EQ8, -512.0, 0.0)
     act(M("S8"), M("blk1"), F.Copy, scale=C(27))
-    ts(C(28), EQ8, -2.0 * BIG, O.mult, float(T0 + BIG), O.add)
+    lin(C(28), EQ8, -2.0 * BIG, float(T0 + BIG))
     act(M("TC"), M("idB"), F.Copy, scale=C(28))
-    ts(C(29), EQ8, 1792.0, O.mult, -2049.0, O.add)
-    ts(INI, PM, 256.0, O.mult, C(29), O.add)
+    lin(C(29), EQ8, 1792.0, -2049.0)
+    lin(INI, PM, 256.0, C(29))
     act(M("nI"), M("idB"), F.Copy, scale=-1.0)
-    ts(A("dumpB", 0, 16), A("l16", 0, 16), PM, O.add, 1025.0, O.add)
-    ts(C(25), PM, BETA, O.mult, -7.5 * BETA, O.add)
-    act(EJ, C(25), F.Exp)
+    lin(A("dumpB", 0, 16), A("l16", 0, 16), 1.0, PM)
+    act(EJ, PM, F.Exp, scale=BETA, bias=-7.5 * BETA)
     P["calls"][-1]["ns"] += 1300.0
     pick(M("DM1"), M("DM0"), [[-1, 128]], O.not_equal, 0, 1, 1.0 - THETA)
     act(M("DM"), M("DM1"), F.Copy, scale=EJ)
-    ts(C(30), BPT, 1024.0 * 1024, O.add)
+    lin(C(30), BPT, 1.0, 1024.0 * 1024)
     act(R("E"), R("r32"), F.Abs, scale=SCE, bias=C(30))
     for k in range(3):
         for r in range(8):
@@ -388,21 +415,20 @@ def rank_program(g, core, T, topo):
 
     ts(C(24), C(4), float(WR - 1024), O.mult, 1024.0, O.add)
     ts(M("PB0"), M("l4"), C(3), O.is_equal, C(24), O.mult)
-    ts(A("col", 32, 40), A("i144", 0, 8), C(2), O.is_equal)
+    ts(A("col", 32, 40), A("l15", 0, 8), C(2), O.is_equal)
     ts(C(31), C(4), -8.0, O.mult, 16.0, O.add)
     ts(M("PB1"), M("l15"), C(31), O.is_lt)
     tt(M("PB"), M("PB0"), M("PB1"), O.mult)
     ts(A("payI", 0, 400, 1, 0, 64), A("payS", 0, 400, 1, 0, 64), 1023, O.bitwise_and)
     ts(A("payH", 0, 400, 1, 64, 128), A("payS", 0, 400, 1, 64, 128), 1.0 / 1024, O.mult, 1025 - 511.5 / 1024, O.add)
     cp(A("payH", 0, 400, 1, 0, 64), A("payI", 0, 400, 1, 0, 64))
-    ts(C(15), SCE, -1025.0, O.mult, BPT, O.add)
+    lin(C(15), SCE, -1025.0, BPT)
     for c in range(8):
         ts(A("PL", 128 * c, 128 * c + 128), M("PB"), C(32 + c), O.mult)
         bank = A("b%d" % (3 + c % 4), 0, 400)
         mm(bank, A("PL", 128 * c, 128 * c + 128), A("payH", 0, 400), True, True)
         act(A("pt", 400 * c, 400 * c + 400), bank, F.Abs, bias=C(15))
-    ts(NOW, EQ8, float(-WR), O.mult, float(WR), O.add)
-    act(A("pt", NONE, NONE + 1), NOW, F.Copy)
+    lin(A("pt", NONE, NONE + 1), EQ8, float(-WR), float(WR))
     for c in range(4):
         ts(A("ut", 256 * c, 256 * c + 256), A("quS", 256 * c, 256 * c + 256), float(-U0), O.add, 1.0 / 2048, O.mult)
 
@@ -436,31 +462,35 @@ def rank_program(g, core, T, topo):
     for st in range(3):
         first, last = st == 0, st == 2
         old, win, land = "land%d" % st, "win%d" % st, "land%d" % (st + 1)
-        head = ((0, 64), (64, 256))
         sg, k1, k2, k3 = (1.0 / 1024, -0.75, 1023.0, MAGIC + 1023.0) if first else (SG, K1, K2, K3)
-        for lo, hi in head:
+
+        def gather(lo, hi):
+            act(A("Ag", 16 * lo, 16 * hi), IND(A("at", 0, 3200), R("Uo", lo, hi)), F.Copy)
+        for lo, hi in [(0, 256)] if first else HEAD:
             tt(R("M1", lo, hi), R(old, lo, hi), R(maskP, lo, hi), O.mult)
             scan(R("SC", lo, hi), R("rst", lo, hi), R("M1", lo, hi))
             ts(L("BWu", lo, hi), W("SC", lo, hi), sg, O.mult, k1, O.add)
+            if first:
+                cp(R("Uo"), IND(A("quS", 0, 1032), L("BWu")))
+            else:
+                ts(R("Uo", lo, hi), IND(A("ut", 0, 1032), L("BWu", lo, hi)), 2048.0, O.mult, float(U0), O.add)
             act(R("cm2", lo, hi), R("SC", lo, hi), F.Identity, bias=k3, scale=sg)
             act(R(SCc, lo, hi), R("cm2", lo, hi), F.Identity, bias=-MAGIC)
-        ts(R("Uo", 0, 64), IND(A("ut", 0, 1032), L("BWu", 0, 64)), 2048.0, O.mult, float(U0), O.add)
-        ts(R("UI", 0, 64), R("Uo", 0, 64), float(-U0), O.add, 1.0 / 2048, O.mult)
-        cp(R("UI", 64, 256), IND(A("ut", 0, 1032), L("BWu", 64, 256)))
-        ts(R("Uo", 64, 256), R("UI", 64, 256), 2048.0, O.mult, float(U0), O.add)
+        for h in range(2):
+            ts(H("xh", h), H(old, h), sg, O.mult, k2, O.add)
+        ts(R("UI"), R("Uo"), float(-U0), O.add, 1.0 / 2048, O.mult)
         banks = IND(A("vt", 0, 1040), L("BWu"))
         if first:
-            cp(R("V1"), banks)
+            ts(R("NVr"), banks, -1.0, O.mult, 0.0, O.max)
+            act(R("V2"), banks, F.Copy)
         else:
             whole(old)
             tt(R("cB"), R(old), R(XP), O.subtract)
             tt(R("V1"), banks, R("cB"), O.subtract)
-        ts(R("NVr"), R("V1"), -1.0, O.mult, 0.0, O.max)
+            ts(R("NVr"), R("V1"), -1.0, O.mult, 0.0, O.max)
+            act(R("cm3"), R("V1"), F.Relu, bias=255.0)
+            act(R("V2"), R("cm3"), F.Identity, bias=-255.0)
         ts(R(nP, 0, 256, 256), R("NVr"), 255.0, O.min)
-        act(R("cm3"), R("V1"), F.Relu, bias=255.0)
-        act(R("V2"), R("cm3"), F.Identity, bias=-255.0)
-        for h in range(2):
-            ts(H("xh", h), H(old, h), sg, O.mult, k2, O.add)
         tt(R("eqd"), R("xh"), R(SCc), O.is_equal)
         mm(R(Z, 0, 256, 256), M("blkZ"), R("eqd"), True, False)
         for a in range(15):
@@ -471,12 +501,13 @@ def rank_program(g, core, T, topo):
         mm(R(Z, 0, 256, 256), M("blk1"), R("NVr"), False, True)
         act(R("nsgn"), R(Z, 0, 256, 256), F.Sign, bias=-16384.0, scale=-1.0)
         BWf = A("sm", 0, 16)
-        cp(BWf, L("BWu"))
+        act(BWf, W(SCc), F.Identity, bias=-1024.0)
+        P.setdefault("first", len(P["calls"]))
         for lo, hi in GATHERS:
-            if first and lo == 0:
+            if (lo, hi) == GATHERS[0 if first else -1]:
                 cp(A("Ag", 16 * lo, 16 * hi), IND(A("at", 0, 3200), R("Uo", lo, hi)))
             else:
-                act(A("Ag", 16 * lo, 16 * hi), IND(A("at", 0, 3200), R("Uo", lo, hi)), F.Copy)
+                gather(lo, hi)
 
         def thr(lo, hi):
             k = [n for n, (a, b) in enumerate(PLACES) if a <= lo < b][0]
@@ -498,20 +529,22 @@ def rank_program(g, core, T, topo):
             if not last:
                 act(R("sS", lo, hi), sg, F.Copy)
             tt(R("M5", lo, hi), RL, R("maskS", lo, hi), O.mult)
-            ts(R("Lu", lo, hi), RL, RL0 + 1.0, O.add)
             scan(R("SC5", lo, hi), R("rst", lo, hi), R("M5", lo, hi))
             lw = L("LWu", lo, hi)
             ts(lw, W("SC5", lo, hi), float(NONE - RL0), O.min, float(RL0), O.add)
             act(R("G", lo, hi), IND(A("pt", 0, 3200), lw), F.Copy)
             act(R("Agl", lo, hi), IND(A("at", 0, 3200), lw), F.Copy)
-            tt(R("t32", lo, hi), R("Agl", lo, hi), R(nP, lo, hi, 256), O.min)
+            for out, less, f, c0 in (("An", "NVr", F.Relu, 0), ("t32", "An", F.Copy, 128)):
+                mm(A(S, c0, c0 + n), M("idB"), R("Agl", lo, hi), True, False)
+                mm(A(S, c0, c0 + n), M("nI"), R(less, lo, hi), False, True)
+                act(R(out, lo, hi), A(S, c0, c0 + n), f)
             for p0, p1 in PLACES:
                 if p0 == lo:
                     mm(thr(p0, p1), M("TC"), R("ones", p0, p1), True, False)
             for a in range(hi // 16 - 1):
                 c = max(lo, 16 * (a + 1))
                 e = R("eqy", c, hi, 256 * a)
-                ts(e, R("Lu", c, hi), -1.0 - RL0, O.add, A("SC5", 16 * a + 15, 16 * a + 16), O.is_equal)
+                ts(e, A(RBANK[k], c, hi), A("SC5", 16 * a + 15, 16 * a + 16), O.is_equal)
                 mm(thr(c, hi), M("W5"), e, False, False)
             tt(R("eqe", lo, hi), R("SC5", lo, hi), RL, O.is_equal)
             mm(thr(lo, hi), M("W5"), R("eqe", lo, hi), False, any(hi == p1 for p0, p1 in PLACES))
@@ -529,21 +562,22 @@ def rank_program(g, core, T, topo):
                     tt(IND(A(win, 0, WIN), L("OWu", p0, p1)), R("t32", p0, p1), R("G", p0, p1), O.add)
         exchange(st, win, land)
         act(A(land, 32 * me, 32 * me + 32), A(win, 256 * me, 256 * me + 32), F.Copy)
-        act(R("nt"), R("t32"), F.Copy, scale=-1.0)
         mm(R("b2"), M("S8"), R("OH"), True, False)
-        mm(R("b2"), M("nI"), R("nt"), False, True)
+        mm(R("b2"), M("idB"), R("Agl"), False, False)
+        mm(R("b2"), M("nI"), R("An"), False, True)
         act(R("tm"), R("b2"), F.Relu)
         tt(A("sm", 16, 32), W("SC5"), A("dumpB", 0, 16), O.min)
         tt(A("sm", 32, 48), A("sm", 16, 32), BWf, O.max)
         cp(L("boU"), A("sm", 32, 48))
         tt(IND(A("vt", 0, 1296), L("boU")), R("V2"), R("tm"), O.add)
         if not last:
-            ts(A("sm", 48, 64), W("SC5"), float(NONE - RL0), O.min, float(RL0), O.add)
+            act(A("sm", 96, 112), W("SC5"), F.Relu, bias=float(NONE - RL0), scale=-1.0)
+            lin(A("sm", 48, 64), A("sm", 96, 112), -1.0, float(NONE))
             tt(A("sm", 64, 80), W("SC6"), BWf, O.max)
             tt(A("sm", 80, 96), W("SC6"), A("sm", 48, 64), O.max)
             cp(A("uaU", 0, 32), A("sm", 64, 96))
             tt(IND(A("ut", 0, WIN), A("uaU", 0, 16)), R("UI"), R("sS"), O.max)
-            tt(IND(A("at", 0, WIN), A("uaU", 16, 32)), R("Agl"), R("nt"), O.add)
+            cp(IND(A("at", 0, WIN), A("uaU", 16, 32)), R("An"))
 
     def store(q, dst, src, view, sem, size):
         def emit():

from concourse.bass import DstId, RemoteDMATransfer
from concourse.mybir import AluOpType as O, ActivationFunctionType as F

WIN = 4096
SCRATCH = {}
for _n in "land0 land1 land2 land3 M1 SC cm cm2 cm3 UI sS M5 SC5 G t32 ywS E r32".split():
    SCRATCH[_n] = ("sbuf", [128, 256], "float32")
for _n in "maskS rst ones V1 V2 NVr eqd eqe w nsgn OH Agl An tm cB l15 i144 l4".split():
    SCRATCH[_n] = ("sbuf", [128, 256], "bfloat16")
for _n in "xh wkh pU prod M6 SC6".split():
    SCRATCH[_n] = ("sbuf", [128, 256], "float16")
for _n in "blk1 blkT blkZ blkL blkS blk2 idB nI DM DM0 DM1 W5 W5a W5b W5c TC S8 PB PB0 PB1 sel8".split():
    SCRATCH[_n] = ("sbuf", [128, 128], "bfloat16")
SCRATCH["Uo"] = ("sbuf", [128, 256], "uint16")
for _n in "BWu LWu OWu boU".split():
    SCRATCH[_n] = ("sbuf", [128, 16], "uint16")
for _n in "ge Ag eqx eqy".split():
    SCRATCH[_n] = ("sbuf", [128, 4096], "bfloat16")
for _n in range(3):
    SCRATCH["win%d" % _n] = ("sbuf", [128, WIN], "float32")
for _n in range(8):
    SCRATCH["b%d" % _n] = ("psum", [128, 512], "float32")
SCRATCH["wkb"] = ("sbuf", [128, 256], "int32")
SCRATCH["l16"] = ("sbuf", [128, 16], "float32")
SCRATCH["pci"] = ("sbuf", [128, 8], "int32")
SCRATCH["selB"] = ("sbuf", [128, 144], "bfloat16")
SCRATCH["quS"] = ("sbuf", [128, 1032], "int32")
SCRATCH["payS"] = ("sbuf", [128, 400], "int32")
SCRATCH["payI"] = ("sbuf", [128, 400], "int32")
SCRATCH["payH"] = ("sbuf", [128, 400], "float16")
SCRATCH["PL"] = ("sbuf", [128, 1024], "bfloat16")
SCRATCH["ut"] = ("sbuf", [128, WIN], "float32")
SCRATCH["vt"] = ("sbuf", [128, 1296], "bfloat16")
SCRATCH["at"] = ("sbuf", [128, WIN], "bfloat16")
SCRATCH["pt"] = ("sbuf", [128, 3200], "float32")
SCRATCH["col"] = ("sbuf", [128, 48], "float32")
SCRATCH["dumpB"] = ("sbuf", [128, 16], "float32")
SCRATCH["uaU"] = ("sbuf", [128, 32], "uint16")
SCRATCH["sm"] = ("sbuf", [128, 112], "float32")
SEMAPHORES = ["sv", "ss", "sp", "sg", "dwk", "dvp", "dqu", "dam", "dpa", "dpb", "dyv", "dyw", "dyc", "loc", "arr0", "arr1", "arr2"]
NONE = 3199
MAGIC = 12582912.0
U0 = NONE - 2048
WR = 17 * 2 ** 17
BIG = 2 ** 22
T0 = 17 * 2 ** 16
KS = 2304
RL0 = U0 + 15 * 2048 + 16 * KS
BETA, THETA = 0.58, 0.40625
HEAD = [(0, 64), (64, 256)]
GATHERS = [(0, 64), (64, 128), (128, 192), (192, 232), (232, 256)]
CHUNKS = [(0, 64), (64, 128), (128, 192), (192, 256)]
GROUPS = [(0, 128), (128, 192), (192, 256)]
PLACES = GROUPS
SBANK, RBANK, TBANK = ["b3", "b4", "b2"], ["b5", "b6", "b5"], ["b7", "b1", "b6"]
HOP, CYCLE, GATHER, SCATTER = 150.0, 0.83, 1.56, 3.8
ROWS = [("s", "Ag"), ("v", "ge"), ("v", "eqx"), ("v", "eqy"), ("s", "pt")] + [("p", "b%d" % k) for k in range(8)]
ROWS += [("v", "M1")]
SAME = {("v", "vt"): ("v", "M1"), ("s", "b1"): ("s", "Ag"), ("v", "eqx"): ("v", "ge"), ("v", "eqd"): ("v", "ge")}
TURNS, PATIENCE = 6, [100.0, 100.0, 200.0]
GOALS = "".split()
BYTE, DMA, SEND, FLIGHT = 0.004, 1350.0, 700.0, 1550.0


def A(name, c0, c1, step=1, p0=0, p1=128):
    return ("A", name, c0, c1, step, p0, p1)


def IND(win, off):
    return ("I", win, off)


def is_view(x):
    return isinstance(x, tuple) and len(x) > 0 and (x[0] == "A" or x[0] == "I")


def hits(a, b):
    if a[2] <= b[1] or b[2] <= a[1]:
        return False
    return not (a[3] > 1 and a[3] == b[3] and (a[1] - b[1]) % a[3] != 0)


def is_psum(name):
    return len(name) == 2 and name[0] == "b"


def resolve(P, x):
    if x[0] == "I":
        return resolve(P, x[1]).indirect(resolve(P, x[2]))
    t = P["T"][x[1]]
    if x[4] == 1:
        return t[x[5]:x[6], x[2]:x[3]]
    return t[x[5]:x[6], x[2]:x[3]:x[4]]


def regions(views):
    out = []
    for v in views:
        if v[0] == "I":
            out += regions([v[1], v[2]])
        else:
            out.append((v[1], v[2], v[3], v[4]))
    return out


def width(x):
    return 16 * width(x[2]) if x[0] == "I" else (x[3] - x[2] + x[4] - 1) // x[4]


def dtype(x):
    return SCRATCH[x[1]][2]


def sync_for(P, q, reads, writes):
    need = []
    for kind, regs in (("r", reads), ("w", writes)):
        for r in regs:
            ps = is_psum(r[0])
            for hk, hr, hq, sem, val, clock in P["hist"].get(r[0], []):
                same = hq == q
                if same or not ps:
                    if (hk == "r" and kind == "r") or (same and kind == "w" and q == "p") or not hits(r, hr):
                        continue
                need.append((sem, val, clock))
    best = {}
    for sem, val, clock in need:
        if P["known"][q].get(sem, 0) < val and (sem not in best or best[sem][0] < val):
            best[sem] = (val, clock)
    for sem in list(best):
        if any(s2 != sem and best[s2][1].get(sem, 0) >= best[sem][0] for s2 in best):
            del best[sem]
    for sem in best:
        val, clock = best[sem]
        P["eng"][q].wait_ge(P["T"].sem[sem], val)
        k = P["known"][q]
        for s2, v2 in clock.items():
            if k.get(s2, 0) < v2:
                k[s2] = v2


def note(P, q, reads, writes, sem, val):
    clock = dict(P["known"].get(q, {}))
    clock[sem] = max(val, clock.get(sem, 0))
    for kind, regs in (("r", reads), ("w", writes)):
        for r in regs:
            lst = P["hist"].setdefault(r[0], [])
            if kind == "w" and r[3] == 1:
                lst[:] = [h for h in lst if not (h[2] == q and r[1] <= h[1][1] and h[1][2] <= r[2])]
            lst.append((kind, r, q, sem, val, clock))


SEM_OF = {"v": "sv", "s": "ss", "p": "sp", "g": "sg"}


def record(P, q, ns, reads, writes, emit, lag=0.0, group=None):
    P["calls"].append({"q": q, "ns": ns, "lag": lag, "r": reads, "w": writes, "emit": emit, "group": group})


def op(P, q, cycles, fn, out, *args, **kw):
    ins = [a for a in args if is_view(a)] + [a for a in kw.values() if is_view(a)]
    reads = regions(ins)
    n = width(out)
    if out[0] == "I":
        writes = regions([out[1]])
        reads += regions([out[2]])
        ns = 50 + n * SCATTER * CYCLE
    else:
        writes = regions([out])
        if any(a[0] == "I" for a in ins):
            ns = 60 + n * GATHER * CYCLE
        elif q == "g":
            ns = 150 + 2 * n * CYCLE
        else:
            ns = max(64, n * cycles) * CYCLE

    def emit():
        sync_for(P, q, reads, writes)
        sem = SEM_OF[q]
        P["cnt"][sem] += 1
        fn(resolve(P, out), *[resolve(P, a) if is_view(a) else a for a in args],
           **{k: (resolve(P, a) if is_view(a) else a) for k, a in kw.items()}).then_inc(P["T"].sem[sem], 1)
        note(P, q, reads, writes, sem, P["cnt"][sem])
    record(P, q, ns, reads, writes, emit, group=(out[1], args[2], args[3]) if q == "p" else None)


def issue_all(P):
    calls = P["calls"]
    seen, closed = {}, {}
    for n, c in enumerate(calls):
        pre = {}
        for kind in "rw":
            for r in c[kind]:
                for m, k2, r2 in seen.get(r[0], []) if c["q"] in P["eng"] else ():
                    if (kind == "w" or k2 == "w") and hits(r, r2):
                        both = c["group"] and calls[m]["group"] and kind == "w"
                        if both and not any(c["group"][1:] + calls[m]["group"][1:]):
                            continue
                        pre[m] = max(pre.get(m, 0.0), 0.0 if both else HOP)
        row = (c["q"], c["w"][0][0]) if c["w"] else None
        row = SAME.get(row, row)
        if row in ROWS:
            if row in closed:
                pre.setdefault(closed[row], 0.0)
            closed[row] = n
        if c["group"]:
            bank, start, stop = c["group"]
            if start:
                if bank in closed:
                    pre.setdefault(closed[bank], 0.0)
                P["open"][bank] = []
            for m in P["open"][bank][:None if stop else 1]:
                pre.setdefault(m, 0.0)
            P["open"][bank].append(n)
            if stop:
                closed[bank] = n
        for kind in "rw":
            for r in c[kind]:
                lst = seen.setdefault(r[0], [])
                if kind == "w" and r[3] == 1 and not c["group"]:
                    lst[:] = [h for h in lst if not (r[1] <= h[2][1] and h[2][2] <= r[2])]
                lst.append((n, kind, r))
        c["pre"], c["post"] = pre, []
        c["banks"] = sorted(set(r[0] for r in c["r"] + c["w"] if is_psum(r[0])))
        for m in pre:
            calls[m]["post"].append(n)
    for n in range(len(calls) - 1, -1, -1):
        c = calls[n]
        c["way"] = c["ns"] + c["lag"] + max([calls[m]["way"] + calls[m]["pre"][n] for m in c["post"]] + [0.0])
        name = c["w"][0][0] if c["w"] and n < P["first"] else None
        c["goal"] = min([GOALS.index(name) if name in GOALS else len(GOALS)] + [calls[m]["goal"] for m in c["post"]])
    order = sorted(range(len(calls)), key=lambda n: (calls[n]["goal"], -calls[n]["way"], n))
    best = None
    for turn in range(TURNS):
        at = eager(calls, order, PATIENCE[turn // 2]) if turn % 2 else place(calls, order, False)
        end = max(at[n] + c["ns"] + c["lag"] for n, c in enumerate(calls))
        if best is None or end < best[0]:
            best = (end, sorted(range(len(calls)), key=lambda n: (at[n], n)))
        back = place(calls, sorted(range(len(calls)), key=lambda n: (-at[n] - calls[n]["ns"], -n)), True)
        order = sorted(range(len(calls)), key=lambda n: (calls[n]["goal"], -back[n] - calls[n]["ns"], n))
    for n in best[1]:
        calls[n]["emit"]()


def place(calls, order, back):
    at, busy = {}, {}
    for n in order:
        c = calls[n]
        if back:
            t = c["lag"] + max([at[m] + calls[m]["ns"] + calls[m]["pre"][n] for m in c["post"]] + [0.0])
        else:
            t = max([at[m] + calls[m]["ns"] + calls[m]["lag"] + hop for m, hop in c["pre"].items()] + [0.0])
        moved = True
        while moved:
            moved = False
            for key in [c["q"]] + c["banks"]:
                lst = busy.setdefault(key, [])
                k = after(lst, t - 2000.0)
                while k < len(lst) and lst[k][0] < t + c["ns"] + HOP:
                    a, b, q = lst[k]
                    gap = 0.0 if q == c["q"] else HOP
                    if a - gap < t + c["ns"] and t < b + gap:
                        t, moved = b + gap, True
                    k += 1
        at[n] = t
        for key in [c["q"]] + c["banks"]:
            busy[key].insert(after(busy[key], t), (t, t + c["ns"], c["q"]))
    return at


def eager(calls, order, patience):
    rank = {n: k for k, n in enumerate(order)}
    left = [len(c["pre"]) for c in calls]
    at, free, used = {}, {}, {}
    ready = {n: 0.0 for n, c in enumerate(calls) if not c["pre"]}
    while ready:
        can = {n: max([t, free.get(calls[n]["q"], 0.0)] + [e + HOP for b in calls[n]["banks"] for q, e in used.get(b, {}).items()
                                                           if q != calls[n]["q"]]) for n, t in ready.items()}
        soon = min(can, key=lambda n: can[n])
        n = min((m for m in can if calls[m]["q"] == calls[soon]["q"] and can[m] <= can[soon] + patience), key=lambda m: rank[m])
        c = calls[n]
        at[n] = can[n]
        free[c["q"]] = at[n] + c["ns"]
        for b in c["banks"]:
            used.setdefault(b, {})[c["q"]] = free[c["q"]]
        del ready[n]
        for m in c["post"]:
            left[m] -= 1
            if left[m] == 0:
                ready[m] = max(at[k] + calls[k]["ns"] + calls[k]["lag"] + hop for k, hop in calls[m]["pre"].items())
    return at


def after(lst, t):
    lo, hi = 0, len(lst)
    while lo < hi:
        mid = (lo + hi) // 2
        if lst[mid][0] < t:
            lo = mid + 1
        else:
            hi = mid
    return lo


def rank_program(g, core, T, topo):
    me = T.rank_of(core)
    if me is None:
        return
    v, s, pe, y = g.vector, g.scalar, g.tensor, g.sync
    P = {"T": T, "hist": {}, "known": {q: {} for q in "vspyg"}, "cnt": {"sv": 0, "ss": 0, "sp": 0, "sg": 0},
         "eng": {"v": v, "s": s, "p": pe, "y": y, "g": g}, "calls": [], "open": {}}

    def short(*views): return 0.5 if all(x[0] == "A" and dtype(x)[-2:] == "16" for x in views) else 1
    def cp(out, in_): op(P, "v", short(out, in_), v.tensor_copy, out, in_)
    def tt(out, a, b, o): op(P, "v", 1 if is_psum(a[1]) or is_psum(b[1]) else 2, v.tensor_tensor, out, a, b, o)
    def ts(out, a, s1, o1, s2=None, o2=None):
        if o2 is None:
            op(P, "v", short(out, a), v.tensor_scalar, out, a, s1, None, o1)
        else:
            op(P, "v", short(out, a), v.tensor_scalar, out, a, s1, s2, o1, o2)
    def scan(out, d0, d1, ini=0.0): op(P, "v", short(out, d0, d1), v.tensor_tensor_scan, out, d0, d1, ini, O.mult, O.add)
    def fill(out, c): op(P, "v", 1, v.memset, out, c)
    def act(out, in_, f, **kw): op(P, "s", 1, s.activation, out, in_, f, **kw)
    def mm(out, l, r, st, sp): op(P, "p", 1, pe.matmul, out, l, r, st, sp)
    def iota(out, pat, base, cm, **kw): op(P, "g", 2, g.iota, out, pat, base, cm, **kw)
    def pick(out, in_, pat, cmp, base, cm, fill=0.0): op(P, "g", 2, g.affine_select, out, in_, pat, cmp, fill, base, cm)
    def H(name, h, c0=0): return A(name, c0 + 128 * h, c0 + 128 * h + 128)
    def R(name, lo=0, hi=256, c0=0): return A(name, c0 + lo, c0 + hi)
    def W(name, lo=0, hi=256): return A(name, lo + 15, hi, 16)
    def L(name, lo=0, hi=256): return A(name, lo // 16, hi // 16)
    def M(name): return A(name, 0, 128)
    def C(k): return A("col", k, k + 1)

    landed = [DMA]

    def load(q, out, src, sem, size):
        P["eng"][q].dma_start(resolve(P, out), src).then_inc(T.sem[sem], 16)
        note(P, "d" + sem, [], regions([out]), sem, 16)
        landed[0] += size * BYTE
        record(P, sem, 1.0, [], regions([out]), lambda: None, lag=landed[0])
    load("y", A("wkb", 0, 256, 1, 0, 8), T.wk[:], "dwk", 8192)
    load("y", A("payS", 0, 400, 1, 0, 64), T.pay[:], "dpa", 102400)
    load("y", A("payS", 0, 400, 1, 64, 128), T.pay[:], "dpb", 102400)
    load("y", A("quS", 0, 1024), T.qu[:], "dqu", 524288)
    load("y", A("at", 0, 3200), T.am[:], "dam", 819200)
    load("y", A("vt", 0, 1024), T.vp[:], "dvp", 262144)

    imp = {"allow_small_or_imprecise_dtypes": True}

    def block(out, tmp, src):
        pick(tmp, src, [[-16, 8], [0, 16]], O.is_ge, 0, 1)
        pick(out, tmp, [[16, 8], [0, 16]], O.is_ge, 15, -1)
    iota(A("pci", 5, 6), [[1, 1]], 0, 1)
    iota(R("l15"), [[0, 16], [1, 16]], 0, 0, **imp)
    fill(R("ones"), 1.0)
    pick(A("sel8", 0, 128, 1, 0, 8), A("ones", 0, 128, 1, 0, 8), [[1, 8], [0, 16]], O.is_equal, 0, -1)
    ts(R("rst"), R("l15"), 0.0, O.not_equal)
    iota(M("l4"), [[1, 8], [0, 16]], 0, 0, **imp)
    iota(A("i144", 0, 144), [[1, 144]], -16, 0, **imp)
    block(M("blk1"), M("blkT"), M("ones"))
    iota(R("r32"), [[1, 8], [0, 32]], 0, 0, **imp)
    pick(M("idB"), M("ones"), [[-1, 128]], O.is_equal, 0, 1)
    iota(M("W5a"), [[0, 128]], -BIG, 0, **imp)
    iota(A("l16", 0, 16), [[16, 16]], 1025, 0, **imp)
    pick(M("W5b"), M("W5a"), [[0, 8], [1, 16]], O.not_equal, -8, 0, float(BIG))
    block(M("W5"), M("W5c"), M("W5b"))
    p0 = A("pci", 5, 6)
    ts(A("pci", 0, 1), p0, 112, O.bitwise_and)
    ts(A("pci", 1, 2), p0, 15, O.bitwise_and)
    ts(A("pci", 2, 3), p0, 7, O.bitwise_and)
    ts(A("pci", 3, 4), p0, 3, O.arith_shift_right, 7, O.bitwise_and)
    ts(A("pci", 4, 5), p0, 6, O.arith_shift_right)
    cp(A("col", 0, 5), A("pci", 0, 5))
    PM, J8, SCE, BPT, Q, SIG, SG, K0, K1, K2, K3 = C(1), C(5), C(6), C(7), C(8), C(9), C(10), C(11), C(12), C(13), C(14)
    EJ, INI, NOW, EQ8 = C(16), C(17), C(18), C(19)
    maskP, nP, SCc, XP, Z = "b0", "b0", "b1", "b2", "b6"
    ts(J8, PM, 8.0, O.is_lt)
    ts(R(maskP), R("l15"), PM, O.is_equal)
    ts(R("maskS"), R("l15"), PM, O.is_equal)
    ts(EQ8, PM, 8.0, O.is_equal)

    def lin(out, x, scale, bias): act(out, x, F.Identity, scale=scale, bias=bias)
    lin(SCE, J8, float(WR), 0.0)
    lin(C(20), J8, float(-WR), float(WR + 1024))
    ts(C(21), PM, float(-WR), O.mult, J8, O.mult)
    lin(BPT, C(21), 1.0, C(20))
    lin(Q, SCE, float(me), BPT)
    act(SIG, Q, F.Sign)
    lin(SG, SIG, 1.0 / 1024, 0.0)
    lin(K1, Q, -1.0 / 1024, 0.25)
    lin(K2, Q, -1.0 / 1024, 1024.0)
    lin(K3, Q, -1.0 / 1024, MAGIC + 1024.0)
    act(A("vt", 1024, 1040), A("ones", 0, 16), F.Copy, scale=0.0)
    fill(A("ut", 1024, 1032), 1.0)
    fill(A("quS", 1024, 1032), NONE)
    ts(A("selB", 0, 144), A("i144", 0, 144), C(0), O.is_equal)
    for name, factor in (("blkL", 2048.0), ("blkS", float(KS)), ("blk2", 2.0), ("blkZ", -16384.0), ("DM0", -THETA)):
        act(M(name), M("blk1"), F.Copy, scale=factor)
    lin(C(27), EQ8, -512.0, 0.0)
    act(M("S8"), M("blk1"), F.Copy, scale=C(27))
    lin(C(28), EQ8, -2.0 * BIG, float(T0 + BIG))
    act(M("TC"), M("idB"), F.Copy, scale=C(28))
    lin(C(29), EQ8, 1792.0, -2049.0)
    lin(INI, PM, 256.0, C(29))
    act(M("nI"), M("idB"), F.Copy, scale=-1.0)
    lin(A("dumpB", 0, 16), A("l16", 0, 16), 1.0, PM)
    act(EJ, PM, F.Exp, scale=BETA, bias=-7.5 * BETA)
    P["calls"][-1]["ns"] += 1300.0
    pick(M("DM1"), M("DM0"), [[-1, 128]], O.not_equal, 0, 1, 1.0 - THETA)
    act(M("DM"), M("DM1"), F.Copy, scale=EJ)
    lin(C(30), BPT, 1.0, 1024.0 * 1024)
    act(R("E"), R("r32"), F.Abs, scale=SCE, bias=C(30))
    for k in range(3):
        for r in range(8):
            pick(A("win%d" % k, 256 * r, 256 * r + 32), A("E", 32 * r, 32 * r + 32), [[0, 32]], O.is_ge, 0, 0)

    ts(C(24), C(4), float(WR - 1024), O.mult, 1024.0, O.add)
    ts(M("PB0"), M("l4"), C(3), O.is_equal, C(24), O.mult)
    ts(A("col", 32, 40), A("l15", 0, 8), C(2), O.is_equal)
    ts(C(31), C(4), -8.0, O.mult, 16.0, O.add)
    ts(M("PB1"), M("l15"), C(31), O.is_lt)
    tt(M("PB"), M("PB0"), M("PB1"), O.mult)
    ts(A("payI", 0, 400, 1, 0, 64), A("payS", 0, 400, 1, 0, 64), 1023, O.bitwise_and)
    ts(A("payH", 0, 400, 1, 64, 128), A("payS", 0, 400, 1, 64, 128), 1.0 / 1024, O.mult, 1025 - 511.5 / 1024, O.add)
    cp(A("payH", 0, 400, 1, 0, 64), A("payI", 0, 400, 1, 0, 64))
    lin(C(15), SCE, -1025.0, BPT)
    for c in range(8):
        ts(A("PL", 128 * c, 128 * c + 128), M("PB"), C(32 + c), O.mult)
        bank = A("b%d" % (3 + c % 4), 0, 400)
        mm(bank, A("PL", 128 * c, 128 * c + 128), A("payH", 0, 400), True, True)
        act(A("pt", 400 * c, 400 * c + 400), bank, F.Abs, bias=C(15))
    lin(A("pt", NONE, NONE + 1), EQ8, float(-WR), float(WR))
    for c in range(4):
        ts(A("ut", 256 * c, 256 * c + 256), A("quS", 256 * c, 256 * c + 256), float(-U0), O.add, 1.0 / 2048, O.mult)

    def whole(src):
        for h in range(2):
            act(H("cm", h), H(src, h), F.Identity, bias=MAGIC, scale=1.0 / 1024)
            act(H(XP, h), H("cm", h), F.Identity, bias=-1024.0 * MAGIC, scale=1024.0)

    wk8 = A("wkh", 0, 256, 1, 0, 8)
    cp(wk8, A("wkb", 0, 256, 1, 0, 8))
    mm(R("b7"), A("sel8", 0, 128, 1, 0, 8), wk8, True, True)
    act(R("land0"), R("b7"), F.Identity, bias=1024.0, scale=1024.0)
    sends = plan(topo, T.cores, me)
    out_n = sum(len(e) for call in sends for r, e in call)
    arrive = sum(len(e) for q in range(8) if q != me for call in plan(topo, T.cores, q) for r, e in call if r == me)

    def exchange(st, win, land):
        src, dst = [(win, 0, WIN, 1)], [(land, 32 * q, 32 * q + 32, 1) for q in range(8) if q != me]

        def emit():
            sync_for(P, "g", src, [])
            for call in sends:
                g.remote_dma_fused([RemoteDMATransfer(
                    dst_ids=[DstId(rid=topo.addr(T.cores[r], core)[0], pnc=topo.addr(T.cores[r], core)[1])],
                    dma_engine_mask=sum(1 << e for e in engines), remote_sem=T.sem["arr%d" % st],
                    src=T[win][:, 256 * r:256 * r + 32], dst=T[land][:, 32 * me:32 * me + 32])
                    for r, engines in call], local_sem=T.sem["loc"])
            note(P, "remote", [], dst, "arr%d" % st, arrive)
        record(P, "g", SEND * len(sends), src, dst, emit, lag=FLIGHT)

    for st in range(3):
        first, last = st == 0, st == 2
        old, win, land = "land%d" % st, "win%d" % st, "land%d" % (st + 1)
        sg, k1, k2, k3 = (1.0 / 1024, -0.75, 1023.0, MAGIC + 1023.0) if first else (SG, K1, K2, K3)

        def gather(lo, hi):
            act(A("Ag", 16 * lo, 16 * hi), IND(A("at", 0, 3200), R("Uo", lo, hi)), F.Copy)
        for lo, hi in [(0, 256)] if first else HEAD:
            tt(R("M1", lo, hi), R(old, lo, hi), R(maskP, lo, hi), O.mult)
            scan(R("SC", lo, hi), R("rst", lo, hi), R("M1", lo, hi))
            ts(L("BWu", lo, hi), W("SC", lo, hi), sg, O.mult, k1, O.add)
            if first:
                cp(R("Uo"), IND(A("quS", 0, 1032), L("BWu")))
            else:
                ts(R("Uo", lo, hi), IND(A("ut", 0, 1032), L("BWu", lo, hi)), 2048.0, O.mult, float(U0), O.add)
            act(R("cm2", lo, hi), R("SC", lo, hi), F.Identity, bias=k3, scale=sg)
            act(R(SCc, lo, hi), R("cm2", lo, hi), F.Identity, bias=-MAGIC)
        for h in range(2):
            ts(H("xh", h), H(old, h), sg, O.mult, k2, O.add)
        ts(R("UI"), R("Uo"), float(-U0), O.add, 1.0 / 2048, O.mult)
        banks = IND(A("vt", 0, 1040), L("BWu"))
        if first:
            ts(R("NVr"), banks, -1.0, O.mult, 0.0, O.max)
            act(R("V2"), banks, F.Copy)
        else:
            whole(old)
            tt(R("cB"), R(old), R(XP), O.subtract)
            tt(R("V1"), banks, R("cB"), O.subtract)
            ts(R("NVr"), R("V1"), -1.0, O.mult, 0.0, O.max)
            act(R("cm3"), R("V1"), F.Relu, bias=255.0)
            act(R("V2"), R("cm3"), F.Identity, bias=-255.0)
        ts(R(nP, 0, 256, 256), R("NVr"), 255.0, O.min)
        tt(R("eqd"), R("xh"), R(SCc), O.is_equal)
        mm(R(Z, 0, 256, 256), M("blkZ"), R("eqd"), True, False)
        for a in range(15):
            lo = 16 * (a + 1)
            e = R("eqx", lo, 256, 256 * a)
            ts(e, R("xh", lo, 256), A(SCc, lo - 1, lo), O.is_equal)
            mm(R(Z, lo, 256, 256), M("blkZ"), e, False, False)
        mm(R(Z, 0, 256, 256), M("blk1"), R("NVr"), False, True)
        act(R("nsgn"), R(Z, 0, 256, 256), F.Sign, bias=-16384.0, scale=-1.0)
        BWf = A("sm", 0, 16)
        act(BWf, W(SCc), F.Identity, bias=-1024.0)
        P.setdefault("first", len(P["calls"]))
        for lo, hi in GATHERS:
            if (lo, hi) == GATHERS[0 if first else -1]:
                cp(A("Ag", 16 * lo, 16 * hi), IND(A("at", 0, 3200), R("Uo", lo, hi)))
            else:
                gather(lo, hi)

        def thr(lo, hi):
            k = [n for n, (a, b) in enumerate(PLACES) if a <= lo < b][0]
            return A(TBANK[k], lo - PLACES[k][0], hi - PLACES[k][0])
        for k, (lo, hi) in enumerate(GROUPS):
            n = hi - lo
            S, D, sg, RL = SBANK[k], A(SBANK[k], 128, 128 + n), A(SBANK[k], 256, 256 + n), A(RBANK[k], lo, hi)
            for c0, c1 in CHUNKS:
                for i in range(16) if lo <= c0 < hi else ():
                    bits = A("ge", 16 * c0 + i, 16 * c1, 16)
                    tt(bits, A("Ag", 16 * c0 + i, 16 * c1, 16), R(nP, c0, c1, 256), O.is_ge)
                    mm(A(S, c0 - lo, c1 - lo), A("selB", 16 - i, 144 - i), bits, i == 0, i == 15)
            act(R("w", lo, hi), A(S, 0, n), F.Exp, bias=-74.0, scale=16 * BETA)
            mm(D, M("DM"), R("w", lo, hi), True, True)
            act(sg, D, F.Sign)
            mm(RL, M("blkS"), R("nsgn", lo, hi), True, False)
            tt(R("pU", lo, hi), R("UI", lo, hi), sg, O.min)
            mm(RL, M("blkL"), R("pU", lo, hi), False, True)
            if not last:
                act(R("sS", lo, hi), sg, F.Copy)
            tt(R("M5", lo, hi), RL, R("maskS", lo, hi), O.mult)
            scan(R("SC5", lo, hi), R("rst", lo, hi), R("M5", lo, hi))
            lw = L("LWu", lo, hi)
            ts(lw, W("SC5", lo, hi), float(NONE - RL0), O.min, float(RL0), O.add)
            act(R("G", lo, hi), IND(A("pt", 0, 3200), lw), F.Copy)
            act(R("Agl", lo, hi), IND(A("at", 0, 3200), lw), F.Copy)
            for out, less, f, c0 in (("An", "NVr", F.Relu, 0), ("t32", "An", F.Copy, 128)):
                mm(A(S, c0, c0 + n), M("idB"), R("Agl", lo, hi), True, False)
                mm(A(S, c0, c0 + n), M("nI"), R(less, lo, hi), False, True)
                act(R(out, lo, hi), A(S, c0, c0 + n), f)
            for p0, p1 in PLACES:
                if p0 == lo:
                    mm(thr(p0, p1), M("TC"), R("ones", p0, p1), True, False)
            for a in range(hi // 16 - 1):
                c = max(lo, 16 * (a + 1))
                e = R("eqy", c, hi, 256 * a)
                ts(e, A(RBANK[k], c, hi), A("SC5", 16 * a + 15, 16 * a + 16), O.is_equal)
                mm(thr(c, hi), M("W5"), e, False, False)
            tt(R("eqe", lo, hi), R("SC5", lo, hi), RL, O.is_equal)
            mm(thr(lo, hi), M("W5"), R("eqe", lo, hi), False, any(hi == p1 for p0, p1 in PLACES))
            for m, (p0, p1) in enumerate(PLACES):
                if p1 == hi:
                    cnt, off = A(TBANK[m], 192, 192 + p1 - p0), A(TBANK[m], 0, p1 - p0)
                    tt(R("OH", p0, p1), R("G", p0, p1), thr(p0, p1), O.is_le)
                    scan(cnt, R("ones", p0, p1), R("OH", p0, p1), INI if m == 0 else so_far)
                    so_far = A(cnt[1], cnt[3] - 1, cnt[3])
                    tt(R("prod", p0, p1), cnt, R("OH", p0, p1), O.mult)
                    mm(off, M("blk2"), R("prod", p0, p1), True, True)
                    tt(R("M6", p0, p1), off, R("maskS", p0, p1), O.mult)
                    scan(R("SC6", p0, p1), R("rst", p0, p1), R("M6", p0, p1))
                    ts(L("OWu", p0, p1), W("SC6", p0, p1), 0.5, O.mult, 2048.0, O.add)
                    tt(IND(A(win, 0, WIN), L("OWu", p0, p1)), R("t32", p0, p1), R("G", p0, p1), O.add)
        exchange(st, win, land)
        act(A(land, 32 * me, 32 * me + 32), A(win, 256 * me, 256 * me + 32), F.Copy)
        mm(R("b2"), M("S8"), R("OH"), True, False)
        mm(R("b2"), M("idB"), R("Agl"), False, False)
        mm(R("b2"), M("nI"), R("An"), False, True)
        act(R("tm"), R("b2"), F.Relu)
        tt(A("sm", 16, 32), W("SC5"), A("dumpB", 0, 16), O.min)
        tt(A("sm", 32, 48), A("sm", 16, 32), BWf, O.max)
        cp(L("boU"), A("sm", 32, 48))
        tt(IND(A("vt", 0, 1296), L("boU")), R("V2"), R("tm"), O.add)
        if not last:
            act(A("sm", 96, 112), W("SC5"), F.Relu, bias=float(NONE - RL0), scale=-1.0)
            lin(A("sm", 48, 64), A("sm", 96, 112), -1.0, float(NONE))
            tt(A("sm", 64, 80), W("SC6"), BWf, O.max)
            tt(A("sm", 80, 96), W("SC6"), A("sm", 48, 64), O.max)
            cp(A("uaU", 0, 32), A("sm", 64, 96))
            tt(IND(A("ut", 0, WIN), A("uaU", 0, 16)), R("UI"), R("sS"), O.max)
            cp(IND(A("at", 0, WIN), A("uaU", 16, 32)), R("An"))

    def store(q, dst, src, view, sem, size):
        def emit():
            sync_for(P, q, regions([view]), [])
            P["eng"][q].dma_start(dst, src).then_inc(T.sem[sem], 16)
        record(P, q, 50.0, regions([view]), [], emit, lag=DMA + size * BYTE)
    store("y", T.yv[:], T.vt[:, 0:1024], A("vt", 0, 1024), "dyv", 262144)
    whole("land3")
    act(R("ywS"), R("cm"), F.Identity, bias=-MAGIC - WR // 1024 * me - 1)
    for h in range(2):
        tt(H("cB", h), H("land3", h), H(XP, h), O.subtract)
    store("s", T.yw[:], T.ywS[0:128:16, 0:256], R("ywS"), "dyw", 8192)
    store("y", T.yc[:], T.cB[:, 0:256], R("cB"), "dyc", 65536)
    issue_all(P)
    for sem in ("sv", "ss", "sp", "sg"):
        g.wait_ge(T.sem[sem], P["cnt"][sem])
    for sem in ("dwk", "dvp", "dqu", "dam", "dpa", "dpb", "dyv", "dyw", "dyc"):
        g.wait_ge(T.sem[sem], 16)
    g.wait_ge(T.sem["loc"], 3 * out_n)
    for k in range(3):
        g.wait_ge(T.sem["arr%d" % k], arrive)


def plan(topo, cores, q):
    src = cores[q]
    others = [(q + k) % len(cores) for k in range(1, len(cores))]
    near = [r for r in others if cores[r] in topo.cores_of(src)]
    far = [r for r in others if r not in near]
    far.sort(key=lambda r: topo.same_plane(src, cores[r]) or topo.mates(src, cores[r]))
    out = [e for e in topo.engines(src, cores[far[0]])]
    inside = [e for e in topo.engines(src, cores[near[0]]) if e not in out]
    n = len(out) // 4
    first = [(r, out[n * k:n * k + n]) for k, r in enumerate(far[:4])]
    first += [(r, inside[n * k:n * k + n]) for k, r in enumerate(near)]
    m = len(out) // 2
    return [first, [(r, out[m * k:m * k + m]) for k, r in enumerate(far[4:])]]
